import numpy as np
import ml_dtypes


def mxq(x, axis, fmt="e4m3"):
    dtype, down = {"e4m3": (ml_dtypes.float8_e4m3fn, 7), "e5m2": (ml_dtypes.float8_e5m2, 14)}[fmt]
    v = np.moveaxis(np.asarray(x, np.float32).astype(ml_dtypes.bfloat16).astype(np.float64), axis, -1)
    blocks = v.reshape(v.shape[:-1] + (-1, 32))
    amax = np.abs(blocks).max(-1, keepdims=True)
    byte = np.maximum(np.where(amax > 0, np.frexp(amax)[1] - 1 + 127, 0) - down, 1)
    scale = np.exp2(byte - 127.0)
    codes = (blocks / scale).astype(np.float32).astype(dtype).astype(np.float64)
    return np.moveaxis((codes * scale).reshape(v.shape), -1, axis)


WIDE = False


def mx_kscale(k):
    if not WIDE:
        return np.ones(k)
    levels = np.array([10, -10, 5, -5, 0])
    if k % 512:
        return np.exp2(np.random.permutation(np.resize(levels, k // 32))).repeat(32)
    a = np.empty((k // 512, 16))
    for p in range(k // 512):
        a[p, :8] = np.random.permutation(np.resize(levels, 8))
        for g in range(8):
            far = levels[np.abs(levels - a[p, g]) >= 10]
            a[p, g + 8] = far[np.random.randint(len(far))]
    return np.exp2(a.ravel()).repeat(32)


BF16 = ml_dtypes.bfloat16


def bf(x):
    return np.asarray(x, np.float32).astype(BF16)


def f64(x):
    return np.asarray(x).astype(np.float64)


E2M1 = np.array([0.0, 0.5, 1.0, 1.5, 2.0, 3.0, 4.0, 6.0, -0.0, -0.5, -1.0, -1.5, -2.0, -3.0, -4.0, -6.0])


def pack_weight(w, fmt):
    k, n = w.shape
    w = f64(bf(w)).reshape(k // 32, 32, n)
    amax = np.abs(w).max(1)
    if fmt == "e4m3":
        byte = np.frexp(amax)[1] - 1 + 127 - 7
    else:
        mant, ex = np.frexp(amax / 6.0)
        byte = np.where(mant > 0.5, ex, ex - 1) + 127
    byte = np.clip(np.where(amax > 0, byte, 1), 1, 254)
    scaled = (w * np.exp2(127.0 - byte)[:, None, :]).reshape(k, n).astype(np.float32)
    by_word = np.ascontiguousarray(scaled.reshape(k // 512, 128, 4, n).transpose(0, 1, 3, 2))
    if fmt == "e4m3":
        words = by_word.astype(ml_dtypes.float8_e4m3fn).view(np.uint8)
    else:
        c = by_word.astype(ml_dtypes.float4_e2m1fn).view(np.uint8) & 0xF
        words = c[..., 0::2] | (c[..., 1::2] << 4)
    return np.ascontiguousarray(words), np.ascontiguousarray(byte.astype(np.uint8).reshape(k // 512, 16, n))


def unpack_weight(words, scales, fmt):
    g, p, n, _ = words.shape
    if fmt == "e4m3":
        vals = np.ascontiguousarray(words).view(ml_dtypes.float8_e4m3fn).astype(np.float64)
    else:
        nib = np.empty((g, p, n, 4), np.uint8)
        nib[..., 0::2] = words & 0xF
        nib[..., 1::2] = words >> 4
        vals = E2M1[nib]
    vals = vals * np.repeat(np.exp2(scales.astype(np.float64) - 127.0), 8, axis=1)[..., None]
    return vals.transpose(0, 1, 3, 2).reshape(g * 512, n)
def pack4(w):
    words, scales = pack_weight(w, "e2m1")
    return words.reshape(words.shape[0], 128, -1), scales


def unpack4(words, scales):
    return unpack_weight(words.reshape(words.shape[0], 128, -1, 2), scales, "e2m1")


P, D, F, R, N, B = 2048, 1024, 1024, 512, 1024, 8


def setup_inputs():
    s = mx_kscale(D)
    c = mx_kscale(F)
    r = mx_kscale(R)
    root = F ** 0.25
    x = np.random.standard_normal((P, D)) * s
    w = np.random.standard_normal((D, F)) / np.sqrt(D) / root / s[:, None] * c
    u = np.random.standard_normal((R, F)) * r[:, None] / c
    v = np.random.standard_normal((R, N)) / np.sqrt(R) / root / r[:, None]
    u_words, u_scales = pack4(u)
    v_words, v_scales = pack4(v)
    return {"x": bf(x), "w": bf(w),
            "u_words": u_words, "u_scales": u_scales,
            "v_words": v_words, "v_scales": v_scales}


def reference(x, w, u_words, u_scales, v_words, v_scales):
    h = np.maximum(mxq(f64(x), 1, "e4m3") @ mxq(f64(w), 0, "e4m3"), 0.0)
    e = unpack4(u_words, u_scales).T @ unpack4(v_words, v_scales)
    y = np.maximum(mxq(h, 1, "e4m3") @ mxq(e, 0, "e4m3"), 0.0)
    return y.reshape(P // B, B, N).max(axis=1)

@@ -1,0 +1,347 @@
+from contextlib import ExitStack
+
+import concourse.mybir as mybir
+from concourse.masks import make_identity
+
+FLOPS = 2 * 2048 * 1024 * 1024 * 2 + 2 * 512 * 1024 * 1024
+
+F32 = mybir.dt.float32
+BF16 = mybir.dt.bfloat16
+I32 = mybir.dt.int32
+U32 = mybir.dt.uint32
+U8 = mybir.dt.uint8
+FP8X4 = mybir.dt.float8_e4m3fn_x4
+FP4X4 = mybir.dt.float4_e2m1fn_x4
+MAX = mybir.AluOpType.max
+RELU = mybir.ActivationFunctionType.Relu
+
+REORDERED = (1, 2, 3)
+
+
+def tile_pointnet_set_encoder_s12_kernel(tc, x, w, u_words, u_scales, v_words, v_scales, out):
+    nc = tc.nc
+    with ExitStack() as ctx:
+        keep = ctx.enter_context(tc.tile_pool(name="keep", bufs=1))
+        psum = ctx.enter_context(tc.psum_pool(name="psum", bufs=1))
+        ctx.enter_context(tc.manual_schedule())
+
+        def sb(shape, dtype, tag, bufs=1):
+            t = keep.tile(shape, dtype, name=tag, tag=tag, bufs=bufs, align_bytes=256)
+            return t
+
+        def bank(shape):
+            t = psum.tile(shape, F32, name="bank", tag="bank", bufs=8)
+            return t
+
+        u_raw = sb([128, 2048], U8, "u_raw")
+        u_w = sb([128, 2048], U8, "u_w")
+        u_pl_raw = sb([128, 1024], U8, "u_pl_raw")
+        u_pl = sb([128, 1024], U8, "u_pl")
+        v_w = sb([128, 2048], U8, "v_w")
+        v_pl = sb([128, 1024], U8, "v_pl")
+        ident = sb([128, 128], F32, "ident")
+        zero = sb([128, 512], BF16, "zero")
+        junk = sb([128, 16], BF16, "junk")
+        x_sb = [sb([128, 4096], BF16, "x_sb%d" % c) for c in range(4)]
+        w_raw = {(g, G): sb([128, 4, 512], BF16, "w_raw%d%d" % (g, G)) for G in range(2) for g in range(2)}
+        w_c = {(g, G): sb([128, 512], U32, "w_c%d%d" % (g, G)) for G in range(2) for g in range(2)}
+        w_s = {(g, G): sb([128, 512], U8, "w_s%d%d" % (g, G)) for G in range(2) for g in range(2)}
+        e_c = {(G, h): sb([128, 512], U32, "e_c%d%d" % (G, h)) for G in range(2) for h in range(2)}
+        e_s = {(G, h): sb([128, 512], U8, "e_s%d%d" % (G, h)) for G in range(2) for h in range(2)}
+        h_c = {(c, G): sb([128, 512], U32, "h_c%d%d" % (c, G)) for c in range(4) for G in range(2)}
+        h_s = {(c, G): sb([128, 512], U8, "h_s%d%d" % (c, G)) for c in range(4) for G in range(2)}
+        acc = [sb([128, 1024], F32, "acc%d" % s) for s in range(2)]
+
+        nc.vector.memset(u_pl_raw[:].bitcast(I32), 0)
+        nc.vector.memset(v_pl[:].bitcast(I32), 0)
+        nc.vector.memset(zero[:], 0.0)
+
+        v32 = v_words[0].bitcast(I32)
+        us32 = u_scales[0].bitcast(I32)
+        vs32 = v_scales[0].bitcast(I32)
+
+        xv = x.rearrange("(s i b) k -> s i b k", s=2, i=128, b=8)
+        wv = w.rearrange("(g p j) f -> g p j f", g=2, p=128, j=4)
+
+        def load_x(c, b0, nb):
+            s, base = c // 2, 4 * (c % 2)
+            nc.sync.dma_start(
+                out=x_sb[c][:].rearrange("p (b k) -> p b k", b=4)[:, b0 : b0 + nb, :],
+                in_=xv[s][:, base + b0 : base + b0 + nb, :],
+            )
+
+        def load_w(g, G):
+            nc.sync.dma_start(out=w_raw[g, G][:], in_=wv[g][:, :, 512 * G : 512 * G + 512])
+
+        for Q in range(4):
+            nc.scalar.dma_start(out=u_pl_raw[32 * Q : 32 * Q + 4, :].bitcast(I32), in_=us32[4 * Q : 4 * Q + 4, :])
+        for Q in range(3):
+            nc.gpsimd.dma_start(out=v_pl[32 * Q : 32 * Q + 4, :].bitcast(I32), in_=vs32[4 * Q : 4 * Q + 4, :])
+        make_identity(nc, ident[:])
+        load_w(0, 0)
+        load_x(0, 0, 2)
+        nc.sync.dma_start(out=u_raw[:].bitcast(I32), in_=u_words[0].bitcast(I32))
+        nc.sync.dma_start(out=v_w[:].bitcast(I32), in_=v32)
+        nc.sync.dma_start(out=v_pl[96:100, :].bitcast(I32), in_=vs32[12:16, :])
+        load_w(1, 0)
+        load_x(0, 2, 2)
+        load_w(0, 1)
+        load_w(1, 1)
+        for c in (1, 2, 3):
+            for b0 in (0, 2):
+                load_x(c, b0, 2)
+        nc.scalar.activation(out=junk[:, 0:1], in_=zero[:, 0:1], func=RELU)
+
+        warm = bank([128, 512])
+
+        def spin(n):
+            for i in range(n):
+                nc.tensor.matmul(warm[:], lhsT=zero[:, 0:128], rhs=zero[:], start=True, stop=True)
+
+        spin(8)
+
+        def permute_u(G):
+            nc.vector.tensor_copy(
+                out=u_w[:].bitcast(I32).rearrange("p (G t q r) -> p G t q r", G=2, t=4, q=16, r=4)[:, G],
+                in_=u_raw[:].bitcast(I32).rearrange("p (G q t r) -> p G t q r", G=2, q=16, t=4, r=4)[:, G],
+            )
+
+        def permute_u_scales(G):
+            nc.vector.tensor_copy(
+                out=u_pl[:].bitcast(I32).rearrange("p (G t q r) -> p G t q r", G=2, t=4, q=16, r=2)[:, G],
+                in_=u_pl_raw[:].bitcast(I32).rearrange("p (G q t r) -> p G t q r", G=2, q=16, t=4, r=2)[:, G],
+            )
+
+        def copy(engine, out, in_):
+            if engine == "S":
+                nc.scalar.copy(out, in_)
+            else:
+                nc.vector.tensor_copy(out=out, in_=in_)
+
+        e_grp = {}
+        e_tmp = {}
+        e_bank = {}
+
+        def u_tile(G, t):
+            c0 = G * 512 + t * 128
+            return u_w[:, 2 * c0 : 2 * c0 + 256].bitcast(FP4X4), u_pl[:, c0 : c0 + 128]
+
+        def e_mm(G, nh, t):
+            if t == 0:
+                e_tmp[G, nh] = sb([128, 4, 512], BF16, "e_tmp", 4)
+            e = bank([128, 512])
+            lhsT, lhsT_scale = u_tile(G, t)
+            nc.tensor.matmul_mx(
+                out=e[:], lhsT=lhsT, lhsT_scale=lhsT_scale,
+                rhs=v_w[:, 1024 * nh : 1024 * nh + 1024].bitcast(FP4X4), rhs_scale=v_pl[:, 512 * nh : 512 * nh + 512],
+                start=True, stop=True,
+            )
+            e_bank[G, nh, t] = e
+
+        def e_out(G, nh, t, engine):
+            copy(engine, e_tmp[G, nh][:, t, :], e_bank[G, nh, t][:])
+
+        def e_weave(G, nh, engine="V"):
+            e_grp[G, nh] = sb([128, 2048], BF16, "e_grp", 4)
+            copy(
+                engine,
+                e_grp[G, nh][:].rearrange("p (n t) -> p n t", t=4), e_tmp[G, nh][:].rearrange("p t n -> p n t"),
+            )
+
+        def e_quant(G, h):
+            nc.vector.quantize_mx(out=e_c[G, h][:].bitcast(FP8X4), scales=e_s[G, h][:], in_=e_grp[G, h][:])
+
+        x_r = {}
+        x_g = {}
+        x_c = {}
+        x_s = {}
+        x_bank = {}
+
+        def x_reorder(c, bp):
+            if bp == 0:
+                x_r[c] = sb([128, 4096], BF16, "x_r", 3)
+            half = slice(1024 * bp, 1024 * bp + 1024)
+            nc.vector.tensor_copy(
+                out=x_r[c][:].bitcast(F32)[:, half].rearrange("p (a u w) -> p a u w", u=2, w=128),
+                in_=x_sb[c][:].bitcast(F32)[:, half].rearrange("p (a w u) -> p a u w", u=2, w=128),
+            )
+
+        def x_transpose(c, bp, g):
+            if (bp, g) == (0, 0):
+                x_g[c] = sb([128, 4096], BF16, "x_g", 2)
+                x_c[c] = sb([128, 1024], U32, "x_c", 2)
+                x_s[c] = sb([128, 1024], U8, "x_s", 2)
+            xt = bank([128, 2, 256])
+            for u in range(2):
+                for bb in range(2):
+                    base = (2 * bp + bb) * 512 + g * 256
+                    if c in REORDERED:
+                        words = x_r[c][:].bitcast(F32)[:, base + 128 * u : base + 128 * u + 128]
+                    else:
+                        words = x_sb[c][:].bitcast(F32)[:, base + u : base + 256 : 2]
+                    nc.tensor.transpose(xt[:, u, 128 * bb : 128 * bb + 128], words, ident[:])
+            x_bank[c, bp, g] = xt
+
+        def x_out(c, bp, g, engine):
+            base = (2 * bp + g) * 1024
+            copy(
+                engine,
+                x_g[c][:, base : base + 1024].bitcast(F32).rearrange("p (n u) -> p n u", u=2),
+                x_bank[c, bp, g][:].rearrange("p u n -> p n u"),
+            )
+
+        def x_quant(c, bp):
+            nc.vector.quantize_mx(
+                out=x_c[c][:, 512 * bp : 512 * bp + 512].bitcast(FP8X4),
+                scales=x_s[c][:, 512 * bp : 512 * bp + 512],
+                in_=x_g[c][:, 2048 * bp : 2048 * bp + 2048],
+            )
+
+        w_grp = {}
+
+        def w_weave(g, G, engine, ts=(0, 1, 2, 3)):
+            if (g, G) not in w_grp:
+                w_grp[g, G] = sb([128, 2048], BF16, "w_grp", 4)
+            dst = w_grp[g, G][:].rearrange("p (t q r j) -> p t q r j", t=4, q=16, r=8, j=4)
+            src = w_raw[g, G][:].rearrange("p j (q t r) -> p t q r j", q=16, t=4, r=8)
+            if engine == "V":
+                nc.vector.tensor_copy(out=dst[:, ts[0] : ts[-1] + 1], in_=src[:, ts[0] : ts[-1] + 1])
+            else:
+                for t in ts:
+                    nc.scalar.copy(dst[:, t], src[:, t])
+
+        def w_quant(g, G):
+            nc.vector.quantize_mx(out=w_c[g, G][:].bitcast(FP8X4), scales=w_s[g, G][:], in_=w_grp[g, G][:])
+
+        h_t = {}
+        h_bank = {}
+
+        def mm1(c, i):
+            G, b = i // 4, i % 4
+            if b == 0:
+                h_t[c, G] = sb([128, 2048], BF16, "h_t", 3)
+            h = bank([128, 4, 128])
+            col = (b // 2) * 512 + (b % 2) * 128
+            for t in range(4):
+                for g in range(2):
+                    k = slice(col + 256 * g, col + 256 * g + 128)
+                    nc.tensor.matmul_mx(
+                        out=h[:, t, :],
+                        lhsT=w_c[g, G][:, 128 * t : 128 * t + 128].bitcast(FP8X4),
+                        lhsT_scale=w_s[g, G][:, 128 * t : 128 * t + 128],
+                        rhs=x_c[c][:, k].bitcast(FP8X4), rhs_scale=x_s[c][:, k],
+                        start=g == 0, stop=g == 1,
+                    )
+            h_bank[c, i] = h
+
+        def h_out(c, i, engine="S"):
+            G, b = i // 4, i % 4
+            dst = h_t[c, G][:, 512 * b : 512 * b + 512].rearrange("p (n t) -> p n t", t=4)
+            src = h_bank[c, i][:].rearrange("p t n -> p n t")
+            if engine == "S":
+                nc.scalar.activation(out=dst, in_=src, func=RELU)
+            else:
+                nc.vector.tensor_scalar_max(dst, src, 0.0)
+
+        def h_quant(c, G):
+            nc.vector.quantize_mx(out=h_c[c, G][:].bitcast(FP8X4), scales=h_s[c, G][:], in_=h_t[c, G][:])
+
+        def mm2(c, b, n0, n):
+            y = bank([128, n])
+            rows = slice(128 * b, 128 * b + 128)
+            nh, j0 = n0 // 512, n0 % 512
+            for G in range(2):
+                nc.tensor.matmul_mx(
+                    out=y[:],
+                    lhsT=h_c[c, G][:, rows].bitcast(FP8X4), lhsT_scale=h_s[c, G][:, rows],
+                    rhs=e_c[G, nh][:, j0 : j0 + n].bitcast(FP8X4), rhs_scale=e_s[G, nh][:, j0 : j0 + n],
+                    start=G == 0, stop=G == 1,
+                )
+            a = acc[c // 2][:, n0 : n0 + n]
+            if c % 2 == 0 and b == 0:
+                nc.scalar.activation(out=a, in_=y[:], func=RELU)
+            else:
+                nc.vector.tensor_tensor(out=a, in0=y[:], in1=a, op=MAX)
+            if c % 2 == 1 and b == 3:
+                s = c // 2
+                nc.sync.dma_start(out=out[128 * s : 128 * s + 128, n0 : n0 + n], in_=a)
+
+        e_units = [(G, nh, t) for nh in range(2) for G in range(2) for t in range(4)]
+        w_weave(0, 0, "S", (0, 1))
+        w_weave(0, 0, "V", (2, 3))
+        permute_u(0)
+        permute_u_scales(0)
+        permute_u_scales(1)
+        permute_u(1)
+        x_transpose(0, 0, 0)
+        x_transpose(0, 0, 1)
+        x_out(0, 0, 0, "S")
+        x_out(0, 0, 1, "S")
+        w_quant(0, 0)
+        for k in range(8):
+            e_mm(*e_units[k])
+        for k in range(5):
+            e_out(*e_units[k], "S")
+        w_weave(1, 0, "V")
+        x_quant(0, 0)
+        w_quant(1, 0)
+        for k in range(8, 12):
+            e_mm(*e_units[k])
+        x_transpose(0, 1, 0)
+        x_transpose(0, 1, 1)
+        e_out(*e_units[5], "V")
+        e_out(*e_units[6], "S")
+        x_out(0, 1, 0, "S")
+        x_out(0, 1, 1, "V")
+        x_quant(0, 1)
+        for k in range(7, 12):
+            e_out(*e_units[k], "S")
+
+        for c in range(4):
+            for i in range(8):
+                mm1(c, i)
+                h_out(c, i)
+                if c == 0:
+                    if i == 0:
+                        x_reorder(1, 0)
+                        w_weave(0, 1, "V", (1, 2, 3))
+                        w_weave(0, 1, "S", (0,))
+                    if i == 1:
+                        x_reorder(1, 1)
+                        w_weave(1, 1, "V", (1, 2, 3))
+                        w_quant(0, 1)
+                        w_weave(1, 1, "S", (0,))
+                        w_quant(1, 1)
+                    if i == 3:
+                        for bp in range(2):
+                            for g in range(2):
+                                x_transpose(1, bp, g)
+                                x_out(1, bp, g, "VS"[g])
+                        for k in range(12, 16):
+                            e_mm(*e_units[k])
+                            e_out(*e_units[k], "VS"[k % 2])
+                if c in (1, 2) and i == 2:
+                    for bp in range(2):
+                        for g in range(2):
+                            x_transpose(c + 1, bp, g)
+                            x_out(c + 1, bp, g, "VS"[g])
+                if c < 3 and i in (4, 5):
+                    x_quant(c + 1, i - 4)
+                if i == 6:
+                    h_quant(c, 0)
+                if c > 0 and i == 1:
+                    h_quant(c - 1, 1)
+                if c == 0 and i >= 6 or c == 1 and i in (0, 2):
+                    x_reorder(2 + c, i % 4 // 2 if c else i - 6)
+                if c in (1, 2) and i in (5, 7):
+                    e_weave(i // 2 - 2, c - 1)
+                if c == 3 and i % 2 == 0:
+                    k = i // 2
+                    e_quant(k % 2, k // 2)
+        h_quant(3, 1)
+
+        for c in range(4):
+            for b in range(4):
+                widths = (512, 256, 256) if (c, b) == (3, 3) else (512, 512)
+                for j, n in enumerate(widths):
+                    mm2(c, b, sum(widths[:j]), n)

@@ -14,8 +14,7 @@ FP8X4 = mybir.dt.float8_e4m3fn_x4
 FP4X4 = mybir.dt.float4_e2m1fn_x4
 MAX = mybir.AluOpType.max
 RELU = mybir.ActivationFunctionType.Relu
-
-REORDERED = (1, 2, 3)
+COPY = mybir.ActivationFunctionType.Copy
 
 
 def tile_pointnet_set_encoder_s12_kernel(tc, x, w, u_words, u_scales, v_words, v_scales, out):
@@ -33,6 +32,13 @@ def tile_pointnet_set_encoder_s12_kernel(tc, x, w, u_words, u_scales, v_words, v
             t = psum.tile(shape, F32, name="bank", tag="bank", bufs=8)
             return t
 
+        def spin(n, lhsT, rhs):
+            for i in range(n):
+                nc.tensor.matmul(warm[:, 0 : rhs.shape[1]], lhsT=lhsT, rhs=rhs, start=True, stop=True)
+
+        def pairs(a, b):
+            return [(i, j) for i in range(a) for j in range(b)]
+
         u_raw = sb([128, 2048], U8, "u_raw")
         u_w = sb([128, 2048], U8, "u_w")
         u_pl_raw = sb([128, 1024], U8, "u_pl_raw")
@@ -40,191 +46,151 @@ def tile_pointnet_set_encoder_s12_kernel(tc, x, w, u_words, u_scales, v_words, v
         v_w = sb([128, 2048], U8, "v_w")
         v_pl = sb([128, 1024], U8, "v_pl")
         ident = sb([128, 128], F32, "ident")
-        zero = sb([128, 512], BF16, "zero")
-        junk = sb([128, 16], BF16, "junk")
-        x_sb = [sb([128, 4096], BF16, "x_sb%d" % c) for c in range(4)]
-        w_raw = {(g, G): sb([128, 4, 512], BF16, "w_raw%d%d" % (g, G)) for G in range(2) for g in range(2)}
-        w_c = {(g, G): sb([128, 512], U32, "w_c%d%d" % (g, G)) for G in range(2) for g in range(2)}
-        w_s = {(g, G): sb([128, 512], U8, "w_s%d%d" % (g, G)) for G in range(2) for g in range(2)}
-        e_c = {(G, h): sb([128, 512], U32, "e_c%d%d" % (G, h)) for G in range(2) for h in range(2)}
-        e_s = {(G, h): sb([128, 512], U8, "e_s%d%d" % (G, h)) for G in range(2) for h in range(2)}
-        h_c = {(c, G): sb([128, 512], U32, "h_c%d%d" % (c, G)) for c in range(4) for G in range(2)}
-        h_s = {(c, G): sb([128, 512], U8, "h_s%d%d" % (c, G)) for c in range(4) for G in range(2)}
+        x_sb = [sb([128, 2048], BF16, "x_sb%d" % q) for q in range(8)]
+        x_c = [sb([128, 1024], U32, "x_c%d" % c) for c in range(4)]
+        x_s = [sb([128, 1024], U8, "x_s%d" % c) for c in range(4)]
+        w_raw = {k: sb([128, 4, 512], BF16, "w_raw%d%d" % k) for k in pairs(2, 2)}
+        w_grp = {k: sb([128, 2048], BF16, "w_grp%d%d" % k) for k in pairs(2, 2)}
+        w_c = {k: sb([128, 512], U32, "w_c%d%d" % k) for k in pairs(2, 2)}
+        w_s = {k: sb([128, 512], U8, "w_s%d%d" % k) for k in pairs(2, 2)}
+        e_grp = {k: sb([128, 2048], BF16, "e_grp%d%d" % k) for k in pairs(2, 2)}
+        e_c = {k: sb([128, 512], U32, "e_c%d%d" % k) for k in pairs(2, 2)}
+        e_s = {k: sb([128, 512], U8, "e_s%d%d" % k) for k in pairs(2, 2)}
+        h_c = {k: sb([128, 512], U32, "h_c%d%d" % k) for k in pairs(4, 2)}
+        h_s = {k: sb([128, 512], U8, "h_s%d%d" % k) for k in pairs(4, 2)}
         acc = [sb([128, 1024], F32, "acc%d" % s) for s in range(2)]
 
-        nc.vector.memset(u_pl_raw[:].bitcast(I32), 0)
-        nc.vector.memset(v_pl[:].bitcast(I32), 0)
-        nc.vector.memset(zero[:], 0.0)
-
-        v32 = v_words[0].bitcast(I32)
         us32 = u_scales[0].bitcast(I32)
         vs32 = v_scales[0].bitcast(I32)
-
         xv = x.rearrange("(s i b) k -> s i b k", s=2, i=128, b=8)
         wv = w.rearrange("(g p j) f -> g p j f", g=2, p=128, j=4)
 
-        def load_x(c, b0, nb):
-            s, base = c // 2, 4 * (c % 2)
-            nc.sync.dma_start(
-                out=x_sb[c][:].rearrange("p (b k) -> p b k", b=4)[:, b0 : b0 + nb, :],
-                in_=xv[s][:, base + b0 : base + b0 + nb, :],
-            )
+        def load_x(q):
+            s, b = q // 4, 2 * (q % 4)
+            nc.sync.dma_start(out=x_sb[q][:].rearrange("p (b k) -> p b k", b=2), in_=xv[s][:, b : b + 2, :])
 
         def load_w(g, G):
             nc.sync.dma_start(out=w_raw[g, G][:], in_=wv[g][:, :, 512 * G : 512 * G + 512])
 
-        for Q in range(4):
-            nc.scalar.dma_start(out=u_pl_raw[32 * Q : 32 * Q + 4, :].bitcast(I32), in_=us32[4 * Q : 4 * Q + 4, :])
-        for Q in range(3):
-            nc.gpsimd.dma_start(out=v_pl[32 * Q : 32 * Q + 4, :].bitcast(I32), in_=vs32[4 * Q : 4 * Q + 4, :])
-        make_identity(nc, ident[:])
-        load_w(0, 0)
-        load_x(0, 0, 2)
-        nc.sync.dma_start(out=u_raw[:].bitcast(I32), in_=u_words[0].bitcast(I32))
-        nc.sync.dma_start(out=v_w[:].bitcast(I32), in_=v32)
-        nc.sync.dma_start(out=v_pl[96:100, :].bitcast(I32), in_=vs32[12:16, :])
-        load_w(1, 0)
-        load_x(0, 2, 2)
-        load_w(0, 1)
-        load_w(1, 1)
-        for c in (1, 2, 3):
-            for b0 in (0, 2):
-                load_x(c, b0, 2)
-        nc.scalar.activation(out=junk[:, 0:1], in_=zero[:, 0:1], func=RELU)
-
-        warm = bank([128, 512])
-
-        def spin(n):
-            for i in range(n):
-                nc.tensor.matmul(warm[:], lhsT=zero[:, 0:128], rhs=zero[:], start=True, stop=True)
-
-        spin(8)
-
-        def permute_u(G):
-            nc.vector.tensor_copy(
-                out=u_w[:].bitcast(I32).rearrange("p (G t q r) -> p G t q r", G=2, t=4, q=16, r=4)[:, G],
-                in_=u_raw[:].bitcast(I32).rearrange("p (G q t r) -> p G t q r", G=2, q=16, t=4, r=4)[:, G],
-            )
-
-        def permute_u_scales(G):
-            nc.vector.tensor_copy(
-                out=u_pl[:].bitcast(I32).rearrange("p (G t q r) -> p G t q r", G=2, t=4, q=16, r=2)[:, G],
-                in_=u_pl_raw[:].bitcast(I32).rearrange("p (G q t r) -> p G t q r", G=2, q=16, t=4, r=2)[:, G],
-            )
+        def load_scales(engine, plane, rows, Q):
+            engine.dma_start(out=plane[32 * Q : 32 * Q + 4, :].bitcast(I32), in_=rows[4 * Q : 4 * Q + 4, :])
 
         def copy(engine, out, in_):
             if engine == "S":
                 nc.scalar.copy(out, in_)
+            elif engine == "A":
+                nc.scalar.activation(out=out, in_=in_, func=COPY)
             else:
                 nc.vector.tensor_copy(out=out, in_=in_)
 
-        e_grp = {}
-        e_tmp = {}
-        e_bank = {}
-
-        def u_tile(G, t):
-            c0 = G * 512 + t * 128
-            return u_w[:, 2 * c0 : 2 * c0 + 256].bitcast(FP4X4), u_pl[:, c0 : c0 + 128]
-
-        def e_mm(G, nh, t):
-            if t == 0:
-                e_tmp[G, nh] = sb([128, 4, 512], BF16, "e_tmp", 4)
-            e = bank([128, 512])
-            lhsT, lhsT_scale = u_tile(G, t)
-            nc.tensor.matmul_mx(
-                out=e[:], lhsT=lhsT, lhsT_scale=lhsT_scale,
-                rhs=v_w[:, 1024 * nh : 1024 * nh + 1024].bitcast(FP4X4), rhs_scale=v_pl[:, 512 * nh : 512 * nh + 512],
-                start=True, stop=True,
-            )
-            e_bank[G, nh, t] = e
-
-        def e_out(G, nh, t, engine):
-            copy(engine, e_tmp[G, nh][:, t, :], e_bank[G, nh, t][:])
-
-        def e_weave(G, nh, engine="V"):
-            e_grp[G, nh] = sb([128, 2048], BF16, "e_grp", 4)
-            copy(
-                engine,
-                e_grp[G, nh][:].rearrange("p (n t) -> p n t", t=4), e_tmp[G, nh][:].rearrange("p t n -> p n t"),
-            )
-
-        def e_quant(G, h):
-            nc.vector.quantize_mx(out=e_c[G, h][:].bitcast(FP8X4), scales=e_s[G, h][:], in_=e_grp[G, h][:])
-
-        x_r = {}
-        x_g = {}
-        x_c = {}
-        x_s = {}
-        x_bank = {}
-
-        def x_reorder(c, bp):
-            if bp == 0:
-                x_r[c] = sb([128, 4096], BF16, "x_r", 3)
-            half = slice(1024 * bp, 1024 * bp + 1024)
+        def permute_u():
             nc.vector.tensor_copy(
-                out=x_r[c][:].bitcast(F32)[:, half].rearrange("p (a u w) -> p a u w", u=2, w=128),
-                in_=x_sb[c][:].bitcast(F32)[:, half].rearrange("p (a w u) -> p a u w", u=2, w=128),
+                out=u_w[:].bitcast(I32).rearrange("p (G t q r) -> p G t q r", G=2, t=4, q=32, r=2),
+                in_=u_raw[:].bitcast(I32).rearrange("p (G q t r) -> p G t q r", G=2, q=32, t=4, r=2),
             )
 
-        def x_transpose(c, bp, g):
-            if (bp, g) == (0, 0):
-                x_g[c] = sb([128, 4096], BF16, "x_g", 2)
-                x_c[c] = sb([128, 1024], U32, "x_c", 2)
-                x_s[c] = sb([128, 1024], U8, "x_s", 2)
-            xt = bank([128, 2, 256])
-            for u in range(2):
-                for bb in range(2):
-                    base = (2 * bp + bb) * 512 + g * 256
-                    if c in REORDERED:
-                        words = x_r[c][:].bitcast(F32)[:, base + 128 * u : base + 128 * u + 128]
-                    else:
-                        words = x_sb[c][:].bitcast(F32)[:, base + u : base + 256 : 2]
-                    nc.tensor.transpose(xt[:, u, 128 * bb : 128 * bb + 128], words, ident[:])
-            x_bank[c, bp, g] = xt
-
-        def x_out(c, bp, g, engine):
-            base = (2 * bp + g) * 1024
-            copy(
-                engine,
-                x_g[c][:, base : base + 1024].bitcast(F32).rearrange("p (n u) -> p n u", u=2),
-                x_bank[c, bp, g][:].rearrange("p u n -> p n u"),
+        def permute_u_scales():
+            nc.vector.tensor_copy(
+                out=u_pl[:].bitcast(I32).rearrange("p (G t q) -> p G t q", G=2, t=4, q=32),
+                in_=u_pl_raw[:].bitcast(I32).rearrange("p (G q t) -> p G t q", G=2, q=32, t=4),
             )
 
-        def x_quant(c, bp):
-            nc.vector.quantize_mx(
-                out=x_c[c][:, 512 * bp : 512 * bp + 512].bitcast(FP8X4),
-                scales=x_s[c][:, 512 * bp : 512 * bp + 512],
-                in_=x_g[c][:, 2048 * bp : 2048 * bp + 2048],
-            )
-
-        w_grp = {}
-
-        def w_weave(g, G, engine, ts=(0, 1, 2, 3)):
-            if (g, G) not in w_grp:
-                w_grp[g, G] = sb([128, 2048], BF16, "w_grp", 4)
-            dst = w_grp[g, G][:].rearrange("p (t q r j) -> p t q r j", t=4, q=16, r=8, j=4)
-            src = w_raw[g, G][:].rearrange("p j (q t r) -> p t q r j", q=16, t=4, r=8)
+        def w_weave(g, G, engine, t0, nt):
+            dst = w_grp[g, G][:].rearrange("p (t q r j) -> p t q j r", t=4, q=32, r=4, j=4)
+            src = w_raw[g, G][:].rearrange("p j (q t r) -> p t q j r", q=32, t=4, r=4)
             if engine == "V":
-                nc.vector.tensor_copy(out=dst[:, ts[0] : ts[-1] + 1], in_=src[:, ts[0] : ts[-1] + 1])
+                nc.vector.tensor_copy(out=dst[:, t0 : t0 + nt], in_=src[:, t0 : t0 + nt])
             else:
-                for t in ts:
-                    nc.scalar.copy(dst[:, t], src[:, t])
+                for t in range(t0, t0 + nt):
+                    nc.scalar.activation(out=dst[:, t], in_=src[:, t], func=COPY)
 
         def w_quant(g, G):
             nc.vector.quantize_mx(out=w_c[g, G][:].bitcast(FP8X4), scales=w_s[g, G][:], in_=w_grp[g, G][:])
 
-        h_t = {}
-        h_bank = {}
+        banks = {}
 
-        def mm1(c, i):
-            G, b = i // 4, i % 4
+        def e_mm(G, nb):
+            e = bank([128, 4, 128])
+            for t in range(4):
+                c0 = G * 512 + t * 128
+                nc.tensor.matmul_mx(
+                    out=e[:, t, :],
+                    lhsT=u_w[:, 2 * c0 : 2 * c0 + 256].bitcast(FP4X4), lhsT_scale=u_pl[:, c0 : c0 + 128],
+                    rhs=v_w[:, 256 * nb : 256 * nb + 256].bitcast(FP4X4), rhs_scale=v_pl[:, 128 * nb : 128 * nb + 128],
+                    start=t == 0, stop=t == 3,
+                )
+            banks["e", G, nb] = e
+
+        def e_out(G, nb, engine):
+            j = nb % 4
+            copy(
+                engine,
+                e_grp[G, nb // 4][:, 512 * j : 512 * j + 512].rearrange("p (n t) -> p n t", t=4),
+                banks["e", G, nb][:].rearrange("p t n -> p n t"),
+            )
+
+        def e_quant(G, nh):
+            nc.vector.quantize_mx(out=e_c[G, nh][:].bitcast(FP8X4), scales=e_s[G, nh][:], in_=e_grp[G, nh][:])
+
+        x_r = {}
+        x_g = {}
+
+        def x_reorder(q, engine):
+            x_r[q] = sb([128, 1024], F32, "x_r", 4)
+            copy(
+                engine,
+                x_r[q][:].rearrange("p (a u w) -> p a u w", u=2, w=128),
+                x_sb[q][:].bitcast(F32).rearrange("p (a w u) -> p a u w", u=2, w=128),
+            )
+
+        def x_transpose(m):
+            q = m // 2
+            xt = bank([128, 2, 2, 128])
+            for g in range(2):
+                base = (m % 2) * 512 + g * 256
+                for u in range(2):
+                    if q in x_r:
+                        words = x_r[q][:, base + 128 * u : base + 128 * u + 128]
+                    else:
+                        words = x_sb[q][:].bitcast(F32)[:, base + u : base + 256 : 2]
+                    nc.tensor.transpose(xt[:, g, u, :], words, ident[:])
+            banks["x", m] = xt
+
+        def x_out(m, engine):
+            c, b = m // 4, m % 4
             if b == 0:
-                h_t[c, G] = sb([128, 2048], BF16, "h_t", 3)
+                x_g[c] = sb([128, 4096], BF16, "x_g", 2)
+            if engine == "A":
+                for g in range(2):
+                    k0 = 1024 * b + 512 * g
+                    nc.scalar.activation(
+                        out=x_g[c][:, k0 : k0 + 512].rearrange("p (n u e) -> p n u e", u=2, e=2),
+                        in_=banks["x", m][:, g].bitcast(BF16).rearrange("p u (n e) -> p n u e", e=2),
+                        func=COPY,
+                    )
+                return
+            copy(
+                engine,
+                x_g[c][:, 1024 * b : 1024 * b + 1024].bitcast(F32).rearrange("p (g n u) -> p g n u", g=2, u=2),
+                banks["x", m][:].rearrange("p g u n -> p g n u"),
+            )
+
+        def x_quant(m, n):
+            c, b = m // 4, m % 4
+            nc.vector.quantize_mx(
+                out=x_c[c][:, 256 * b : 256 * (b + n)].bitcast(FP8X4),
+                scales=x_s[c][:, 256 * b : 256 * (b + n)],
+                in_=x_g[c][:, 1024 * b : 1024 * (b + n)],
+            )
+
+        h_t = {}
+
+        def mm1(m, G):
+            c, b = m // 4, m % 4
             h = bank([128, 4, 128])
-            col = (b // 2) * 512 + (b % 2) * 128
             for t in range(4):
                 for g in range(2):
-                    k = slice(col + 256 * g, col + 256 * g + 128)
+                    k = slice(256 * b + 128 * g, 256 * b + 128 * g + 128)
                     nc.tensor.matmul_mx(
                         out=h[:, t, :],
                         lhsT=w_c[g, G][:, 128 * t : 128 * t + 128].bitcast(FP8X4),
@@ -232,116 +198,170 @@ def tile_pointnet_set_encoder_s12_kernel(tc, x, w, u_words, u_scales, v_words, v
                         rhs=x_c[c][:, k].bitcast(FP8X4), rhs_scale=x_s[c][:, k],
                         start=g == 0, stop=g == 1,
                     )
-            h_bank[c, i] = h
+            banks["h", m, G] = h
 
-        def h_out(c, i, engine="S"):
-            G, b = i // 4, i % 4
+        def h_out(m, G, engine="S"):
+            c, b = m // 4, m % 4
+            if b == 0:
+                h_t[c, G] = sb([128, 2048], BF16, "h_t", 4)
             dst = h_t[c, G][:, 512 * b : 512 * b + 512].rearrange("p (n t) -> p n t", t=4)
-            src = h_bank[c, i][:].rearrange("p t n -> p n t")
+            src = banks["h", m, G][:].rearrange("p t n -> p n t")
             if engine == "S":
                 nc.scalar.activation(out=dst, in_=src, func=RELU)
             else:
                 nc.vector.tensor_scalar_max(dst, src, 0.0)
 
-        def h_quant(c, G):
-            nc.vector.quantize_mx(out=h_c[c, G][:].bitcast(FP8X4), scales=h_s[c, G][:], in_=h_t[c, G][:])
+        def h_quant(m, G, n):
+            c, b = m // 4, m % 4
+            nc.vector.quantize_mx(
+                out=h_c[c, G][:, 128 * b : 128 * (b + n)].bitcast(FP8X4),
+                scales=h_s[c, G][:, 128 * b : 128 * (b + n)],
+                in_=h_t[c, G][:, 512 * b : 512 * (b + n)],
+            )
 
-        def mm2(c, b, n0, n):
-            y = bank([128, n])
+        def mm2_pass(m, n0, n, G):
+            c, b = m // 4, m % 4
+            if G == 0:
+                banks["y", m, n0] = bank([128, n])
             rows = slice(128 * b, 128 * b + 128)
             nh, j0 = n0 // 512, n0 % 512
-            for G in range(2):
-                nc.tensor.matmul_mx(
-                    out=y[:],
-                    lhsT=h_c[c, G][:, rows].bitcast(FP8X4), lhsT_scale=h_s[c, G][:, rows],
-                    rhs=e_c[G, nh][:, j0 : j0 + n].bitcast(FP8X4), rhs_scale=e_s[G, nh][:, j0 : j0 + n],
-                    start=G == 0, stop=G == 1,
-                )
-            a = acc[c // 2][:, n0 : n0 + n]
-            if c % 2 == 0 and b == 0:
+            nc.tensor.matmul_mx(
+                out=banks["y", m, n0][:],
+                lhsT=h_c[c, G][:, rows].bitcast(FP8X4), lhsT_scale=h_s[c, G][:, rows],
+                rhs=e_c[G, nh][:, j0 : j0 + n].bitcast(FP8X4), rhs_scale=e_s[G, nh][:, j0 : j0 + n],
+                start=G == 0, stop=G == 1,
+            )
+
+        def mm2(m, n0, n=512):
+            mm2_pass(m, n0, n, 0)
+            mm2_pass(m, n0, n, 1)
+            y_out(m, n0, n)
+
+        def y_out(m, n0, n):
+            y = banks["y", m, n0]
+            s = m // 8
+            a = acc[s][:, n0 : n0 + n]
+            if m % 8 == 0:
                 nc.scalar.activation(out=a, in_=y[:], func=RELU)
             else:
                 nc.vector.tensor_tensor(out=a, in0=y[:], in1=a, op=MAX)
-            if c % 2 == 1 and b == 3:
-                s = c // 2
+            if m % 8 == 7:
                 nc.sync.dma_start(out=out[128 * s : 128 * s + 128, n0 : n0 + n], in_=a)
 
-        e_units = [(G, nh, t) for nh in range(2) for G in range(2) for t in range(4)]
-        w_weave(0, 0, "S", (0, 1))
-        w_weave(0, 0, "V", (2, 3))
-        permute_u(0)
-        permute_u_scales(0)
-        permute_u_scales(1)
-        permute_u(1)
-        x_transpose(0, 0, 0)
-        x_transpose(0, 0, 1)
-        x_out(0, 0, 0, "S")
-        x_out(0, 0, 1, "S")
+        nc.gpsimd.memset(v_pl[:].bitcast(I32), 0)
+        nc.vector.memset(u_pl_raw[:].bitcast(I32), 0)
+        zero = sb([128, 512], BF16, "zero")
+        nc.vector.memset(zero[:], 0.0)
+        nc.sync.dma_start(out=u_raw[:].bitcast(I32), in_=u_words[0].bitcast(I32))
+        nc.sync.dma_start(out=v_w[:].bitcast(I32), in_=v_words[0].bitcast(I32))
+        load_x(0)
+        for Q in range(4):
+            load_scales(nc.scalar, u_pl_raw, us32, Q)
+        load_scales(nc.scalar, v_pl, vs32, 3)
+        for Q in range(3):
+            load_scales(nc.gpsimd, v_pl, vs32, Q)
+        make_identity(nc, ident[:])
+        load_w(0, 0)
+        load_w(1, 0)
+        load_x(1)
+        load_w(0, 1)
+        load_x(2)
+        load_w(1, 1)
+        for q in range(3, 8):
+            load_x(q)
+        warm = bank([128, 512])
+        spin(4, zero[:, 0:128], zero[:])
+        spin(2, ident[:], ident[:])
+
+        permute_u()
+        permute_u_scales()
+        x_transpose(0)
+        x_transpose(1)
+        spin(2, x_sb[0][:, 0:128], x_sb[0][:, 0:512])
+        x_out(0, "A")
+        x_out(1, "S")
+        w_weave(0, 0, "V", 0, 4)
         w_quant(0, 0)
-        for k in range(8):
-            e_mm(*e_units[k])
-        for k in range(5):
-            e_out(*e_units[k], "S")
-        w_weave(1, 0, "V")
-        x_quant(0, 0)
+        w_weave(1, 0, "V", 0, 4)
+        x_quant(0, 2)
+        for k in range(12):
+            if k == 6:
+                x_transpose(2)
+                x_transpose(3)
+            e_mm(k // 4 % 2, k % 4 + k // 8 * 4)
+            e_out(k // 4 % 2, k % 4 + k // 8 * 4, "S")
+        x_out(2, "V")
         w_quant(1, 0)
-        for k in range(8, 12):
-            e_mm(*e_units[k])
-        x_transpose(0, 1, 0)
-        x_transpose(0, 1, 1)
-        e_out(*e_units[5], "V")
-        e_out(*e_units[6], "S")
-        x_out(0, 1, 0, "S")
-        x_out(0, 1, 1, "V")
-        x_quant(0, 1)
-        for k in range(7, 12):
-            e_out(*e_units[k], "S")
+        x_out(3, "V")
+        w_weave(0, 1, "V", 0, 4)
+        x_quant(2, 2)
+        w_quant(0, 1)
+        w_weave(1, 1, "V", 0, 4)
+        for q in range(2):
+            for m in (2 * q, 2 * q + 1):
+                mm1(m, 0)
+                h_out(m, 0)
+            for m in (2 * q + 4, 2 * q + 5):
+                x_transpose(m)
+            x_out(2 * q + 4, "SV"[q])
+            x_out(2 * q + 5, "SV"[q])
+            if q == 0:
+                e_quant(0, 0)
+                w_quant(1, 1)
+        x_quant(4, 2)
+        e_quant(1, 0)
+        for m in range(4):
+            mm1(m, 1)
+            h_out(m, 1)
+            if m == 0:
+                x_quant(6, 2)
+                h_quant(0, 0, 4)
+                e_quant(0, 1)
+        x_reorder(4, "V")
+        for m in range(4, 6):
+            for G in range(2):
+                mm1(m, G)
+                h_out(m, G)
+                e_mm(1, 2 * m - 4 + G)
+                e_out(1, 2 * m - 4 + G, "V")
+                if (m, G) == (4, 0):
+                    h_quant(0, 1, 4)
+                if (m, G) == (4, 1):
+                    x_reorder(5, "V")
 
-        for c in range(4):
-            for i in range(8):
-                mm1(c, i)
-                h_out(c, i)
-                if c == 0:
-                    if i == 0:
-                        x_reorder(1, 0)
-                        w_weave(0, 1, "V", (1, 2, 3))
-                        w_weave(0, 1, "S", (0,))
-                    if i == 1:
-                        x_reorder(1, 1)
-                        w_weave(1, 1, "V", (1, 2, 3))
-                        w_quant(0, 1)
-                        w_weave(1, 1, "S", (0,))
-                        w_quant(1, 1)
-                    if i == 3:
-                        for bp in range(2):
-                            for g in range(2):
-                                x_transpose(1, bp, g)
-                                x_out(1, bp, g, "VS"[g])
-                        for k in range(12, 16):
-                            e_mm(*e_units[k])
-                            e_out(*e_units[k], "VS"[k % 2])
-                if c in (1, 2) and i == 2:
-                    for bp in range(2):
-                        for g in range(2):
-                            x_transpose(c + 1, bp, g)
-                            x_out(c + 1, bp, g, "VS"[g])
-                if c < 3 and i in (4, 5):
-                    x_quant(c + 1, i - 4)
-                if i == 6:
-                    h_quant(c, 0)
-                if c > 0 and i == 1:
-                    h_quant(c - 1, 1)
-                if c == 0 and i >= 6 or c == 1 and i in (0, 2):
-                    x_reorder(2 + c, i % 4 // 2 if c else i - 6)
-                if c in (1, 2) and i in (5, 7):
-                    e_weave(i // 2 - 2, c - 1)
-                if c == 3 and i % 2 == 0:
-                    k = i // 2
-                    e_quant(k % 2, k // 2)
-        h_quant(3, 1)
-
-        for c in range(4):
-            for b in range(4):
-                widths = (512, 256, 256) if (c, b) == (3, 3) else (512, 512)
-                for j, n in enumerate(widths):
-                    mm2(c, b, sum(widths[:j]), n)
+        todo = [(m, 0) for m in range(2)] + [(m, 512) for m in range(2)] + [(m, n0) for m in range(2, 15) for n0 in (0, 512)]
+        for m in range(6, 16):
+            if m == 9:
+                x_reorder(6, "S")
+                x_reorder(7, "S")
+            for G in range(2):
+                if m in (6, 10) and G == 1:
+                    for mm in range(m + 2, m + 6):
+                        x_transpose(mm)
+                        x_out(mm, "S")
+                mm1(m, G)
+                h_out(m, G)
+                if (m, G) == (6, 0):
+                    e_quant(1, 1)
+                if m >= 12:
+                    h_quant(m - 1 + G, 1 - G, 1)
+                if (m, G) in ((6, 1), (7, 0), (10, 1), (11, 0)):
+                    x_quant(2 * m - 4 - 4 * (m // 10), 2)
+                mm2(*todo.pop(0))
+                if G == 0 and m < 14:
+                    mm2(*todo.pop(0))
+                if G == 0 and m % 2 == 0 and m < 12:
+                    h_quant(m - 2, 0, 2)
+                    h_quant(m - 2, 1, 2)
+            if m == 11:
+                h_quant(10, 0, 2)
+                h_quant(10, 1, 1)
+        h_quant(15, 1, 1)
+        for m, n0 in todo:
+            mm2(m, n0)
+        last = [(0, 512), (512, 256), (768, 256)]
+        for G in range(2):
+            for n0, n in last:
+                mm2_pass(15, n0, n, G)
+        for n0, n in last:
+            y_out(15, n0, n)

@@ -248,86 +248,80 @@ def tile_pointnet_set_encoder_s12_kernel(tc, x, w, u_words, u_scales, v_words, v
             if m % 8 == 7:
                 nc.sync.dma_start(out=out[128 * s : 128 * s + 128, n0 : n0 + n], in_=a)
 
-        nc.gpsimd.memset(v_pl[:].bitcast(I32), 0)
+        nc.vector.memset(v_pl[:].bitcast(I32), 0)
         nc.vector.memset(u_pl_raw[:].bitcast(I32), 0)
-        zero = sb([128, 512], BF16, "zero")
-        nc.vector.memset(zero[:], 0.0)
-        nc.sync.dma_start(out=u_raw[:].bitcast(I32), in_=u_words[0].bitcast(I32))
-        nc.sync.dma_start(out=v_w[:].bitcast(I32), in_=v_words[0].bitcast(I32))
+        make_identity(nc, ident[:])
         load_x(0)
-        for Q in range(4):
-            load_scales(nc.scalar, u_pl_raw, us32, Q)
-        load_scales(nc.scalar, v_pl, vs32, 3)
+        nc.sync.dma_start(out=u_raw[:].bitcast(I32), in_=u_words[0].bitcast(I32))
+        load_x(1)
         for Q in range(3):
             load_scales(nc.gpsimd, v_pl, vs32, Q)
-        make_identity(nc, ident[:])
-        load_w(0, 0)
-        load_w(1, 0)
-        load_x(1)
-        load_w(0, 1)
-        load_x(2)
-        load_w(1, 1)
-        for q in range(3, 8):
+        load_scales(nc.scalar, v_pl, vs32, 3)
+        for Q in range(4):
+            load_scales(nc.scalar, u_pl_raw, us32, Q)
+        nc.sync.dma_start(out=v_w[:].bitcast(I32), in_=v_words[0].bitcast(I32))
+        for G in range(2):
+            for g in range(2):
+                load_w(g, G)
+        for q in range(2, 8):
             load_x(q)
         warm = bank([128, 512])
-        spin(4, zero[:, 0:128], zero[:])
-        spin(2, ident[:], ident[:])
+        spin(4, ident[:], ident[:])
 
+        for q in range(2):
+            x_transpose(2 * q)
+            x_transpose(2 * q + 1)
+            spin((2, 1)[q], x_sb[0][:, 0:128], x_sb[0][:, 0:512])
+        x_out(0, "A")
         permute_u()
         permute_u_scales()
-        x_transpose(0)
-        x_transpose(1)
-        spin(2, x_sb[0][:, 0:128], x_sb[0][:, 0:512])
-        x_out(0, "A")
-        x_out(1, "S")
-        w_weave(0, 0, "V", 0, 4)
-        w_quant(0, 0)
-        w_weave(1, 0, "V", 0, 4)
+        x_out(1, "V")
+        x_out(2, "S")
         x_quant(0, 2)
-        for k in range(12):
-            if k == 6:
-                x_transpose(2)
-                x_transpose(3)
+        x_out(3, "S")
+        for k in range(13):
             e_mm(k // 4 % 2, k % 4 + k // 8 * 4)
             e_out(k // 4 % 2, k % 4 + k // 8 * 4, "S")
-        x_out(2, "V")
-        w_quant(1, 0)
-        x_out(3, "V")
-        w_weave(0, 1, "V", 0, 4)
-        x_quant(2, 2)
-        w_quant(0, 1)
-        w_weave(1, 1, "V", 0, 4)
+            if k == 0:
+                w_weave(0, 0, "V", 0, 4)
+                w_weave(1, 0, "V", 0, 4)
+                w_quant(0, 0)
+                w_quant(1, 0)
+                w_weave(0, 1, "V", 0, 4)
+                x_quant(2, 2)
+                w_quant(0, 1)
+                w_weave(1, 1, "V", 0, 4)
         for q in range(2):
             for m in (2 * q, 2 * q + 1):
                 mm1(m, 0)
                 h_out(m, 0)
             for m in (2 * q + 4, 2 * q + 5):
                 x_transpose(m)
-            x_out(2 * q + 4, "SV"[q])
-            x_out(2 * q + 5, "SV"[q])
-            if q == 0:
-                e_quant(0, 0)
-                w_quant(1, 1)
+        x_out(4, "V")
+        w_quant(1, 1)
+        x_out(5, "V")
+        x_out(6, "V")
         x_quant(4, 2)
-        e_quant(1, 0)
+        x_out(7, "V")
+        e_quant(0, 0)
         for m in range(4):
             mm1(m, 1)
             h_out(m, 1)
-            if m == 0:
-                x_quant(6, 2)
-                h_quant(0, 0, 4)
-                e_quant(0, 1)
+        e_quant(1, 0)
+        x_quant(6, 2)
+        h_quant(0, 0, 4)
+        h_quant(0, 1, 4)
         x_reorder(4, "V")
         for m in range(4, 6):
             for G in range(2):
                 mm1(m, G)
                 h_out(m, G)
-                e_mm(1, 2 * m - 4 + G)
-                e_out(1, 2 * m - 4 + G, "V")
-                if (m, G) == (4, 0):
-                    h_quant(0, 1, 4)
+                if (m, G) != (5, 1):
+                    e_mm(1, 2 * m - 3 + G)
+                    e_out(1, 2 * m - 3 + G, "VS"[G])
                 if (m, G) == (4, 1):
                     x_reorder(5, "V")
+        e_quant(0, 1)
 
         todo = [(m, 0) for m in range(2)] + [(m, 512) for m in range(2)] + [(m, n0) for m in range(2, 15) for n0 in (0, 512)]
         for m in range(6, 16):
@@ -359,9 +353,5 @@ def tile_pointnet_set_encoder_s12_kernel(tc, x, w, u_words, u_scales, v_words, v
         h_quant(15, 1, 1)
         for m, n0 in todo:
             mm2(m, n0)
-        last = [(0, 512), (512, 256), (768, 256)]
-        for G in range(2):
-            for n0, n in last:
-                mm2_pass(15, n0, n, G)
-        for n0, n in last:
-            y_out(15, n0, n)
+        for n0, n in ((0, 512), (512, 256), (768, 256)):
+            mm2(15, n0, n)

@@ -162,7 +162,7 @@ def tile_pointnet_set_encoder_s12_kernel(tc, x, w, u_words, u_scales, v_words, v
                 x_g[c] = sb([128, 4096], BF16, "x_g", 2)
             if engine == "A":
                 for g in range(2):
-                    k0 = 1024 * b + 512 * g
+                    k0 = 2048 * (b // 2) + 1024 * g + 512 * (b % 2)
                     nc.scalar.activation(
                         out=x_g[c][:, k0 : k0 + 512].rearrange("p (n u e) -> p n u e", u=2, e=2),
                         in_=banks["x", m][:, g].bitcast(BF16).rearrange("p u (n e) -> p n u e", e=2),
@@ -171,7 +171,7 @@ def tile_pointnet_set_encoder_s12_kernel(tc, x, w, u_words, u_scales, v_words, v
                 return
             copy(
                 engine,
-                x_g[c][:, 1024 * b : 1024 * b + 1024].bitcast(F32).rearrange("p (g n u) -> p g n u", g=2, u=2),
+                x_g[c][:].bitcast(F32).rearrange("p (q g b n u) -> p q b g n u", q=2, g=2, b=2, u=2)[:, b // 2, b % 2],
                 banks["x", m][:].rearrange("p g u n -> p g n u"),
             )
 
@@ -190,7 +190,8 @@ def tile_pointnet_set_encoder_s12_kernel(tc, x, w, u_words, u_scales, v_words, v
             h = bank([128, 4, 128])
             for t in range(4):
                 for g in range(2):
-                    k = slice(256 * b + 128 * g, 256 * b + 128 * g + 128)
+                    k0 = 512 * (b // 2) + 256 * g + 128 * (b % 2)
+                    k = slice(k0, k0 + 128)
                     nc.tensor.matmul_mx(
                         out=h[:, t, :],
                         lhsT=w_c[g, G][:, 128 * t : 128 * t + 128].bitcast(FP8X4),
@@ -210,6 +211,38 @@ def tile_pointnet_set_encoder_s12_kernel(tc, x, w, u_words, u_scales, v_words, v
                 nc.scalar.activation(out=dst, in_=src, func=RELU)
             else:
                 nc.vector.tensor_scalar_max(dst, src, 0.0)
+
+        h_half = {}
+
+        def mm1_wide(m, G, tp):
+            c, b = m // 4, m % 4
+            h = bank([128, 2, 256])
+            for tt in range(2):
+                t = 2 * tp + tt
+                for g in range(2):
+                    k = slice(256 * b + 256 * g, 256 * b + 256 * g + 256)
+                    nc.tensor.matmul_mx(
+                        out=h[:, tt, :],
+                        lhsT=w_c[g, G][:, 128 * t : 128 * t + 128].bitcast(FP8X4),
+                        lhsT_scale=w_s[g, G][:, 128 * t : 128 * t + 128],
+                        rhs=x_c[c][:, k].bitcast(FP8X4), rhs_scale=x_s[c][:, k],
+                        start=g == 0, stop=g == 1,
+                    )
+            if tp == 0:
+                h_half[m, G] = sb([128, 2, 512], BF16, "h_half", 2)
+            nc.scalar.activation(
+                out=h_half[m, G][:, tp, :].rearrange("p (n e) -> p n e", e=2), in_=h[:].rearrange("p e n -> p n e"), func=RELU
+            )
+
+        def h_zip(m, G, engine):
+            c, b = m // 4, m % 4
+            if b == 0:
+                h_t[c, G] = sb([128, 2048], BF16, "h_t", 4)
+            copy(
+                engine,
+                h_t[c, G][:, 512 * b : 512 * b + 1024].bitcast(F32).rearrange("p (n u) -> p n u", u=2),
+                h_half[m, G][:].bitcast(F32).rearrange("p u n -> p n u"),
+            )
 
         def h_quant(m, G, n):
             c, b = m // 4, m % 4
@@ -248,25 +281,31 @@ def tile_pointnet_set_encoder_s12_kernel(tc, x, w, u_words, u_scales, v_words, v
             if m % 8 == 7:
                 nc.sync.dma_start(out=out[128 * s : 128 * s + 128, n0 : n0 + n], in_=a)
 
+        zero = sb([128, 512], BF16, "zero")
         nc.vector.memset(v_pl[:].bitcast(I32), 0)
         nc.vector.memset(u_pl_raw[:].bitcast(I32), 0)
-        make_identity(nc, ident[:])
+        nc.vector.memset(zero[:], 0.0)
+        nc.vector.memset(ident[:], 0.0)
         load_x(0)
         nc.sync.dma_start(out=u_raw[:].bitcast(I32), in_=u_words[0].bitcast(I32))
         load_x(1)
         for Q in range(3):
             load_scales(nc.gpsimd, v_pl, vs32, Q)
+        make_identity(nc, ident[:], nomemset=True)
         load_scales(nc.scalar, v_pl, vs32, 3)
         for Q in range(4):
             load_scales(nc.scalar, u_pl_raw, us32, Q)
         nc.sync.dma_start(out=v_w[:].bitcast(I32), in_=v_words[0].bitcast(I32))
-        for G in range(2):
-            for g in range(2):
-                load_w(g, G)
-        for q in range(2, 8):
+        load_w(0, 0)
+        load_w(1, 0)
+        load_w(0, 1)
+        load_x(2)
+        load_w(1, 1)
+        load_x(3)
+        for q in range(4, 8):
             load_x(q)
         warm = bank([128, 512])
-        spin(4, ident[:], ident[:])
+        spin(4, zero[:, 0:128], zero[:])
 
         for q in range(2):
             x_transpose(2 * q)
@@ -324,32 +363,37 @@ def tile_pointnet_set_encoder_s12_kernel(tc, x, w, u_words, u_scales, v_words, v
         e_quant(0, 1)
 
         todo = [(m, 0) for m in range(2)] + [(m, 512) for m in range(2)] + [(m, n0) for m in range(2, 15) for n0 in (0, 512)]
+        WIDE = (8, 10)
         for m in range(6, 16):
-            if m == 9:
-                x_reorder(6, "S")
-                x_reorder(7, "S")
             for G in range(2):
                 if m in (6, 10) and G == 1:
                     for mm in range(m + 2, m + 6):
                         x_transpose(mm)
                         x_out(mm, "S")
-                mm1(m, G)
-                h_out(m, G)
+                if m - m % 2 in WIDE:
+                    mm1_wide(m - m % 2, m % 2, G)
+                else:
+                    mm1(m, G)
+                    h_out(m, G)
                 if (m, G) == (6, 0):
                     e_quant(1, 1)
-                if m >= 12:
+                if m >= 13 or (m, G) == (12, 1):
                     h_quant(m - 1 + G, 1 - G, 1)
                 if (m, G) in ((6, 1), (7, 0), (10, 1), (11, 0)):
                     x_quant(2 * m - 4 - 4 * (m // 10), 2)
+                if m == 8:
+                    x_reorder(6 + G, "S")
+                zipped = G == 0 and (m - 1) - (m - 1) % 2 in WIDE
+                if zipped:
+                    h_zip((m - 1) - (m - 1) % 2, (m - 1) % 2, "V")
                 mm2(*todo.pop(0))
+                if zipped:
+                    h_quant((m - 1) - (m - 1) % 2, (m - 1) % 2, 2)
                 if G == 0 and m < 14:
                     mm2(*todo.pop(0))
-                if G == 0 and m % 2 == 0 and m < 12:
+                if G == 0 and m in (6, 8):
                     h_quant(m - 2, 0, 2)
                     h_quant(m - 2, 1, 2)
-            if m == 11:
-                h_quant(10, 0, 2)
-                h_quant(10, 1, 1)
         h_quant(15, 1, 1)
         for m, n0 in todo:
             mm2(m, n0)

@@ -32,10 +32,6 @@ def tile_pointnet_set_encoder_s12_kernel(tc, x, w, u_words, u_scales, v_words, v
             t = psum.tile(shape, F32, name="bank", tag="bank", bufs=8)
             return t
 
-        def spin(n, lhsT, rhs):
-            for i in range(n):
-                nc.tensor.matmul(warm[:, 0 : rhs.shape[1]], lhsT=lhsT, rhs=rhs, start=True, stop=True)
-
         def pairs(a, b):
             return [(i, j) for i in range(a) for j in range(b)]
 
@@ -281,10 +277,8 @@ def tile_pointnet_set_encoder_s12_kernel(tc, x, w, u_words, u_scales, v_words, v
             if m % 8 == 7:
                 nc.sync.dma_start(out=out[128 * s : 128 * s + 128, n0 : n0 + n], in_=a)
 
-        zero = sb([128, 512], BF16, "zero")
         nc.vector.memset(v_pl[:].bitcast(I32), 0)
         nc.vector.memset(u_pl_raw[:].bitcast(I32), 0)
-        nc.vector.memset(zero[:], 0.0)
         nc.vector.memset(ident[:], 0.0)
         load_x(0)
         nc.sync.dma_start(out=u_raw[:].bitcast(I32), in_=u_words[0].bitcast(I32))
@@ -304,13 +298,10 @@ def tile_pointnet_set_encoder_s12_kernel(tc, x, w, u_words, u_scales, v_words, v
         load_x(3)
         for q in range(4, 8):
             load_x(q)
-        warm = bank([128, 512])
-        spin(4, zero[:, 0:128], zero[:])
 
         for q in range(2):
             x_transpose(2 * q)
             x_transpose(2 * q + 1)
-            spin((2, 1)[q], x_sb[0][:, 0:128], x_sb[0][:, 0:512])
         x_out(0, "A")
         permute_u()
         permute_u_scales()

@@ -157,13 +157,16 @@ def tile_pointnet_set_encoder_s12_kernel(tc, x, w, u_words, u_scales, v_words, v
             if b == 0:
                 x_g[c] = sb([128, 4096], BF16, "x_g", 2)
             if engine == "A":
-                for g in range(2):
-                    k0 = 2048 * (b // 2) + 1024 * g + 512 * (b % 2)
-                    nc.scalar.activation(
-                        out=x_g[c][:, k0 : k0 + 512].rearrange("p (n u e) -> p n u e", u=2, e=2),
-                        in_=banks["x", m][:, g].bitcast(BF16).rearrange("p u (n e) -> p n u e", e=2),
-                        func=COPY,
-                    )
+                k0 = 2048 * (b // 2) + 512 * (b % 2)
+                nc.scalar.activation(
+                    out=x_g[c][:, k0 : k0 + 512].rearrange("p (n u e) -> p n u e", u=2, e=2),
+                    in_=banks["x", m][:, 0].bitcast(BF16).rearrange("p u (n e) -> p n u e", e=2),
+                    func=COPY,
+                )
+                nc.scalar.copy(
+                    x_g[c][:, k0 + 1024 : k0 + 1536].bitcast(F32).rearrange("p (n u) -> p n u", u=2),
+                    banks["x", m][:, 1].rearrange("p u n -> p n u"),
+                )
                 return
             copy(
                 engine,
@@ -281,8 +284,8 @@ def tile_pointnet_set_encoder_s12_kernel(tc, x, w, u_words, u_scales, v_words, v
         nc.vector.memset(u_pl_raw[:].bitcast(I32), 0)
         nc.vector.memset(ident[:], 0.0)
         load_x(0)
-        nc.sync.dma_start(out=u_raw[:].bitcast(I32), in_=u_words[0].bitcast(I32))
         load_x(1)
+        nc.sync.dma_start(out=u_raw[:].bitcast(I32), in_=u_words[0].bitcast(I32))
         for Q in range(3):
             load_scales(nc.gpsimd, v_pl, vs32, Q)
         make_identity(nc, ident[:], nomemset=True)
@@ -303,15 +306,15 @@ def tile_pointnet_set_encoder_s12_kernel(tc, x, w, u_words, u_scales, v_words, v
             x_transpose(2 * q)
             x_transpose(2 * q + 1)
         x_out(0, "A")
-        permute_u()
         permute_u_scales()
+        permute_u()
         x_out(1, "V")
         x_out(2, "S")
         x_quant(0, 2)
         x_out(3, "S")
-        for k in range(13):
+        for k in range(15):
             e_mm(k // 4 % 2, k % 4 + k // 8 * 4)
-            e_out(k // 4 % 2, k % 4 + k // 8 * 4, "S")
+            e_out(k // 4 % 2, k % 4 + k // 8 * 4, "V" if k == 0 else "S")
             if k == 0:
                 w_weave(0, 0, "V", 0, 4)
                 w_weave(1, 0, "V", 0, 4)
@@ -346,9 +349,9 @@ def tile_pointnet_set_encoder_s12_kernel(tc, x, w, u_words, u_scales, v_words, v
             for G in range(2):
                 mm1(m, G)
                 h_out(m, G)
-                if (m, G) != (5, 1):
-                    e_mm(1, 2 * m - 3 + G)
-                    e_out(1, 2 * m - 3 + G, "VS"[G])
+                if 2 * m + G < 9:
+                    e_mm(1, 2 * m + G - 1)
+                    e_out(1, 2 * m + G - 1, "VS"[G])
                 if (m, G) == (4, 1):
                     x_reorder(5, "V")
         e_quant(0, 1)
@@ -377,8 +380,10 @@ def tile_pointnet_set_encoder_s12_kernel(tc, x, w, u_words, u_scales, v_words, v
                 zipped = G == 0 and (m - 1) - (m - 1) % 2 in WIDE
                 if zipped:
                     h_zip((m - 1) - (m - 1) % 2, (m - 1) % 2, "V")
+                if zipped and m == 12:
+                    h_quant(10, 1, 2)
                 mm2(*todo.pop(0))
-                if zipped:
+                if zipped and m < 12:
                     h_quant((m - 1) - (m - 1) % 2, (m - 1) % 2, 2)
                 if G == 0 and m < 14:
                     mm2(*todo.pop(0))

@@ -228,7 +228,7 @@ def tile_pointnet_set_encoder_s12_kernel(tc, x, w, u_words, u_scales, v_words, v
                         start=g == 0, stop=g == 1,
                     )
             if tp == 0:
-                h_half[m, G] = sb([128, 2, 512], BF16, "h_half", 2)
+                h_half[m, G] = sb([128, 2, 512], BF16, "h_half", 3)
             nc.scalar.activation(
                 out=h_half[m, G][:, tp, :].rearrange("p (n e) -> p n e", e=2), in_=h[:].rearrange("p e n -> p n e"), func=RELU
             )
@@ -239,8 +239,8 @@ def tile_pointnet_set_encoder_s12_kernel(tc, x, w, u_words, u_scales, v_words, v
                 h_t[c, G] = sb([128, 2048], BF16, "h_t", 4)
             copy(
                 engine,
-                h_t[c, G][:, 512 * b : 512 * b + 1024].bitcast(F32).rearrange("p (n u) -> p n u", u=2),
-                h_half[m, G][:].bitcast(F32).rearrange("p u n -> p n u"),
+                h_t[c, G][:, 512 * b : 512 * b + 1024].bitcast(F32).rearrange("p (n i u) -> p n u i", i=2, u=2),
+                h_half[m, G][:].bitcast(F32).rearrange("p u (n i) -> p n u i", i=2),
             )
 
         def h_quant(m, G, n):
@@ -342,8 +342,8 @@ def tile_pointnet_set_encoder_s12_kernel(tc, x, w, u_words, u_scales, v_words, v
             h_out(m, 1)
         e_quant(1, 0)
         x_quant(6, 2)
-        h_quant(0, 0, 4)
-        h_quant(0, 1, 4)
+        h_quant(0, 0, 2)
+        h_quant(0, 1, 2)
         x_reorder(4, "V")
         for m in range(4, 6):
             for G in range(2):
@@ -357,7 +357,7 @@ def tile_pointnet_set_encoder_s12_kernel(tc, x, w, u_words, u_scales, v_words, v
         e_quant(0, 1)
 
         todo = [(m, 0) for m in range(2)] + [(m, 512) for m in range(2)] + [(m, n0) for m in range(2, 15) for n0 in (0, 512)]
-        WIDE = (8, 10)
+        WIDE = (6, 8, 10)
         for m in range(6, 16):
             for G in range(2):
                 if m in (6, 10) and G == 1:
@@ -366,6 +366,8 @@ def tile_pointnet_set_encoder_s12_kernel(tc, x, w, u_words, u_scales, v_words, v
                         x_out(mm, "S")
                 if m - m % 2 in WIDE:
                     mm1_wide(m - m % 2, m % 2, G)
+                    if G == 1 and m in (8, 9):
+                        h_zip(m - m % 2, m % 2, "S")
                 else:
                     mm1(m, G)
                     h_out(m, G)
@@ -378,18 +380,20 @@ def tile_pointnet_set_encoder_s12_kernel(tc, x, w, u_words, u_scales, v_words, v
                 if m == 8:
                     x_reorder(6 + G, "S")
                 zipped = G == 0 and (m - 1) - (m - 1) % 2 in WIDE
-                if zipped:
+                if zipped and m - 1 not in (8, 9):
                     h_zip((m - 1) - (m - 1) % 2, (m - 1) % 2, "V")
-                if zipped and m == 12:
-                    h_quant(10, 1, 2)
+                if zipped and m in (12,):
+                    h_quant(m - 2, 1, 2)
                 mm2(*todo.pop(0))
-                if zipped and m < 12:
+                if zipped and m not in (12,):
                     h_quant((m - 1) - (m - 1) % 2, (m - 1) % 2, 2)
                 if G == 0 and m < 14:
                     mm2(*todo.pop(0))
-                if G == 0 and m in (6, 8):
-                    h_quant(m - 2, 0, 2)
-                    h_quant(m - 2, 1, 2)
+                if G == 0 and m == 6:
+                    h_quant(2, 0, 2)
+                    h_quant(2, 1, 2)
+                    h_quant(4, 0, 2)
+                    h_quant(4, 1, 2)
         h_quant(15, 1, 1)
         for m, n0 in todo:
             mm2(m, n0)

@@ -284,8 +284,8 @@ def tile_pointnet_set_encoder_s12_kernel(tc, x, w, u_words, u_scales, v_words, v
         nc.vector.memset(u_pl_raw[:].bitcast(I32), 0)
         nc.vector.memset(ident[:], 0.0)
         load_x(0)
-        load_x(1)
         nc.sync.dma_start(out=u_raw[:].bitcast(I32), in_=u_words[0].bitcast(I32))
+        load_x(1)
         for Q in range(3):
             load_scales(nc.gpsimd, v_pl, vs32, Q)
         make_identity(nc, ident[:], nomemset=True)
@@ -347,8 +347,7 @@ def tile_pointnet_set_encoder_s12_kernel(tc, x, w, u_words, u_scales, v_words, v
         x_reorder(4, "V")
         for m in range(4, 6):
             for G in range(2):
-                mm1(m, G)
-                h_out(m, G)
+                mm1_wide(4, m % 2, G)
                 if 2 * m + G < 9:
                     e_mm(1, 2 * m + G - 1)
                     e_out(1, 2 * m + G - 1, "VS"[G])
@@ -392,6 +391,8 @@ def tile_pointnet_set_encoder_s12_kernel(tc, x, w, u_words, u_scales, v_words, v
                 if G == 0 and m == 6:
                     h_quant(2, 0, 2)
                     h_quant(2, 1, 2)
+                    h_zip(4, 0, "V")
+                    h_zip(4, 1, "V")
                     h_quant(4, 0, 2)
                     h_quant(4, 1, 2)
         h_quant(15, 1, 1)

@@ -16,6 +16,9 @@ MAX = mybir.AluOpType.max
 RELU = mybir.ActivationFunctionType.Relu
 COPY = mybir.ActivationFunctionType.Copy
 
+PE_PAIRS = 4
+WIDE = (6,)
+
 
 def tile_pointnet_set_encoder_s12_kernel(tc, x, w, u_words, u_scales, v_words, v_scales, out):
     nc = tc.nc
@@ -32,8 +35,7 @@ def tile_pointnet_set_encoder_s12_kernel(tc, x, w, u_words, u_scales, v_words, v
             t = psum.tile(shape, F32, name="bank", tag="bank", bufs=8)
             return t
 
-        def pairs(a, b):
-            return [(i, j) for i in range(a) for j in range(b)]
+        quarters = [(i, j) for i in range(2) for j in range(2)]
 
         u_raw = sb([128, 2048], U8, "u_raw")
         u_w = sb([128, 2048], U8, "u_w")
@@ -42,31 +44,46 @@ def tile_pointnet_set_encoder_s12_kernel(tc, x, w, u_words, u_scales, v_words, v
         v_w = sb([128, 2048], U8, "v_w")
         v_pl = sb([128, 1024], U8, "v_pl")
         ident = sb([128, 128], F32, "ident")
-        x_sb = [sb([128, 2048], BF16, "x_sb%d" % q) for q in range(8)]
-        x_c = [sb([128, 1024], U32, "x_c%d" % c) for c in range(4)]
-        x_s = [sb([128, 1024], U8, "x_s%d" % c) for c in range(4)]
-        w_raw = {k: sb([128, 4, 512], BF16, "w_raw%d%d" % k) for k in pairs(2, 2)}
-        w_grp = {k: sb([128, 2048], BF16, "w_grp%d%d" % k) for k in pairs(2, 2)}
-        w_c = {k: sb([128, 512], U32, "w_c%d%d" % k) for k in pairs(2, 2)}
-        w_s = {k: sb([128, 512], U8, "w_s%d%d" % k) for k in pairs(2, 2)}
-        e_grp = {k: sb([128, 2048], BF16, "e_grp%d%d" % k) for k in pairs(2, 2)}
-        e_c = {k: sb([128, 512], U32, "e_c%d%d" % k) for k in pairs(2, 2)}
-        e_s = {k: sb([128, 512], U8, "e_s%d%d" % k) for k in pairs(2, 2)}
-        h_c = {k: sb([128, 512], U32, "h_c%d%d" % k) for k in pairs(4, 2)}
-        h_s = {k: sb([128, 512], U8, "h_s%d%d" % k) for k in pairs(4, 2)}
+        x_sb = [sb([128, 2048], BF16, "x_sb%d" % q) for q in range(PE_PAIRS)]
+        x_c = [sb([128, 512], U32, "x_c%d" % q) for q in range(8)]
+        x_s = [sb([128, 512], U8, "x_s%d" % q) for q in range(8)]
+        w_raw = {k: sb([128, 4, 512], BF16, "w_raw%d%d" % k) for k in quarters}
+        w_grp = {k: sb([128, 2048], BF16, "w_grp%d%d" % k) for k in quarters}
+        w_c = {k: sb([128, 512], U32, "w_c%d%d" % k) for k in quarters}
+        w_s = {k: sb([128, 512], U8, "w_s%d%d" % k) for k in quarters}
+        e_grp = {k: sb([128, 2048], BF16, "e_grp%d%d" % k) for k in quarters}
+        e_c = {k: sb([128, 512], U32, "e_c%d%d" % k) for k in quarters}
+        e_s = {k: sb([128, 512], U8, "e_s%d%d" % k) for k in quarters}
+        h_c = [sb([128, 512], U32, "h_c%d" % q) for q in range(8)]
+        h_s = [sb([128, 512], U8, "h_s%d" % q) for q in range(8)]
         acc = [sb([128, 1024], F32, "acc%d" % s) for s in range(2)]
 
         us32 = u_scales[0].bitcast(I32)
         vs32 = v_scales[0].bitcast(I32)
-        xv = x.rearrange("(s i b) k -> s i b k", s=2, i=128, b=8)
-        wv = w.rearrange("(g p j) f -> g p j f", g=2, p=128, j=4)
+        x_rows = x.rearrange("(s i b) k -> s i b k", s=2, i=128, b=8)
+        x_quads = x.rearrange("(s c i b) (g Q k) -> s c Q i b g k", s=2, c=4, i=32, b=8, g=2, Q=4)
+        w_rows = w.rearrange("(g p j) f -> g p j f", g=2, p=128, j=4)
 
         def load_x(q):
             s, b = q // 4, 2 * (q % 4)
-            nc.sync.dma_start(out=x_sb[q][:].rearrange("p (b k) -> p b k", b=2), in_=xv[s][:, b : b + 2, :])
+            nc.sync.dma_start(out=x_sb[q][:].rearrange("p (b k) -> p b k", b=2), in_=x_rows[s][:, b : b + 2, :])
+
+        x_q = {}
+
+        def load_x_quads(q0, n):
+            s, b = q0 // 4, 2 * (q0 % 4)
+            t = sb([128, 2048 * n], BF16, "x_q%d" % q0)
+            for c in range(4):
+                for Q in (0, 2, 1, 3):
+                    nc.sync.dma_start(
+                        out=t[32 * Q : 32 * Q + 32, :].rearrange("p (a c k) -> p a c k", c=4, k=128)[:, :, c, :],
+                        in_=x_quads[s, c, Q][:, b : b + 2 * n].rearrange("i b g k -> i (b g) k"),
+                    )
+            for j in range(n):
+                x_q[q0 + j] = t[:, 2048 * j : 2048 * j + 2048]
 
         def load_w(g, G):
-            nc.sync.dma_start(out=w_raw[g, G][:], in_=wv[g][:, :, 512 * G : 512 * G + 512])
+            nc.sync.dma_start(out=w_raw[g, G][:], in_=w_rows[g][:, :, 512 * G : 512 * G + 512])
 
         def load_scales(engine, plane, rows, Q):
             engine.dma_start(out=plane[32 * Q : 32 * Q + 4, :].bitcast(I32), in_=rows[4 * Q : 4 * Q + 4, :])
@@ -74,8 +91,6 @@ def tile_pointnet_set_encoder_s12_kernel(tc, x, w, u_words, u_scales, v_words, v
         def copy(engine, out, in_):
             if engine == "S":
                 nc.scalar.copy(out, in_)
-            elif engine == "A":
-                nc.scalar.activation(out=out, in_=in_, func=COPY)
             else:
                 nc.vector.tensor_copy(out=out, in_=in_)
 
@@ -91,21 +106,19 @@ def tile_pointnet_set_encoder_s12_kernel(tc, x, w, u_words, u_scales, v_words, v
                 in_=u_pl_raw[:].bitcast(I32).rearrange("p (G q t) -> p G t q", G=2, q=32, t=4),
             )
 
-        def w_weave(g, G, engine, t0, nt):
-            dst = w_grp[g, G][:].rearrange("p (t q r j) -> p t q j r", t=4, q=32, r=4, j=4)
-            src = w_raw[g, G][:].rearrange("p j (q t r) -> p t q j r", q=32, t=4, r=4)
-            if engine == "V":
-                nc.vector.tensor_copy(out=dst[:, t0 : t0 + nt], in_=src[:, t0 : t0 + nt])
-            else:
-                for t in range(t0, t0 + nt):
-                    nc.scalar.activation(out=dst[:, t], in_=src[:, t], func=COPY)
+        def w_weave(g, G):
+            nc.vector.tensor_copy(
+                out=w_grp[g, G][:].rearrange("p (t q r j) -> p t q j r", t=4, q=32, r=4, j=4),
+                in_=w_raw[g, G][:].rearrange("p j (q t r) -> p t q j r", q=32, t=4, r=4),
+            )
 
         def w_quant(g, G):
             nc.vector.quantize_mx(out=w_c[g, G][:].bitcast(FP8X4), scales=w_s[g, G][:], in_=w_grp[g, G][:])
 
         banks = {}
 
-        def e_mm(G, nb):
+        def e_mm(k):
+            G, nb = k // 4 % 2, k % 4 + k // 8 * 4
             e = bank([128, 4, 128])
             for t in range(4):
                 c0 = G * 512 + t * 128
@@ -115,96 +128,111 @@ def tile_pointnet_set_encoder_s12_kernel(tc, x, w, u_words, u_scales, v_words, v
                     rhs=v_w[:, 256 * nb : 256 * nb + 256].bitcast(FP4X4), rhs_scale=v_pl[:, 128 * nb : 128 * nb + 128],
                     start=t == 0, stop=t == 3,
                 )
-            banks["e", G, nb] = e
+            banks["e", k] = e
 
-        def e_out(G, nb, engine):
-            j = nb % 4
+        def e_out(k, engine):
+            j = k % 4
             copy(
                 engine,
-                e_grp[G, nb // 4][:, 512 * j : 512 * j + 512].rearrange("p (n t) -> p n t", t=4),
-                banks["e", G, nb][:].rearrange("p t n -> p n t"),
+                e_grp[k // 4 % 2, k // 8][:, 512 * j : 512 * j + 512].rearrange("p (n t) -> p n t", t=4),
+                banks["e", k][:].rearrange("p t n -> p n t"),
             )
 
         def e_quant(G, nh):
             nc.vector.quantize_mx(out=e_c[G, nh][:].bitcast(FP8X4), scales=e_s[G, nh][:], in_=e_grp[G, nh][:])
 
-        x_r = {}
         x_g = {}
 
-        def x_reorder(q, engine):
-            x_r[q] = sb([128, 1024], F32, "x_r", 4)
-            copy(
-                engine,
-                x_r[q][:].rearrange("p (a u w) -> p a u w", u=2, w=128),
-                x_sb[q][:].bitcast(F32).rearrange("p (a w u) -> p a u w", u=2, w=128),
-            )
-
         def x_transpose(m):
-            q = m // 2
             xt = bank([128, 2, 2, 128])
             for g in range(2):
                 base = (m % 2) * 512 + g * 256
                 for u in range(2):
-                    if q in x_r:
-                        words = x_r[q][:, base + 128 * u : base + 128 * u + 128]
-                    else:
-                        words = x_sb[q][:].bitcast(F32)[:, base + u : base + 256 : 2]
-                    nc.tensor.transpose(xt[:, g, u, :], words, ident[:])
+                    nc.tensor.transpose(xt[:, g, u, :], x_sb[m // 2][:].bitcast(F32)[:, base + u : base + 256 : 2], ident[:])
             banks["x", m] = xt
 
         def x_out(m, engine):
-            c, b = m // 4, m % 4
+            q, b = m // 2, m % 2
             if b == 0:
-                x_g[c] = sb([128, 4096], BF16, "x_g", 2)
+                x_g[q] = sb([128, 2048], BF16, "x_g", 3)
             if engine == "A":
-                k0 = 2048 * (b // 2) + 512 * (b % 2)
                 nc.scalar.activation(
-                    out=x_g[c][:, k0 : k0 + 512].rearrange("p (n u e) -> p n u e", u=2, e=2),
+                    out=x_g[q][:, 1024 * b : 1024 * b + 512].rearrange("p (n u e) -> p n u e", u=2, e=2),
                     in_=banks["x", m][:, 0].bitcast(BF16).rearrange("p u (n e) -> p n u e", e=2),
                     func=COPY,
                 )
                 nc.scalar.copy(
-                    x_g[c][:, k0 + 1024 : k0 + 1536].bitcast(F32).rearrange("p (n u) -> p n u", u=2),
+                    x_g[q][:, 1024 * b + 512 : 1024 * b + 1024].bitcast(F32).rearrange("p (n u) -> p n u", u=2),
                     banks["x", m][:, 1].rearrange("p u n -> p n u"),
                 )
                 return
             copy(
                 engine,
-                x_g[c][:].bitcast(F32).rearrange("p (q g b n u) -> p q b g n u", q=2, g=2, b=2, u=2)[:, b // 2, b % 2],
+                x_g[q][:, 1024 * b : 1024 * b + 1024].bitcast(F32).rearrange("p (g n u) -> p g n u", g=2, u=2),
                 banks["x", m][:].rearrange("p g u n -> p g n u"),
             )
 
-        def x_quant(m, n):
-            c, b = m // 4, m % 4
-            nc.vector.quantize_mx(
-                out=x_c[c][:, 256 * b : 256 * (b + n)].bitcast(FP8X4),
-                scales=x_s[c][:, 256 * b : 256 * (b + n)],
-                in_=x_g[c][:, 1024 * b : 1024 * (b + n)],
+        x_r = {}
+        x_t = {}
+
+        def x_split(q, engine="S"):
+            x_r[q] = sb([128, 1024], F32, "x_r", 2)
+            copy(
+                engine,
+                x_r[q][:].rearrange("p (a u j) -> p a u j", u=2, j=32),
+                x_q[q].bitcast(F32).rearrange("p (a j u) -> p a u j", u=2, j=32),
             )
+
+        def x_turn(q):
+            x_t[q] = sb([128, 1024], F32, "x_t", 2)
+            nc.vector.transpose(x_t[q][:], x_r[q][:])
+
+        def x_join(q, engine="S"):
+            x_g[q] = sb([128, 2048], BF16, "x_g", 3)
+            if q in WIDE:
+                for g in range(2):
+                    copy(
+                        engine,
+                        x_g[q][:, 1024 * g : 1024 * g + 1024].bitcast(F32).rearrange("p (b c i u) -> p b c i u", b=2, u=2, i=32),
+                        x_t[q][:].rearrange("p (b g c u i) -> p g b c i u", b=2, g=2, u=2, i=32)[:, g],
+                    )
+            else:
+                copy(
+                    engine,
+                    x_g[q][:].bitcast(F32).rearrange("p (a i u) -> p a i u", u=2, i=32),
+                    x_t[q][:].rearrange("p (a u i) -> p a i u", u=2, i=32),
+                )
+
+        def x_quant(q):
+            nc.vector.quantize_mx(out=x_c[q][:].bitcast(FP8X4), scales=x_s[q][:], in_=x_g[q][:])
 
         h_t = {}
 
         def mm1(m, G):
-            c, b = m // 4, m % 4
             h = bank([128, 4, 128])
             for t in range(4):
                 for g in range(2):
-                    k0 = 512 * (b // 2) + 256 * g + 128 * (b % 2)
-                    k = slice(k0, k0 + 128)
+                    k = slice(256 * (m % 2) + 128 * g, 256 * (m % 2) + 128 * g + 128)
                     nc.tensor.matmul_mx(
                         out=h[:, t, :],
                         lhsT=w_c[g, G][:, 128 * t : 128 * t + 128].bitcast(FP8X4),
                         lhsT_scale=w_s[g, G][:, 128 * t : 128 * t + 128],
-                        rhs=x_c[c][:, k].bitcast(FP8X4), rhs_scale=x_s[c][:, k],
+                        rhs=x_c[m // 2][:, k].bitcast(FP8X4), rhs_scale=x_s[m // 2][:, k],
                         start=g == 0, stop=g == 1,
                     )
             banks["h", m, G] = h
 
+        def part(m, G):
+            return 2 * G + m % 2 if m // 2 in WIDE else 2 * (m % 2) + G
+
+        def h_tile(q):
+            if q not in h_t:
+                h_t[q] = sb([128, 2048], BF16, "h_t", 3)
+            return h_t[q]
+
         def h_out(m, G, engine="S"):
-            c, b = m // 4, m % 4
-            if b == 0:
-                h_t[c, G] = sb([128, 2048], BF16, "h_t", 4)
-            dst = h_t[c, G][:, 512 * b : 512 * b + 512].rearrange("p (n t) -> p n t", t=4)
+            j = part(m, G)
+            dst = h_tile(m // 2)[:, 512 * j : 512 * j + 512].rearrange("p (n t) -> p n t", t=4)
             src = banks["h", m, G][:].rearrange("p t n -> p n t")
             if engine == "S":
                 nc.scalar.activation(out=dst, in_=src, func=RELU)
@@ -213,63 +241,57 @@ def tile_pointnet_set_encoder_s12_kernel(tc, x, w, u_words, u_scales, v_words, v
 
         h_half = {}
 
-        def mm1_wide(m, G, tp):
-            c, b = m // 4, m % 4
+        def mm1_wide(q, G, tp):
             h = bank([128, 2, 256])
             for tt in range(2):
                 t = 2 * tp + tt
                 for g in range(2):
-                    k = slice(256 * b + 256 * g, 256 * b + 256 * g + 256)
+                    k = slice(256 * g, 256 * g + 256)
                     nc.tensor.matmul_mx(
                         out=h[:, tt, :],
                         lhsT=w_c[g, G][:, 128 * t : 128 * t + 128].bitcast(FP8X4),
                         lhsT_scale=w_s[g, G][:, 128 * t : 128 * t + 128],
-                        rhs=x_c[c][:, k].bitcast(FP8X4), rhs_scale=x_s[c][:, k],
+                        rhs=x_c[q][:, k].bitcast(FP8X4), rhs_scale=x_s[q][:, k],
                         start=g == 0, stop=g == 1,
                     )
+            banks["h", q, G, tp] = h
+
+        def h_out_wide(q, G, tp):
             if tp == 0:
-                h_half[m, G] = sb([128, 2, 512], BF16, "h_half", 3)
+                h_half[q, G] = sb([128, 2, 512], BF16, "h_half", 2)
             nc.scalar.activation(
-                out=h_half[m, G][:, tp, :].rearrange("p (n e) -> p n e", e=2), in_=h[:].rearrange("p e n -> p n e"), func=RELU
+                out=h_half[q, G][:, tp, :].rearrange("p (n e) -> p n e", e=2),
+                in_=banks["h", q, G, tp][:].rearrange("p e n -> p n e"), func=RELU,
             )
 
-        def h_zip(m, G, engine):
-            c, b = m // 4, m % 4
-            if b == 0:
-                h_t[c, G] = sb([128, 2048], BF16, "h_t", 4)
+        def h_zip(q, G, engine):
             copy(
                 engine,
-                h_t[c, G][:, 512 * b : 512 * b + 1024].bitcast(F32).rearrange("p (n i u) -> p n u i", i=2, u=2),
-                h_half[m, G][:].bitcast(F32).rearrange("p u (n i) -> p n u i", i=2),
+                h_tile(q)[:, 1024 * G : 1024 * G + 1024].bitcast(F32).rearrange("p (n i u) -> p n u i", i=2, u=2),
+                h_half[q, G][:].bitcast(F32).rearrange("p u (n i) -> p n u i", i=2),
             )
 
-        def h_quant(m, G, n):
-            c, b = m // 4, m % 4
+        def h_quant(q, j0, n):
             nc.vector.quantize_mx(
-                out=h_c[c, G][:, 128 * b : 128 * (b + n)].bitcast(FP8X4),
-                scales=h_s[c, G][:, 128 * b : 128 * (b + n)],
-                in_=h_t[c, G][:, 512 * b : 512 * (b + n)],
-            )
-
-        def mm2_pass(m, n0, n, G):
-            c, b = m // 4, m % 4
-            if G == 0:
-                banks["y", m, n0] = bank([128, n])
-            rows = slice(128 * b, 128 * b + 128)
-            nh, j0 = n0 // 512, n0 % 512
-            nc.tensor.matmul_mx(
-                out=banks["y", m, n0][:],
-                lhsT=h_c[c, G][:, rows].bitcast(FP8X4), lhsT_scale=h_s[c, G][:, rows],
-                rhs=e_c[G, nh][:, j0 : j0 + n].bitcast(FP8X4), rhs_scale=e_s[G, nh][:, j0 : j0 + n],
-                start=G == 0, stop=G == 1,
+                out=h_c[q][:, 128 * j0 : 128 * (j0 + n)].bitcast(FP8X4),
+                scales=h_s[q][:, 128 * j0 : 128 * (j0 + n)],
+                in_=h_t[q][:, 512 * j0 : 512 * (j0 + n)],
             )
 
         def mm2(m, n0, n=512):
-            mm2_pass(m, n0, n, 0)
-            mm2_pass(m, n0, n, 1)
-            y_out(m, n0, n)
+            y = bank([128, n])
+            nh, j0 = n0 // 512, n0 % 512
+            for G in range(2):
+                k = slice(128 * part(m, G), 128 * part(m, G) + 128)
+                nc.tensor.matmul_mx(
+                    out=y[:],
+                    lhsT=h_c[m // 2][:, k].bitcast(FP8X4), lhsT_scale=h_s[m // 2][:, k],
+                    rhs=e_c[G, nh][:, j0 : j0 + n].bitcast(FP8X4), rhs_scale=e_s[G, nh][:, j0 : j0 + n],
+                    start=G == 0, stop=G == 1,
+                )
+            banks["y", m, n0] = y
 
-        def y_out(m, n0, n):
+        def y_out(m, n0, n=512):
             y = banks["y", m, n0]
             s = m // 8
             a = acc[s][:, n0 : n0 + n]
@@ -299,31 +321,30 @@ def tile_pointnet_set_encoder_s12_kernel(tc, x, w, u_words, u_scales, v_words, v
         load_x(2)
         load_w(1, 1)
         load_x(3)
-        for q in range(4, 8):
-            load_x(q)
+        load_x_quads(4, 2)
+        load_x_quads(6, 2)
 
-        for q in range(2):
-            x_transpose(2 * q)
-            x_transpose(2 * q + 1)
+        for m in range(4):
+            x_transpose(m)
         x_out(0, "A")
         permute_u_scales()
         permute_u()
         x_out(1, "V")
         x_out(2, "S")
-        x_quant(0, 2)
+        x_quant(0)
         x_out(3, "S")
         for k in range(15):
-            e_mm(k // 4 % 2, k % 4 + k // 8 * 4)
-            e_out(k // 4 % 2, k % 4 + k // 8 * 4, "V" if k == 0 else "S")
+            e_mm(k)
+            e_out(k, "V" if k == 0 else "S")
             if k == 0:
-                w_weave(0, 0, "V", 0, 4)
-                w_weave(1, 0, "V", 0, 4)
+                w_weave(0, 0)
+                w_weave(1, 0)
                 w_quant(0, 0)
                 w_quant(1, 0)
-                w_weave(0, 1, "V", 0, 4)
-                x_quant(2, 2)
+                w_weave(0, 1)
+                x_quant(1)
                 w_quant(0, 1)
-                w_weave(1, 1, "V", 0, 4)
+                w_weave(1, 1)
         for q in range(2):
             for m in (2 * q, 2 * q + 1):
                 mm1(m, 0)
@@ -334,69 +355,64 @@ def tile_pointnet_set_encoder_s12_kernel(tc, x, w, u_words, u_scales, v_words, v
         w_quant(1, 1)
         x_out(5, "V")
         x_out(6, "V")
-        x_quant(4, 2)
+        x_quant(2)
         x_out(7, "V")
         e_quant(0, 0)
         for m in range(4):
             mm1(m, 1)
             h_out(m, 1)
         e_quant(1, 0)
-        x_quant(6, 2)
-        h_quant(0, 0, 2)
-        h_quant(0, 1, 2)
-        x_reorder(4, "V")
-        for m in range(4, 6):
-            for G in range(2):
-                mm1_wide(4, m % 2, G)
-                if 2 * m + G < 9:
-                    e_mm(1, 2 * m + G - 1)
-                    e_out(1, 2 * m + G - 1, "VS"[G])
-                if (m, G) == (4, 1):
-                    x_reorder(5, "V")
+        x_quant(3)
+        h_quant(0, 0, 4)
+        e_mm(15)
+        e_out(15, "V")
         e_quant(0, 1)
+        e_quant(1, 1)
+        h_quant(1, 0, 4)
 
         todo = [(m, 0) for m in range(2)] + [(m, 512) for m in range(2)] + [(m, n0) for m in range(2, 15) for n0 in (0, 512)]
-        WIDE = (6, 8, 10)
-        for m in range(6, 16):
-            for G in range(2):
-                if m in (6, 10) and G == 1:
-                    for mm in range(m + 2, m + 6):
-                        x_transpose(mm)
-                        x_out(mm, "S")
-                if m - m % 2 in WIDE:
-                    mm1_wide(m - m % 2, m % 2, G)
-                    if G == 1 and m in (8, 9):
-                        h_zip(m - m % 2, m % 2, "S")
-                else:
-                    mm1(m, G)
-                    h_out(m, G)
-                if (m, G) == (6, 0):
-                    e_quant(1, 1)
-                if m >= 13 or (m, G) == (12, 1):
-                    h_quant(m - 1 + G, 1 - G, 1)
-                if (m, G) in ((6, 1), (7, 0), (10, 1), (11, 0)):
-                    x_quant(2 * m - 4 - 4 * (m // 10), 2)
-                if m == 8:
-                    x_reorder(6 + G, "S")
-                zipped = G == 0 and (m - 1) - (m - 1) % 2 in WIDE
-                if zipped and m - 1 not in (8, 9):
-                    h_zip((m - 1) - (m - 1) % 2, (m - 1) % 2, "V")
-                if zipped and m in (12,):
-                    h_quant(m - 2, 1, 2)
-                mm2(*todo.pop(0))
-                if zipped and m not in (12,):
-                    h_quant((m - 1) - (m - 1) % 2, (m - 1) % 2, 2)
-                if G == 0 and m < 14:
-                    mm2(*todo.pop(0))
-                if G == 0 and m == 6:
-                    h_quant(2, 0, 2)
-                    h_quant(2, 1, 2)
-                    h_zip(4, 0, "V")
-                    h_zip(4, 1, "V")
-                    h_quant(4, 0, 2)
-                    h_quant(4, 1, 2)
-        h_quant(15, 1, 1)
-        for m, n0 in todo:
-            mm2(m, n0)
+        waiting = []
+
+        def second():
+            mm2(*todo[0])
+            waiting.append(todo.pop(0))
+
+        def drain(keep_back):
+            while len(waiting) > keep_back or (waiting and waiting[0][0] % 8 == 0):
+                y_out(*waiting.pop(0))
+
+        for slot in range(8, 32):
+            m, G = slot // 2, slot % 2
+            q = slot // 4
+            if q in WIDE:
+                mm1_wide(q, m % 2, G)
+            else:
+                mm1(m, G)
+            if slot > 8:
+                second()
+            if slot >= 24 and G == 1:
+                second()
+            if q in WIDE:
+                h_out_wide(q, m % 2, G)
+            else:
+                h_out(m, G)
+            if slot % 2 == 1 and (slot - 0) // 4 in WIDE:
+                h_zip((slot - 0) // 4, (slot - 0) // 2 % 2, "S")
+            drain(1 if slot < 26 else 0)
+            for lead, step in ((7, x_split), (6, x_turn), (4, lambda p: x_join(p, "V" if p in (4,) else "S")), (3, x_quant)):
+                if (slot + lead) % 4 == 0 and PE_PAIRS <= (slot + lead) // 4 < 8:
+                    step((slot + lead) // 4)
+            if slot < 26:
+                if slot % 4 == 1 and slot >= 12:
+                    h_quant(q - 1, 0, 4)
+            elif slot % 2 == 0:
+                h_quant((m - 1) // 2, 2 * ((m - 1) % 2), 2)
+            if slot == 30:
+                h_quant(7, 2, 1)
+        h_quant(7, 3, 1)
+        while todo:
+            second()
+            drain(0)
         for n0, n in ((0, 512), (512, 256), (768, 256)):
             mm2(15, n0, n)
+            y_out(15, n0, n)

@@ -321,8 +321,8 @@ def tile_pointnet_set_encoder_s12_kernel(tc, x, w, u_words, u_scales, v_words, v
         load_x(2)
         load_w(1, 1)
         load_x(3)
-        load_x_quads(4, 2)
-        load_x_quads(6, 2)
+        for q in range(PE_PAIRS, 8):
+            load_x_quads(q, 1)
 
         for m in range(4):
             x_transpose(m)

@@ -16,8 +16,10 @@ MAX = mybir.AluOpType.max
 RELU = mybir.ActivationFunctionType.Relu
 COPY = mybir.ActivationFunctionType.Copy
 
-PE_PAIRS = 4
-WIDE = (6,)
+PE_PAIRS = 5
+WIDE = (2, 3, 6)
+H_BANKS = range(8)
+Y_BANKS = range(0, 8)
 
 
 def tile_pointnet_set_encoder_s12_kernel(tc, x, w, u_words, u_scales, v_words, v_scales, out):
@@ -31,8 +33,13 @@ def tile_pointnet_set_encoder_s12_kernel(tc, x, w, u_words, u_scales, v_words, v
             t = keep.tile(shape, dtype, name=tag, tag=tag, bufs=bufs, align_bytes=256)
             return t
 
-        def bank(shape):
-            t = psum.tile(shape, F32, name="bank", tag="bank", bufs=8)
+        by_age = list(range(8))
+
+        def bank(shape, among=range(8)):
+            i = [j for j in by_age if j in among][0]
+            by_age.remove(i)
+            by_age.append(i)
+            t = psum.tile(shape, F32, name="bank%d" % i, tag="bank%d" % i)
             return t
 
         quarters = [(i, j) for i in range(2) for j in range(2)]
@@ -142,13 +149,26 @@ def tile_pointnet_set_encoder_s12_kernel(tc, x, w, u_words, u_scales, v_words, v
             nc.vector.quantize_mx(out=e_c[G, nh][:].bitcast(FP8X4), scales=e_s[G, nh][:], in_=e_grp[G, nh][:])
 
         x_g = {}
+        x_r = {}
+
+        def x_sort(q, engine):
+            x_r[q] = sb([128, 1024], F32, "x_r", 2)
+            copy(
+                engine,
+                x_r[q][:].rearrange("p (a u w) -> p a u w", u=2, w=128),
+                x_sb[q][:].bitcast(F32).rearrange("p (a w u) -> p a u w", u=2, w=128),
+            )
 
         def x_transpose(m):
             xt = bank([128, 2, 2, 128])
             for g in range(2):
                 base = (m % 2) * 512 + g * 256
                 for u in range(2):
-                    nc.tensor.transpose(xt[:, g, u, :], x_sb[m // 2][:].bitcast(F32)[:, base + u : base + 256 : 2], ident[:])
+                    if m // 2 in x_r:
+                        words = x_r[m // 2][:, base + 128 * u : base + 128 * u + 128]
+                    else:
+                        words = x_sb[m // 2][:].bitcast(F32)[:, base + u : base + 256 : 2]
+                    nc.tensor.transpose(xt[:, g, u, :], words, ident[:])
             banks["x", m] = xt
 
         def x_out(m, engine):
@@ -166,13 +186,13 @@ def tile_pointnet_set_encoder_s12_kernel(tc, x, w, u_words, u_scales, v_words, v
                     banks["x", m][:, 1].rearrange("p u n -> p n u"),
                 )
                 return
-            copy(
-                engine,
-                x_g[q][:, 1024 * b : 1024 * b + 1024].bitcast(F32).rearrange("p (g n u) -> p g n u", g=2, u=2),
-                banks["x", m][:].rearrange("p g u n -> p g n u"),
-            )
+            words = x_g[q][:].bitcast(F32)
+            if q in WIDE:
+                dst = words.rearrange("p (g b n u) -> p b g n u", g=2, b=2, u=2)[:, b]
+            else:
+                dst = words.rearrange("p (b g n u) -> p b g n u", g=2, b=2, u=2)[:, b]
+            copy(engine, dst, banks["x", m][:].rearrange("p g u n -> p g n u"))
 
-        x_r = {}
         x_t = {}
 
         def x_split(q, engine="S"):
@@ -209,7 +229,7 @@ def tile_pointnet_set_encoder_s12_kernel(tc, x, w, u_words, u_scales, v_words, v
         h_t = {}
 
         def mm1(m, G):
-            h = bank([128, 4, 128])
+            h = bank([128, 4, 128], H_BANKS if m >= 4 else range(8))
             for t in range(4):
                 for g in range(2):
                     k = slice(256 * (m % 2) + 128 * g, 256 * (m % 2) + 128 * g + 128)
@@ -242,7 +262,7 @@ def tile_pointnet_set_encoder_s12_kernel(tc, x, w, u_words, u_scales, v_words, v
         h_half = {}
 
         def mm1_wide(q, G, tp):
-            h = bank([128, 2, 256])
+            h = bank([128, 2, 256], H_BANKS)
             for tt in range(2):
                 t = 2 * tp + tt
                 for g in range(2):
@@ -279,7 +299,7 @@ def tile_pointnet_set_encoder_s12_kernel(tc, x, w, u_words, u_scales, v_words, v
             )
 
         def mm2(m, n0, n=512):
-            y = bank([128, n])
+            y = bank([128, n], Y_BANKS)
             nh, j0 = n0 // 512, n0 % 512
             for G in range(2):
                 k = slice(128 * part(m, G), 128 * part(m, G) + 128)
@@ -321,6 +341,7 @@ def tile_pointnet_set_encoder_s12_kernel(tc, x, w, u_words, u_scales, v_words, v
         load_x(2)
         load_w(1, 1)
         load_x(3)
+        load_x(4)
         for q in range(PE_PAIRS, 8):
             load_x_quads(q, 1)
 
@@ -367,6 +388,7 @@ def tile_pointnet_set_encoder_s12_kernel(tc, x, w, u_words, u_scales, v_words, v
         e_mm(15)
         e_out(15, "V")
         e_quant(0, 1)
+        x_sort(4, "V")
         e_quant(1, 1)
         h_quant(1, 0, 4)
 
@@ -381,9 +403,14 @@ def tile_pointnet_set_encoder_s12_kernel(tc, x, w, u_words, u_scales, v_words, v
             while len(waiting) > keep_back or (waiting and waiting[0][0] % 8 == 0):
                 y_out(*waiting.pop(0))
 
+        def due(slot, lead):
+            return (slot + lead) % 4 == 0 and PE_PAIRS <= (slot + lead) // 4 < 8
+
         for slot in range(8, 32):
-            m, G = slot // 2, slot % 2
-            q = slot // 4
+            q, m, G = slot // 4, slot // 2, slot % 2
+            if slot == 12:
+                x_transpose(8)
+                x_transpose(9)
             if q in WIDE:
                 mm1_wide(q, m % 2, G)
             else:
@@ -392,20 +419,30 @@ def tile_pointnet_set_encoder_s12_kernel(tc, x, w, u_words, u_scales, v_words, v
                 second()
             if slot >= 24 and G == 1:
                 second()
+            if slot == 12:
+                x_out(8, "S")
+                x_out(9, "S")
             if q in WIDE:
                 h_out_wide(q, m % 2, G)
             else:
                 h_out(m, G)
-            if slot % 2 == 1 and (slot - 0) // 4 in WIDE:
-                h_zip((slot - 0) // 4, (slot - 0) // 2 % 2, "S")
+            if due(slot, 9):
+                x_split((slot + 9) // 4)
+            if due(slot, 5):
+                x_join((slot + 5) // 4)
             drain(1 if slot < 26 else 0)
-            for lead, step in ((7, x_split), (6, x_turn), (4, lambda p: x_join(p, "V" if p in (4,) else "S")), (3, x_quant)):
-                if (slot + lead) % 4 == 0 and PE_PAIRS <= (slot + lead) // 4 < 8:
-                    step((slot + lead) // 4)
+            if G == 0 and (slot - 1) // 4 in WIDE:
+                h_zip((slot - 1) // 4, (slot - 1) // 2 % 2, "V" if slot < 25 else "S")
+            if slot == 13:
+                x_quant(4)
+            if due(slot, 8):
+                x_turn((slot + 8) // 4)
+            if due(slot, 4):
+                x_quant((slot + 4) // 4)
             if slot < 26:
                 if slot % 4 == 1 and slot >= 12:
                     h_quant(q - 1, 0, 4)
-            elif slot % 2 == 0:
+            elif G == 0:
                 h_quant((m - 1) // 2, 2 * ((m - 1) % 2), 2)
             if slot == 30:
                 h_quant(7, 2, 1)

@@ -1,7 +1,6 @@
 from contextlib import ExitStack
 
 import concourse.mybir as mybir
-from concourse.masks import make_identity
 
 FLOPS = 2 * 2048 * 1024 * 1024 * 2 + 2 * 512 * 1024 * 1024
 
@@ -18,8 +17,6 @@ COPY = mybir.ActivationFunctionType.Copy
 
 PE_PAIRS = 5
 WIDE = (2, 3, 6)
-H_BANKS = range(8)
-Y_BANKS = range(0, 8)
 
 
 def tile_pointnet_set_encoder_s12_kernel(tc, x, w, u_words, u_scales, v_words, v_scales, out):
@@ -33,14 +30,11 @@ def tile_pointnet_set_encoder_s12_kernel(tc, x, w, u_words, u_scales, v_words, v
             t = keep.tile(shape, dtype, name=tag, tag=tag, bufs=bufs, align_bytes=256)
             return t
 
-        by_age = list(range(8))
+        banks = {}
 
-        def bank(shape, among=range(8)):
-            i = [j for j in by_age if j in among][0]
-            by_age.remove(i)
-            by_age.append(i)
-            t = psum.tile(shape, F32, name="bank%d" % i, tag="bank%d" % i)
-            return t
+        def bank(key, shape):
+            banks[key] = psum.tile(shape, F32, name="bank", tag="bank", bufs=8)
+            return banks[key]
 
         quarters = [(i, j) for i in range(2) for j in range(2)]
 
@@ -98,6 +92,8 @@ def tile_pointnet_set_encoder_s12_kernel(tc, x, w, u_words, u_scales, v_words, v
         def copy(engine, out, in_):
             if engine == "S":
                 nc.scalar.copy(out, in_)
+            elif engine == "A":
+                nc.scalar.activation(out=out, in_=in_, func=COPY)
             else:
                 nc.vector.tensor_copy(out=out, in_=in_)
 
@@ -107,10 +103,10 @@ def tile_pointnet_set_encoder_s12_kernel(tc, x, w, u_words, u_scales, v_words, v
                 in_=u_raw[:].bitcast(I32).rearrange("p (G q t r) -> p G t q r", G=2, q=32, t=4, r=2),
             )
 
-        def permute_u_scales():
+        def permute_u_scales(rows=slice(0, 128)):
             nc.vector.tensor_copy(
-                out=u_pl[:].bitcast(I32).rearrange("p (G t q) -> p G t q", G=2, t=4, q=32),
-                in_=u_pl_raw[:].bitcast(I32).rearrange("p (G q t) -> p G t q", G=2, q=32, t=4),
+                out=u_pl[rows, :].bitcast(I32).rearrange("p (G t q) -> p G t q", G=2, t=4, q=32),
+                in_=u_pl_raw[rows, :].bitcast(I32).rearrange("p (G q t) -> p G t q", G=2, q=32, t=4),
             )
 
         def w_weave(g, G):
@@ -122,11 +118,10 @@ def tile_pointnet_set_encoder_s12_kernel(tc, x, w, u_words, u_scales, v_words, v
         def w_quant(g, G):
             nc.vector.quantize_mx(out=w_c[g, G][:].bitcast(FP8X4), scales=w_s[g, G][:], in_=w_grp[g, G][:])
 
-        banks = {}
 
         def e_mm(k):
             G, nb = k // 4 % 2, k % 4 + k // 8 * 4
-            e = bank([128, 4, 128])
+            e = bank(("e", k), [128, 4, 128])
             for t in range(4):
                 c0 = G * 512 + t * 128
                 nc.tensor.matmul_mx(
@@ -135,7 +130,6 @@ def tile_pointnet_set_encoder_s12_kernel(tc, x, w, u_words, u_scales, v_words, v
                     rhs=v_w[:, 256 * nb : 256 * nb + 256].bitcast(FP4X4), rhs_scale=v_pl[:, 128 * nb : 128 * nb + 128],
                     start=t == 0, stop=t == 3,
                 )
-            banks["e", k] = e
 
         def e_out(k, engine):
             j = k % 4
@@ -160,7 +154,7 @@ def tile_pointnet_set_encoder_s12_kernel(tc, x, w, u_words, u_scales, v_words, v
             )
 
         def x_transpose(m):
-            xt = bank([128, 2, 2, 128])
+            xt = bank(("x", m), [128, 2, 2, 128])
             for g in range(2):
                 base = (m % 2) * 512 + g * 256
                 for u in range(2):
@@ -169,7 +163,6 @@ def tile_pointnet_set_encoder_s12_kernel(tc, x, w, u_words, u_scales, v_words, v
                     else:
                         words = x_sb[m // 2][:].bitcast(F32)[:, base + u : base + 256 : 2]
                     nc.tensor.transpose(xt[:, g, u, :], words, ident[:])
-            banks["x", m] = xt
 
         def x_out(m, engine):
             q, b = m // 2, m % 2
@@ -223,13 +216,17 @@ def tile_pointnet_set_encoder_s12_kernel(tc, x, w, u_words, u_scales, v_words, v
                     x_t[q][:].rearrange("p (a u i) -> p a i u", u=2, i=32),
                 )
 
-        def x_quant(q):
-            nc.vector.quantize_mx(out=x_c[q][:].bitcast(FP8X4), scales=x_s[q][:], in_=x_g[q][:])
+        def x_quant(q, b0=0, n=2):
+            nc.vector.quantize_mx(
+                out=x_c[q][:, 256 * b0 : 256 * (b0 + n)].bitcast(FP8X4),
+                scales=x_s[q][:, 256 * b0 : 256 * (b0 + n)],
+                in_=x_g[q][:, 1024 * b0 : 1024 * (b0 + n)],
+            )
 
         h_t = {}
 
         def mm1(m, G):
-            h = bank([128, 4, 128], H_BANKS if m >= 4 else range(8))
+            h = bank(("h", m, G), [128, 4, 128])
             for t in range(4):
                 for g in range(2):
                     k = slice(256 * (m % 2) + 128 * g, 256 * (m % 2) + 128 * g + 128)
@@ -240,7 +237,6 @@ def tile_pointnet_set_encoder_s12_kernel(tc, x, w, u_words, u_scales, v_words, v
                         rhs=x_c[m // 2][:, k].bitcast(FP8X4), rhs_scale=x_s[m // 2][:, k],
                         start=g == 0, stop=g == 1,
                     )
-            banks["h", m, G] = h
 
         def part(m, G):
             return 2 * G + m % 2 if m // 2 in WIDE else 2 * (m % 2) + G
@@ -262,7 +258,7 @@ def tile_pointnet_set_encoder_s12_kernel(tc, x, w, u_words, u_scales, v_words, v
         h_half = {}
 
         def mm1_wide(q, G, tp):
-            h = bank([128, 2, 256], H_BANKS)
+            h = bank(("h", q, G, tp), [128, 2, 256])
             for tt in range(2):
                 t = 2 * tp + tt
                 for g in range(2):
@@ -274,7 +270,6 @@ def tile_pointnet_set_encoder_s12_kernel(tc, x, w, u_words, u_scales, v_words, v
                         rhs=x_c[q][:, k].bitcast(FP8X4), rhs_scale=x_s[q][:, k],
                         start=g == 0, stop=g == 1,
                     )
-            banks["h", q, G, tp] = h
 
         def h_out_wide(q, G, tp):
             if tp == 0:
@@ -298,10 +293,10 @@ def tile_pointnet_set_encoder_s12_kernel(tc, x, w, u_words, u_scales, v_words, v
                 in_=h_t[q][:, 512 * j0 : 512 * (j0 + n)],
             )
 
-        def mm2(m, n0, n=512):
-            y = bank([128, n], Y_BANKS)
+        def mm2(m, n0, n=512, passes=(0, 1)):
+            y = bank(("y", m, n0), [128, n]) if 0 in passes else banks["y", m, n0]
             nh, j0 = n0 // 512, n0 % 512
-            for G in range(2):
+            for G in passes:
                 k = slice(128 * part(m, G), 128 * part(m, G) + 128)
                 nc.tensor.matmul_mx(
                     out=y[:],
@@ -309,7 +304,6 @@ def tile_pointnet_set_encoder_s12_kernel(tc, x, w, u_words, u_scales, v_words, v
                     rhs=e_c[G, nh][:, j0 : j0 + n].bitcast(FP8X4), rhs_scale=e_s[G, nh][:, j0 : j0 + n],
                     start=G == 0, stop=G == 1,
                 )
-            banks["y", m, n0] = y
 
         def y_out(m, n0, n=512):
             y = banks["y", m, n0]
@@ -322,17 +316,25 @@ def tile_pointnet_set_encoder_s12_kernel(tc, x, w, u_words, u_scales, v_words, v
             if m % 8 == 7:
                 nc.sync.dma_start(out=out[128 * s : 128 * s + 128, n0 : n0 + n], in_=a)
 
+        load_scales(nc.gpsimd, u_pl_raw, us32, 0)
         nc.vector.memset(v_pl[:].bitcast(I32), 0)
-        nc.vector.memset(u_pl_raw[:].bitcast(I32), 0)
+        nc.vector.memset(u_pl[:].bitcast(I32), 0)
+        ones = sb([128, 32], F32, "ones")
+        column = sb([128, 32], F32, "column")
+        lane = sb([128, 32], F32, "lane")
+        nc.vector.memset(ones[:], 1.0)
+        nc.vector.tensor_tensor_scan(out=column[:], data0=ones[:], data1=ones[:], initial=0.0, op0=mybir.AluOpType.mult, op1=mybir.AluOpType.add)
         nc.vector.memset(ident[:], 0.0)
+        nc.vector.transpose(lane[:], column[:])
+        for Q in range(4):
+            rows = slice(32 * Q, 32 * Q + 32)
+            nc.vector.tensor_tensor(out=ident[rows, rows], in0=column[rows, :], in1=lane[rows, :], op=mybir.AluOpType.is_equal)
         load_x(0)
         nc.sync.dma_start(out=u_raw[:].bitcast(I32), in_=u_words[0].bitcast(I32))
         load_x(1)
-        for Q in range(3):
-            load_scales(nc.gpsimd, v_pl, vs32, Q)
-        make_identity(nc, ident[:], nomemset=True)
-        load_scales(nc.scalar, v_pl, vs32, 3)
         for Q in range(4):
+            load_scales(nc.gpsimd if Q < 2 else nc.scalar, v_pl, vs32, Q)
+        for Q in range(1, 4):
             load_scales(nc.scalar, u_pl_raw, us32, Q)
         nc.sync.dma_start(out=v_w[:].bitcast(I32), in_=v_words[0].bitcast(I32))
         load_w(0, 0)
@@ -342,28 +344,29 @@ def tile_pointnet_set_encoder_s12_kernel(tc, x, w, u_words, u_scales, v_words, v
         load_w(1, 1)
         load_x(3)
         load_x(4)
-        for q in range(PE_PAIRS, 8):
-            load_x_quads(q, 1)
+        load_x_quads(5, 1)
+        load_x_quads(6, 2)
 
         for m in range(4):
             x_transpose(m)
         x_out(0, "A")
-        permute_u_scales()
         permute_u()
-        x_out(1, "V")
+        for Q in range(4):
+            permute_u_scales(slice(32 * Q, 32 * Q + 4))
+        x_out(1, "S")
         x_out(2, "S")
         x_quant(0)
         x_out(3, "S")
+        x_quant(1)
         for k in range(15):
             e_mm(k)
-            e_out(k, "V" if k == 0 else "S")
+            e_out(k, "S")
             if k == 0:
                 w_weave(0, 0)
                 w_weave(1, 0)
                 w_quant(0, 0)
                 w_quant(1, 0)
                 w_weave(0, 1)
-                x_quant(1)
                 w_quant(0, 1)
                 w_weave(1, 1)
         for q in range(2):
@@ -392,6 +395,7 @@ def tile_pointnet_set_encoder_s12_kernel(tc, x, w, u_words, u_scales, v_words, v
         e_quant(1, 1)
         h_quant(1, 0, 4)
 
+
         todo = [(m, 0) for m in range(2)] + [(m, 512) for m in range(2)] + [(m, n0) for m in range(2, 15) for n0 in (0, 512)]
         waiting = []
 
@@ -408,37 +412,40 @@ def tile_pointnet_set_encoder_s12_kernel(tc, x, w, u_words, u_scales, v_words, v
 
         for slot in range(8, 32):
             q, m, G = slot // 4, slot // 2, slot % 2
-            if slot == 12:
-                x_transpose(8)
-                x_transpose(9)
+            turn = slot % 4 == 0 and 4 <= q + 1 < PE_PAIRS
+            if turn:
+                x_transpose(2 * q + 2)
+                x_transpose(2 * q + 3)
             if q in WIDE:
                 mm1_wide(q, m % 2, G)
             else:
                 mm1(m, G)
-            if slot > 8:
+            if slot > 9:
                 second()
-            if slot >= 24 and G == 1:
+            if slot >= 22 and G == 1:
                 second()
-            if slot == 12:
-                x_out(8, "S")
-                x_out(9, "S")
+            if turn:
+                x_out(2 * q + 2, "S")
+                x_out(2 * q + 3, "V")
             if q in WIDE:
                 h_out_wide(q, m % 2, G)
             else:
                 h_out(m, G)
-            if due(slot, 9):
-                x_split((slot + 9) // 4)
-            if due(slot, 5):
-                x_join((slot + 5) // 4)
+            if due(slot, 7):
+                x_split((slot + 7) // 4)
+            if due(slot, 4):
+                x_join((slot + 4) // 4)
             drain(1 if slot < 26 else 0)
             if G == 0 and (slot - 1) // 4 in WIDE:
-                h_zip((slot - 1) // 4, (slot - 1) // 2 % 2, "V" if slot < 25 else "S")
-            if slot == 13:
-                x_quant(4)
-            if due(slot, 8):
-                x_turn((slot + 8) // 4)
-            if due(slot, 4):
-                x_quant((slot + 4) // 4)
+                h_zip((slot - 1) // 4, (slot - 1) // 2 % 2, "V" if slot < 27 else "S")
+            if slot % 4 == 1 and 4 <= q + 1 < PE_PAIRS:
+                x_quant(q + 1)
+            if slot % 4 == 2 and 5 <= q + 2 < PE_PAIRS:
+                x_sort(q + 2, "S")
+            if due(slot, 6):
+                x_turn((slot + 6) // 4)
+            if due(slot, 3):
+                x_quant((slot + 3) // 4)
             if slot < 26:
                 if slot % 4 == 1 and slot >= 12:
                     h_quant(q - 1, 0, 4)
@@ -450,6 +457,6 @@ def tile_pointnet_set_encoder_s12_kernel(tc, x, w, u_words, u_scales, v_words, v
         while todo:
             second()
             drain(0)
-        for n0, n in ((0, 512), (512, 256), (768, 256)):
+        for n0, n in ((0, 256), (256, 256), (512, 256), (768, 256)):
             mm2(15, n0, n)
             y_out(15, n0, n)

@@ -1,6 +1,7 @@
 from contextlib import ExitStack
 
 import concourse.mybir as mybir
+from concourse.masks import make_identity
 
 FLOPS = 2 * 2048 * 1024 * 1024 * 2 + 2 * 512 * 1024 * 1024
 
@@ -316,25 +317,17 @@ def tile_pointnet_set_encoder_s12_kernel(tc, x, w, u_words, u_scales, v_words, v
             if m % 8 == 7:
                 nc.sync.dma_start(out=out[128 * s : 128 * s + 128, n0 : n0 + n], in_=a)
 
-        load_scales(nc.gpsimd, u_pl_raw, us32, 0)
         nc.vector.memset(v_pl[:].bitcast(I32), 0)
-        nc.vector.memset(u_pl[:].bitcast(I32), 0)
-        ones = sb([128, 32], F32, "ones")
-        column = sb([128, 32], F32, "column")
-        lane = sb([128, 32], F32, "lane")
-        nc.vector.memset(ones[:], 1.0)
-        nc.vector.tensor_tensor_scan(out=column[:], data0=ones[:], data1=ones[:], initial=0.0, op0=mybir.AluOpType.mult, op1=mybir.AluOpType.add)
+        nc.vector.memset(u_pl_raw[:].bitcast(I32), 0)
         nc.vector.memset(ident[:], 0.0)
-        nc.vector.transpose(lane[:], column[:])
-        for Q in range(4):
-            rows = slice(32 * Q, 32 * Q + 32)
-            nc.vector.tensor_tensor(out=ident[rows, rows], in0=column[rows, :], in1=lane[rows, :], op=mybir.AluOpType.is_equal)
         load_x(0)
         nc.sync.dma_start(out=u_raw[:].bitcast(I32), in_=u_words[0].bitcast(I32))
         load_x(1)
+        for Q in range(3):
+            load_scales(nc.gpsimd, v_pl, vs32, Q)
+        make_identity(nc, ident[:], nomemset=True)
+        load_scales(nc.scalar, v_pl, vs32, 3)
         for Q in range(4):
-            load_scales(nc.gpsimd if Q < 2 else nc.scalar, v_pl, vs32, Q)
-        for Q in range(1, 4):
             load_scales(nc.scalar, u_pl_raw, us32, Q)
         nc.sync.dma_start(out=v_w[:].bitcast(I32), in_=v_words[0].bitcast(I32))
         load_w(0, 0)
@@ -350,9 +343,8 @@ def tile_pointnet_set_encoder_s12_kernel(tc, x, w, u_words, u_scales, v_words, v
         for m in range(4):
             x_transpose(m)
         x_out(0, "A")
+        permute_u_scales()
         permute_u()
-        for Q in range(4):
-            permute_u_scales(slice(32 * Q, 32 * Q + 4))
         x_out(1, "S")
         x_out(2, "S")
         x_quant(0)

@@ -17,7 +17,7 @@ RELU = mybir.ActivationFunctionType.Relu
 COPY = mybir.ActivationFunctionType.Copy
 
 PE_PAIRS = 5
-WIDE = (2, 3, 6)
+WIDE = (2, 3, 4, 6)
 
 
 def tile_pointnet_set_encoder_s12_kernel(tc, x, w, u_words, u_scales, v_words, v_scales, out):
@@ -345,20 +345,20 @@ def tile_pointnet_set_encoder_s12_kernel(tc, x, w, u_words, u_scales, v_words, v
         x_out(0, "A")
         permute_u_scales()
         permute_u()
-        x_out(1, "S")
+        x_out(1, "V")
         x_out(2, "S")
         x_quant(0)
         x_out(3, "S")
-        x_quant(1)
         for k in range(15):
             e_mm(k)
-            e_out(k, "S")
+            e_out(k, "V" if k == 0 else "S")
             if k == 0:
                 w_weave(0, 0)
                 w_weave(1, 0)
                 w_quant(0, 0)
                 w_quant(1, 0)
                 w_weave(0, 1)
+                x_quant(1)
                 w_quant(0, 1)
                 w_weave(1, 1)
         for q in range(2):
@@ -372,7 +372,7 @@ def tile_pointnet_set_encoder_s12_kernel(tc, x, w, u_words, u_scales, v_words, v
         x_out(5, "V")
         x_out(6, "V")
         x_quant(2)
-        x_out(7, "V")
+        x_out(7, "S")
         e_quant(0, 0)
         for m in range(4):
             mm1(m, 1)
@@ -381,7 +381,7 @@ def tile_pointnet_set_encoder_s12_kernel(tc, x, w, u_words, u_scales, v_words, v
         x_quant(3)
         h_quant(0, 0, 4)
         e_mm(15)
-        e_out(15, "V")
+        e_out(15, "S")
         e_quant(0, 1)
         x_sort(4, "V")
         e_quant(1, 1)
@@ -414,17 +414,17 @@ def tile_pointnet_set_encoder_s12_kernel(tc, x, w, u_words, u_scales, v_words, v
                 mm1(m, G)
             if slot > 9:
                 second()
-            if slot >= 22 and G == 1:
+            if slot >= 24 and G == 1:
                 second()
             if turn:
                 x_out(2 * q + 2, "S")
-                x_out(2 * q + 3, "V")
+                x_out(2 * q + 3, "S")
             if q in WIDE:
                 h_out_wide(q, m % 2, G)
             else:
                 h_out(m, G)
             if due(slot, 7):
-                x_split((slot + 7) // 4)
+                x_split((slot + 7) // 4, "V" if (slot + 7) // 4 in (5,) else "S")
             if due(slot, 4):
                 x_join((slot + 4) // 4)
             drain(1 if slot < 26 else 0)

@@ -17,7 +17,7 @@ RELU = mybir.ActivationFunctionType.Relu
 COPY = mybir.ActivationFunctionType.Copy
 
 PE_PAIRS = 5
-WIDE = (2, 3, 4, 6)
+WIDE = (1, 2, 3, 4, 5, 6)
 
 
 def tile_pointnet_set_encoder_s12_kernel(tc, x, w, u_words, u_scales, v_words, v_scales, out):
@@ -116,8 +116,12 @@ def tile_pointnet_set_encoder_s12_kernel(tc, x, w, u_words, u_scales, v_words, v
                 in_=w_raw[g, G][:].rearrange("p j (q t r) -> p t q j r", q=32, t=4, r=4),
             )
 
-        def w_quant(g, G):
-            nc.vector.quantize_mx(out=w_c[g, G][:].bitcast(FP8X4), scales=w_s[g, G][:], in_=w_grp[g, G][:])
+        def w_quant(g, G, t0=0, n=4):
+            nc.vector.quantize_mx(
+                out=w_c[g, G][:, 128 * t0 : 128 * (t0 + n)].bitcast(FP8X4),
+                scales=w_s[g, G][:, 128 * t0 : 128 * (t0 + n)],
+                in_=w_grp[g, G][:, 512 * t0 : 512 * (t0 + n)],
+            )
 
 
         def e_mm(k):
@@ -170,13 +174,14 @@ def tile_pointnet_set_encoder_s12_kernel(tc, x, w, u_words, u_scales, v_words, v
             if b == 0:
                 x_g[q] = sb([128, 2048], BF16, "x_g", 3)
             if engine == "A":
+                second_half = 1024 if q in WIDE else 512
                 nc.scalar.activation(
-                    out=x_g[q][:, 1024 * b : 1024 * b + 512].rearrange("p (n u e) -> p n u e", u=2, e=2),
+                    out=x_g[q][:, 0:512].rearrange("p (n u e) -> p n u e", u=2, e=2),
                     in_=banks["x", m][:, 0].bitcast(BF16).rearrange("p u (n e) -> p n u e", e=2),
                     func=COPY,
                 )
                 nc.scalar.copy(
-                    x_g[q][:, 1024 * b + 512 : 1024 * b + 1024].bitcast(F32).rearrange("p (n u) -> p n u", u=2),
+                    x_g[q][:, second_half : second_half + 512].bitcast(F32).rearrange("p (n u) -> p n u", u=2),
                     banks["x", m][:, 1].rearrange("p u n -> p n u"),
                 )
                 return
@@ -230,7 +235,8 @@ def tile_pointnet_set_encoder_s12_kernel(tc, x, w, u_words, u_scales, v_words, v
             h = bank(("h", m, G), [128, 4, 128])
             for t in range(4):
                 for g in range(2):
-                    k = slice(256 * (m % 2) + 128 * g, 256 * (m % 2) + 128 * g + 128)
+                    k0 = 256 * g + 128 * (m % 2) if m // 2 in WIDE else 256 * (m % 2) + 128 * g
+                    k = slice(k0, k0 + 128)
                     nc.tensor.matmul_mx(
                         out=h[:, t, :],
                         lhsT=w_c[g, G][:, 128 * t : 128 * t + 128].bitcast(FP8X4),
@@ -244,7 +250,7 @@ def tile_pointnet_set_encoder_s12_kernel(tc, x, w, u_words, u_scales, v_words, v
 
         def h_tile(q):
             if q not in h_t:
-                h_t[q] = sb([128, 2048], BF16, "h_t", 3)
+                h_t[q] = sb([128, 2048], BF16, "h_t", 4)
             return h_t[q]
 
         def h_out(m, G, engine="S"):
@@ -274,7 +280,7 @@ def tile_pointnet_set_encoder_s12_kernel(tc, x, w, u_words, u_scales, v_words, v
 
         def h_out_wide(q, G, tp):
             if tp == 0:
-                h_half[q, G] = sb([128, 2, 512], BF16, "h_half", 2)
+                h_half[q, G] = sb([128, 2, 512], BF16, "h_half", 3)
             nc.scalar.activation(
                 out=h_half[q, G][:, tp, :].rearrange("p (n e) -> p n e", e=2),
                 in_=banks["h", q, G, tp][:].rearrange("p e n -> p n e"), func=RELU,
@@ -367,6 +373,8 @@ def tile_pointnet_set_encoder_s12_kernel(tc, x, w, u_words, u_scales, v_words, v
                 h_out(m, 0)
             for m in (2 * q + 4, 2 * q + 5):
                 x_transpose(m)
+        e_mm(15)
+        e_out(15, "S")
         x_out(4, "V")
         w_quant(1, 1)
         x_out(5, "V")
@@ -374,16 +382,18 @@ def tile_pointnet_set_encoder_s12_kernel(tc, x, w, u_words, u_scales, v_words, v
         x_quant(2)
         x_out(7, "S")
         e_quant(0, 0)
-        for m in range(4):
+        for m in range(2):
             mm1(m, 1)
             h_out(m, 1)
+        for tp in range(2):
+            mm1_wide(1, 1, tp)
+            h_out_wide(1, 1, tp)
         e_quant(1, 0)
         x_quant(3)
         h_quant(0, 0, 4)
-        e_mm(15)
-        e_out(15, "S")
         e_quant(0, 1)
         x_sort(4, "V")
+        h_zip(1, 1, "V")
         e_quant(1, 1)
         h_quant(1, 0, 4)
 
@@ -428,8 +438,8 @@ def tile_pointnet_set_encoder_s12_kernel(tc, x, w, u_words, u_scales, v_words, v
             if due(slot, 4):
                 x_join((slot + 4) // 4)
             drain(1 if slot < 26 else 0)
-            if G == 0 and (slot - 1) // 4 in WIDE:
-                h_zip((slot - 1) // 4, (slot - 1) // 2 % 2, "V" if slot < 27 else "S")
+            if G == 0 and slot > 8 and (slot - 1) // 4 in WIDE:
+                h_zip((slot - 1) // 4, (slot - 1) // 2 % 2, "S" if slot >= 24 else "V")
             if slot % 4 == 1 and 4 <= q + 1 < PE_PAIRS:
                 x_quant(q + 1)
             if slot % 4 == 2 and 5 <= q + 2 < PE_PAIRS:
@@ -438,12 +448,10 @@ def tile_pointnet_set_encoder_s12_kernel(tc, x, w, u_words, u_scales, v_words, v
                 x_turn((slot + 6) // 4)
             if due(slot, 3):
                 x_quant((slot + 3) // 4)
-            if slot < 26:
-                if slot % 4 == 1 and slot >= 12:
-                    h_quant(q - 1, 0, 4)
-            elif G == 0:
-                h_quant((m - 1) // 2, 2 * ((m - 1) % 2), 2)
+            if slot % 4 == 1 and slot >= 12:
+                h_quant(q - 1, 0, 4)
             if slot == 30:
+                h_quant(7, 0, 2)
                 h_quant(7, 2, 1)
         h_quant(7, 3, 1)
         while todo:

@@ -16,8 +16,12 @@ MAX = mybir.AluOpType.max
 RELU = mybir.ActivationFunctionType.Relu
 COPY = mybir.ActivationFunctionType.Copy
 
-PE_PAIRS = 5
-WIDE = (1, 2, 3, 4, 5, 6)
+NARROW = ((0, 0), (0, 1), (1, 0), (7, 0), (7, 1))
+FIRST_SECOND = 2
+LATE = 16
+HOLD_UNTIL = 18
+ZIP_ON_SCALAR = 4
+PICK_LEAD = 5
 
 
 def tile_pointnet_set_encoder_s12_kernel(tc, x, w, u_words, u_scales, v_words, v_scales, out):
@@ -46,7 +50,7 @@ def tile_pointnet_set_encoder_s12_kernel(tc, x, w, u_words, u_scales, v_words, v
         v_w = sb([128, 2048], U8, "v_w")
         v_pl = sb([128, 1024], U8, "v_pl")
         ident = sb([128, 128], F32, "ident")
-        x_sb = [sb([128, 2048], BF16, "x_sb%d" % q) for q in range(PE_PAIRS)]
+        x_sb = [sb([128, 2048], BF16, "x_sb%d" % q) for q in range(4)]
         x_c = [sb([128, 512], U32, "x_c%d" % q) for q in range(8)]
         x_s = [sb([128, 512], U8, "x_s%d" % q) for q in range(8)]
         w_raw = {k: sb([128, 4, 512], BF16, "w_raw%d%d" % k) for k in quarters}
@@ -63,26 +67,23 @@ def tile_pointnet_set_encoder_s12_kernel(tc, x, w, u_words, u_scales, v_words, v
         us32 = u_scales[0].bitcast(I32)
         vs32 = v_scales[0].bitcast(I32)
         x_rows = x.rearrange("(s i b) k -> s i b k", s=2, i=128, b=8)
-        x_quads = x.rearrange("(s c i b) (g Q k) -> s c Q i b g k", s=2, c=4, i=32, b=8, g=2, Q=4)
         w_rows = w.rearrange("(g p j) f -> g p j f", g=2, p=128, j=4)
 
         def load_x(q):
-            s, b = q // 4, 2 * (q % 4)
-            nc.sync.dma_start(out=x_sb[q][:].rearrange("p (b k) -> p b k", b=2), in_=x_rows[s][:, b : b + 2, :])
+            nc.sync.dma_start(out=x_sb[q][:].rearrange("p (b k) -> p b k", b=2), in_=x_rows[0][:, 2 * q : 2 * q + 2, :])
 
-        x_q = {}
+        x_d = {}
 
-        def load_x_quads(q0, n):
-            s, b = q0 // 4, 2 * (q0 % 4)
-            t = sb([128, 2048 * n], BF16, "x_q%d" % q0)
-            for c in range(4):
+        def load_x_twice(q0, n, s, r):
+            rows = x.rearrange("(s i m r) k -> s r i m k", s=2, i=16, r=4 // n)[s, r]
+            t = sb([128, 2, 16 * n, 128], BF16, "x_d%d" % q0)
+            for g in range(2):
                 for Q in (0, 2, 1, 3):
-                    nc.sync.dma_start(
-                        out=t[32 * Q : 32 * Q + 32, :].rearrange("p (a c k) -> p a c k", c=4, k=128)[:, :, c, :],
-                        in_=x_quads[s, c, Q][:, b : b + 2 * n].rearrange("i b g k -> i (b g) k"),
-                    )
+                    for u in range(2):
+                        k0 = 512 * g + 128 * Q + 2 * u
+                        nc.sync.dma_start(out=t[32 * Q + u : 32 * Q + 32 : 2, g, :, 0:126], in_=rows[:, :, k0 : k0 + 126])
             for j in range(n):
-                x_q[q0 + j] = t[:, 2048 * j : 2048 * j + 2048]
+                x_d[q0 + j] = t[:].bitcast(F32).rearrange("p g (c a b) (j u) -> p a g c b j u", c=8, b=2, u=2)[:, j, :, :, :, :, 0]
 
         def load_w(g, G):
             nc.sync.dma_start(out=w_raw[g, G][:], in_=w_rows[g][:, :, 512 * G : 512 * G + 512])
@@ -93,8 +94,6 @@ def tile_pointnet_set_encoder_s12_kernel(tc, x, w, u_words, u_scales, v_words, v
         def copy(engine, out, in_):
             if engine == "S":
                 nc.scalar.copy(out, in_)
-            elif engine == "A":
-                nc.scalar.activation(out=out, in_=in_, func=COPY)
             else:
                 nc.vector.tensor_copy(out=out, in_=in_)
 
@@ -104,10 +103,10 @@ def tile_pointnet_set_encoder_s12_kernel(tc, x, w, u_words, u_scales, v_words, v
                 in_=u_raw[:].bitcast(I32).rearrange("p (G q t r) -> p G t q r", G=2, q=32, t=4, r=2),
             )
 
-        def permute_u_scales(rows=slice(0, 128)):
+        def permute_u_scales():
             nc.vector.tensor_copy(
-                out=u_pl[rows, :].bitcast(I32).rearrange("p (G t q) -> p G t q", G=2, t=4, q=32),
-                in_=u_pl_raw[rows, :].bitcast(I32).rearrange("p (G q t) -> p G t q", G=2, q=32, t=4),
+                out=u_pl[:].bitcast(I32).rearrange("p (G t q) -> p G t q", G=2, t=4, q=32),
+                in_=u_pl_raw[:].bitcast(I32).rearrange("p (G q t) -> p G t q", G=2, q=32, t=4),
             )
 
         def w_weave(g, G):
@@ -116,13 +115,8 @@ def tile_pointnet_set_encoder_s12_kernel(tc, x, w, u_words, u_scales, v_words, v
                 in_=w_raw[g, G][:].rearrange("p j (q t r) -> p t q j r", q=32, t=4, r=4),
             )
 
-        def w_quant(g, G, t0=0, n=4):
-            nc.vector.quantize_mx(
-                out=w_c[g, G][:, 128 * t0 : 128 * (t0 + n)].bitcast(FP8X4),
-                scales=w_s[g, G][:, 128 * t0 : 128 * (t0 + n)],
-                in_=w_grp[g, G][:, 512 * t0 : 512 * (t0 + n)],
-            )
-
+        def w_quant(g, G):
+            nc.vector.quantize_mx(out=w_c[g, G][:].bitcast(FP8X4), scales=w_s[g, G][:], in_=w_grp[g, G][:])
 
         def e_mm(k):
             G, nb = k // 4 % 2, k % 4 + k // 8 * 4
@@ -150,161 +144,112 @@ def tile_pointnet_set_encoder_s12_kernel(tc, x, w, u_words, u_scales, v_words, v
         x_g = {}
         x_r = {}
 
-        def x_sort(q, engine):
-            x_r[q] = sb([128, 1024], F32, "x_r", 2)
-            copy(
-                engine,
-                x_r[q][:].rearrange("p (a u w) -> p a u w", u=2, w=128),
-                x_sb[q][:].bitcast(F32).rearrange("p (a w u) -> p a u w", u=2, w=128),
-            )
-
-        def x_transpose(m):
-            xt = bank(("x", m), [128, 2, 2, 128])
+        def x_transpose(q, b):
+            xt = bank(("x", q, b), [128, 2, 2, 128])
             for g in range(2):
-                base = (m % 2) * 512 + g * 256
+                base = b * 512 + g * 256
                 for u in range(2):
-                    if m // 2 in x_r:
-                        words = x_r[m // 2][:, base + 128 * u : base + 128 * u + 128]
-                    else:
-                        words = x_sb[m // 2][:].bitcast(F32)[:, base + u : base + 256 : 2]
-                    nc.tensor.transpose(xt[:, g, u, :], words, ident[:])
+                    nc.tensor.transpose(xt[:, g, u, :], x_sb[q][:].bitcast(F32)[:, base + u : base + 256 : 2], ident[:])
 
-        def x_out(m, engine):
-            q, b = m // 2, m % 2
-            if b == 0:
+        def x_out(q, b, engine):
+            if q not in x_g:
                 x_g[q] = sb([128, 2048], BF16, "x_g", 3)
+            dst = x_g[q][:].bitcast(F32).rearrange("p (g b n u) -> p b g n u", g=2, b=2, u=2)[:, b]
             if engine == "A":
-                second_half = 1024 if q in WIDE else 512
                 nc.scalar.activation(
                     out=x_g[q][:, 0:512].rearrange("p (n u e) -> p n u e", u=2, e=2),
-                    in_=banks["x", m][:, 0].bitcast(BF16).rearrange("p u (n e) -> p n u e", e=2),
+                    in_=banks["x", q, b][:, 0].bitcast(BF16).rearrange("p u (n e) -> p n u e", e=2),
                     func=COPY,
                 )
-                nc.scalar.copy(
-                    x_g[q][:, second_half : second_half + 512].bitcast(F32).rearrange("p (n u) -> p n u", u=2),
-                    banks["x", m][:, 1].rearrange("p u n -> p n u"),
-                )
+                nc.scalar.copy(dst[:, 1], banks["x", q, b][:, 1].rearrange("p u n -> p n u"))
                 return
-            words = x_g[q][:].bitcast(F32)
-            if q in WIDE:
-                dst = words.rearrange("p (g b n u) -> p b g n u", g=2, b=2, u=2)[:, b]
-            else:
-                dst = words.rearrange("p (b g n u) -> p b g n u", g=2, b=2, u=2)[:, b]
-            copy(engine, dst, banks["x", m][:].rearrange("p g u n -> p g n u"))
+            copy(engine, dst, banks["x", q, b][:].rearrange("p g u n -> p g n u"))
 
-        x_t = {}
-
-        def x_split(q, engine="S"):
+        def x_pick(q):
             x_r[q] = sb([128, 1024], F32, "x_r", 2)
-            copy(
-                engine,
-                x_r[q][:].rearrange("p (a u j) -> p a u j", u=2, j=32),
-                x_q[q].bitcast(F32).rearrange("p (a j u) -> p a u j", u=2, j=32),
-            )
+            if q == 7:
+                for g in range(2):
+                    nc.scalar.copy(
+                        x_r[q][:, 512 * g : 512 * g + 512].rearrange("p (b c j) -> p b c j", b=2, c=8),
+                        x_d[q][:, g].rearrange("p c b j -> p b c j"),
+                    )
+            else:
+                nc.scalar.copy(x_r[q][:].rearrange("p (g c b j) -> p g c b j", g=2, c=8, b=2), x_d[q])
 
         def x_turn(q):
-            x_t[q] = sb([128, 1024], F32, "x_t", 2)
-            nc.vector.transpose(x_t[q][:], x_r[q][:])
-
-        def x_join(q, engine="S"):
             x_g[q] = sb([128, 2048], BF16, "x_g", 3)
-            if q in WIDE:
-                for g in range(2):
-                    copy(
-                        engine,
-                        x_g[q][:, 1024 * g : 1024 * g + 1024].bitcast(F32).rearrange("p (b c i u) -> p b c i u", b=2, u=2, i=32),
-                        x_t[q][:].rearrange("p (b g c u i) -> p g b c i u", b=2, g=2, u=2, i=32)[:, g],
-                    )
-            else:
-                copy(
-                    engine,
-                    x_g[q][:].bitcast(F32).rearrange("p (a i u) -> p a i u", u=2, i=32),
-                    x_t[q][:].rearrange("p (a u i) -> p a i u", u=2, i=32),
-                )
+            nc.vector.transpose(x_g[q][:].bitcast(F32), x_r[q][:])
 
-        def x_quant(q, b0=0, n=2):
-            nc.vector.quantize_mx(
-                out=x_c[q][:, 256 * b0 : 256 * (b0 + n)].bitcast(FP8X4),
-                scales=x_s[q][:, 256 * b0 : 256 * (b0 + n)],
-                in_=x_g[q][:, 1024 * b0 : 1024 * (b0 + n)],
-            )
+        def x_quant(q):
+            nc.vector.quantize_mx(out=x_c[q][:].bitcast(FP8X4), scales=x_s[q][:], in_=x_g[q][:])
 
         h_t = {}
+        h_half = {}
 
-        def mm1(m, G):
-            h = bank(("h", m, G), [128, 4, 128])
-            for t in range(4):
-                for g in range(2):
-                    k0 = 256 * g + 128 * (m % 2) if m // 2 in WIDE else 256 * (m % 2) + 128 * g
-                    k = slice(k0, k0 + 128)
-                    nc.tensor.matmul_mx(
-                        out=h[:, t, :],
-                        lhsT=w_c[g, G][:, 128 * t : 128 * t + 128].bitcast(FP8X4),
-                        lhsT_scale=w_s[g, G][:, 128 * t : 128 * t + 128],
-                        rhs=x_c[m // 2][:, k].bitcast(FP8X4), rhs_scale=x_s[m // 2][:, k],
-                        start=g == 0, stop=g == 1,
-                    )
+        def wide(q, G):
+            return (q, G) not in NARROW
 
-        def part(m, G):
-            return 2 * G + m % 2 if m // 2 in WIDE else 2 * (m % 2) + G
+        def part(q, b, G):
+            return 2 * b + G if q == 7 else 2 * G + b
 
         def h_tile(q):
             if q not in h_t:
                 h_t[q] = sb([128, 2048], BF16, "h_t", 4)
             return h_t[q]
 
-        def h_out(m, G, engine="S"):
-            j = part(m, G)
-            dst = h_tile(m // 2)[:, 512 * j : 512 * j + 512].rearrange("p (n t) -> p n t", t=4)
-            src = banks["h", m, G][:].rearrange("p t n -> p n t")
-            if engine == "S":
-                nc.scalar.activation(out=dst, in_=src, func=RELU)
-            else:
-                nc.vector.tensor_scalar_max(dst, src, 0.0)
-
-        h_half = {}
-
-        def mm1_wide(q, G, tp):
-            h = bank(("h", q, G, tp), [128, 2, 256])
-            for tt in range(2):
-                t = 2 * tp + tt
+        def first(q, G, j):
+            n = 256 if wide(q, G) else 128
+            h = bank(("h", q, G, j), [128, 512 // n, n])
+            for tt in range(512 // n):
+                t = 2 * j + tt if n == 256 else tt
                 for g in range(2):
-                    k = slice(256 * g, 256 * g + 256)
+                    k0 = 256 * g if n == 256 else 256 * g + 128 * j
                     nc.tensor.matmul_mx(
                         out=h[:, tt, :],
                         lhsT=w_c[g, G][:, 128 * t : 128 * t + 128].bitcast(FP8X4),
                         lhsT_scale=w_s[g, G][:, 128 * t : 128 * t + 128],
-                        rhs=x_c[q][:, k].bitcast(FP8X4), rhs_scale=x_s[q][:, k],
+                        rhs=x_c[q][:, k0 : k0 + n].bitcast(FP8X4), rhs_scale=x_s[q][:, k0 : k0 + n],
                         start=g == 0, stop=g == 1,
                     )
 
-        def h_out_wide(q, G, tp):
-            if tp == 0:
-                h_half[q, G] = sb([128, 2, 512], BF16, "h_half", 3)
-            nc.scalar.activation(
-                out=h_half[q, G][:, tp, :].rearrange("p (n e) -> p n e", e=2),
-                in_=banks["h", q, G, tp][:].rearrange("p e n -> p n e"), func=RELU,
-            )
+        def h_out(q, G, j):
+            src = banks["h", q, G, j][:]
+            if wide(q, G):
+                if j == 0:
+                    h_half[q, G] = sb([128, 2, 512], BF16, "h_half", 3)
+                dst = h_half[q, G][:, j, :]
+                if q < 4:
+                    dst, src = dst.rearrange("p (n e) -> p n e", e=2), src.rearrange("p e n -> p n e")
+                else:
+                    dst, src = dst.rearrange("p (a c e) -> p a c e", c=8, e=2), src.rearrange("p e (c a) -> p a c e", c=8)
+            else:
+                dst = h_tile(q)[:, 512 * part(q, j, G) : 512 * part(q, j, G) + 512]
+                if q < 4:
+                    dst, src = dst.rearrange("p (n t) -> p n t", t=4), src.rearrange("p t n -> p n t")
+                else:
+                    dst, src = dst.rearrange("p (i c t) -> p i c t", c=8, t=4), src.rearrange("p t (c i) -> p i c t", c=8)
+            nc.scalar.activation(out=dst, in_=src, func=RELU)
 
         def h_zip(q, G, engine):
-            copy(
-                engine,
-                h_tile(q)[:, 1024 * G : 1024 * G + 1024].bitcast(F32).rearrange("p (n i u) -> p n u i", i=2, u=2),
-                h_half[q, G][:].bitcast(F32).rearrange("p u (n i) -> p n u i", i=2),
-            )
+            if wide(q, G):
+                copy(
+                    engine,
+                    h_tile(q)[:, 1024 * G : 1024 * G + 1024].bitcast(F32).rearrange("p (n i u) -> p n u i", i=2, u=2),
+                    h_half[q, G][:].bitcast(F32).rearrange("p u (n i) -> p n u i", i=2),
+                )
 
-        def h_quant(q, j0, n):
+        def h_quant(q, j0=0, n=4):
             nc.vector.quantize_mx(
                 out=h_c[q][:, 128 * j0 : 128 * (j0 + n)].bitcast(FP8X4),
                 scales=h_s[q][:, 128 * j0 : 128 * (j0 + n)],
                 in_=h_t[q][:, 512 * j0 : 512 * (j0 + n)],
             )
 
-        def mm2(m, n0, n=512, passes=(0, 1)):
-            y = bank(("y", m, n0), [128, n]) if 0 in passes else banks["y", m, n0]
+        def mm2(m, n0, n=512):
+            y = bank(("y", m, n0), [128, n])
             nh, j0 = n0 // 512, n0 % 512
-            for G in passes:
-                k = slice(128 * part(m, G), 128 * part(m, G) + 128)
+            for G in range(2):
+                k = slice(128 * part(m // 2, m % 2, G), 128 * part(m // 2, m % 2, G) + 128)
                 nc.tensor.matmul_mx(
                     out=y[:],
                     lhsT=h_c[m // 2][:, k].bitcast(FP8X4), lhsT_scale=h_s[m // 2][:, k],
@@ -342,19 +287,19 @@ def tile_pointnet_set_encoder_s12_kernel(tc, x, w, u_words, u_scales, v_words, v
         load_x(2)
         load_w(1, 1)
         load_x(3)
-        load_x(4)
-        load_x_quads(5, 1)
-        load_x_quads(6, 2)
+        for q in range(4, 8):
+            load_x_twice(q, 1, 1, q - 4)
 
-        for m in range(4):
-            x_transpose(m)
-        x_out(0, "A")
+        for q in range(2):
+            for b in range(2):
+                x_transpose(q, b)
+        x_out(0, 0, "A")
         permute_u_scales()
         permute_u()
-        x_out(1, "V")
-        x_out(2, "S")
+        x_out(0, 1, "V")
+        x_out(1, 0, "S")
         x_quant(0)
-        x_out(3, "S")
+        x_out(1, 1, "S")
         for k in range(15):
             e_mm(k)
             e_out(k, "V" if k == 0 else "S")
@@ -368,35 +313,31 @@ def tile_pointnet_set_encoder_s12_kernel(tc, x, w, u_words, u_scales, v_words, v
                 w_quant(0, 1)
                 w_weave(1, 1)
         for q in range(2):
-            for m in (2 * q, 2 * q + 1):
-                mm1(m, 0)
-                h_out(m, 0)
-            for m in (2 * q + 4, 2 * q + 5):
-                x_transpose(m)
+            for j in range(2):
+                first(q, 0, j)
+                h_out(q, 0, j)
+            for b in range(2):
+                x_transpose(q + 2, b)
         e_mm(15)
         e_out(15, "S")
-        x_out(4, "V")
+        x_out(2, 0, "V")
         w_quant(1, 1)
-        x_out(5, "V")
-        x_out(6, "V")
+        x_out(2, 1, "V")
+        x_out(3, 0, "V")
         x_quant(2)
-        x_out(7, "S")
+        x_out(3, 1, "S")
         e_quant(0, 0)
-        for m in range(2):
-            mm1(m, 1)
-            h_out(m, 1)
-        for tp in range(2):
-            mm1_wide(1, 1, tp)
-            h_out_wide(1, 1, tp)
+        for q in range(2):
+            for j in range(2):
+                first(q, 1, j)
+                h_out(q, 1, j)
         e_quant(1, 0)
         x_quant(3)
-        h_quant(0, 0, 4)
+        h_quant(0)
         e_quant(0, 1)
-        x_sort(4, "V")
         h_zip(1, 1, "V")
         e_quant(1, 1)
-        h_quant(1, 0, 4)
-
+        h_quant(1)
 
         todo = [(m, 0) for m in range(2)] + [(m, 512) for m in range(2)] + [(m, n0) for m in range(2, 15) for n0 in (0, 512)]
         waiting = []
@@ -410,53 +351,35 @@ def tile_pointnet_set_encoder_s12_kernel(tc, x, w, u_words, u_scales, v_words, v
                 y_out(*waiting.pop(0))
 
         def due(slot, lead):
-            return (slot + lead) % 4 == 0 and PE_PAIRS <= (slot + lead) // 4 < 8
+            return (slot + lead) % 4 == 0 and 4 <= (slot + lead) // 4 + 2 < 8
 
-        for slot in range(8, 32):
-            q, m, G = slot // 4, slot // 2, slot % 2
-            turn = slot % 4 == 0 and 4 <= q + 1 < PE_PAIRS
-            if turn:
-                x_transpose(2 * q + 2)
-                x_transpose(2 * q + 3)
-            if q in WIDE:
-                mm1_wide(q, m % 2, G)
-            else:
-                mm1(m, G)
-            if slot > 9:
+        slots = [(q, G, j) for q in range(2, 7) for G in range(2) for j in range(2)]
+        slots = slots + [(7, G, j) for j in range(2) for G in range(2)]
+        for slot, (q, G, j) in enumerate(slots):
+            first(q, G, j)
+            if slot >= FIRST_SECOND:
                 second()
-            if slot >= 24 and G == 1:
+            if slot >= LATE and slot % 2 == 1:
                 second()
-            if turn:
-                x_out(2 * q + 2, "S")
-                x_out(2 * q + 3, "S")
-            if q in WIDE:
-                h_out_wide(q, m % 2, G)
-            else:
-                h_out(m, G)
-            if due(slot, 7):
-                x_split((slot + 7) // 4, "V" if (slot + 7) // 4 in (5,) else "S")
-            if due(slot, 4):
-                x_join((slot + 4) // 4)
-            drain(1 if slot < 26 else 0)
-            if G == 0 and slot > 8 and (slot - 1) // 4 in WIDE:
-                h_zip((slot - 1) // 4, (slot - 1) // 2 % 2, "S" if slot >= 24 else "V")
-            if slot % 4 == 1 and 4 <= q + 1 < PE_PAIRS:
-                x_quant(q + 1)
-            if slot % 4 == 2 and 5 <= q + 2 < PE_PAIRS:
-                x_sort(q + 2, "S")
-            if due(slot, 6):
-                x_turn((slot + 6) // 4)
+            h_out(q, G, j)
+            if due(slot, PICK_LEAD):
+                x_pick((slot + PICK_LEAD) // 4 + 2)
+            drain(1 if slot < HOLD_UNTIL else 0)
+            if slot % 2 == 0 and 0 < slot <= 20:
+                h_zip(*slots[slot - 1][:2], "S" if slot // 2 >= ZIP_ON_SCALAR else "V")
+            if due(slot, PICK_LEAD - 1):
+                x_turn((slot + PICK_LEAD - 1) // 4 + 2)
             if due(slot, 3):
-                x_quant((slot + 3) // 4)
-            if slot % 4 == 1 and slot >= 12:
-                h_quant(q - 1, 0, 4)
-            if slot == 30:
+                x_quant((slot + 3) // 4 + 2)
+            if slot % 4 == 1 and slot >= 4:
+                h_quant(q - 1)
+            if slot == 22:
                 h_quant(7, 0, 2)
                 h_quant(7, 2, 1)
         h_quant(7, 3, 1)
         while todo:
             second()
             drain(0)
-        for n0, n in ((0, 256), (256, 256), (512, 256), (768, 256)):
-            mm2(15, n0, n)
-            y_out(15, n0, n)
+        for n0 in range(0, 1024, 256):
+            mm2(15, n0, 256)
+            y_out(15, n0, 256)

@@ -21,7 +21,10 @@ FIRST_SECOND = 2
 LATE = 16
 HOLD_UNTIL = 18
 ZIP_ON_SCALAR = 4
-PICK_LEAD = 5
+PICK_LEAD = 6
+SPLIT_LEAD = 7
+TWICE = (4, 5, 6, 7)
+SPLIT_ON_VECTOR = (5,)
 
 
 def tile_pointnet_set_encoder_s12_kernel(tc, x, w, u_words, u_scales, v_words, v_scales, out):
@@ -74,16 +77,26 @@ def tile_pointnet_set_encoder_s12_kernel(tc, x, w, u_words, u_scales, v_words, v
 
         x_d = {}
 
-        def load_x_twice(q0, n, s, r):
-            rows = x.rearrange("(s i m r) k -> s r i m k", s=2, i=16, r=4 // n)[s, r]
-            t = sb([128, 2, 16 * n, 128], BF16, "x_d%d" % q0)
+        def load_x_twice(q):
+            t = sb([128, 2, 16, 128], BF16, "x_d%d" % q)
+            flat = x.rearrange("p k -> (p k)")
+            for g in range(2):
+                for u in range(2):
+                    first_word = 1024 * 1024 - 2 + 2 * u
+                    rows = flat[first_word : first_word + 1024 * 1024].rearrange("(i m r k) -> r i m k", i=16, m=16, r=4)[q - 4]
+                    for Q in (0, 2, 1, 3):
+                        k0 = 512 * g + 128 * Q
+                        nc.sync.dma_start(out=t[32 * Q + u : 32 * Q + 32 : 2, g], in_=rows[:, :, k0 : k0 + 128])
+            x_d[q] = t[:].bitcast(F32).rearrange("p g (c b) (j u) -> p g c b j u", b=2, u=2)[:, :, :, :, :, 1]
+
+        def load_x_once(q):
+            t = sb([128, 2, 8, 128], BF16, "x_d%d" % q)
+            rows = x.rearrange("(s i m r) k -> s r i m k", s=2, i=32, r=4)[1, q - 4]
             for g in range(2):
                 for Q in (0, 2, 1, 3):
-                    for u in range(2):
-                        k0 = 512 * g + 128 * Q + 2 * u
-                        nc.sync.dma_start(out=t[32 * Q + u : 32 * Q + 32 : 2, g, :, 0:126], in_=rows[:, :, k0 : k0 + 126])
-            for j in range(n):
-                x_d[q0 + j] = t[:].bitcast(F32).rearrange("p g (c a b) (j u) -> p a g c b j u", c=8, b=2, u=2)[:, j, :, :, :, :, 0]
+                    k0 = 512 * g + 128 * Q
+                    nc.sync.dma_start(out=t[32 * Q : 32 * Q + 32, g], in_=rows[:, :, k0 : k0 + 128])
+            x_d[q] = t[:].bitcast(F32).rearrange("p g m (j u) -> p (g m) u j", u=2)
 
         def load_w(g, G):
             nc.sync.dma_start(out=w_raw[g, G][:], in_=w_rows[g][:, :, 512 * G : 512 * G + 512])
@@ -167,7 +180,9 @@ def tile_pointnet_set_encoder_s12_kernel(tc, x, w, u_words, u_scales, v_words, v
 
         def x_pick(q):
             x_r[q] = sb([128, 1024], F32, "x_r", 2)
-            if q == 7:
+            if q not in TWICE:
+                copy("V" if q in SPLIT_ON_VECTOR else "S", x_r[q][:].rearrange("p (a u j) -> p a u j", u=2, j=32), x_d[q])
+            elif q == 7:
                 for g in range(2):
                     nc.scalar.copy(
                         x_r[q][:, 512 * g : 512 * g + 512].rearrange("p (b c j) -> p b c j", b=2, c=8),
@@ -176,9 +191,23 @@ def tile_pointnet_set_encoder_s12_kernel(tc, x, w, u_words, u_scales, v_words, v
             else:
                 nc.scalar.copy(x_r[q][:].rearrange("p (g c b j) -> p g c b j", g=2, c=8, b=2), x_d[q])
 
+        x_t = {}
+
         def x_turn(q):
-            x_g[q] = sb([128, 2048], BF16, "x_g", 3)
-            nc.vector.transpose(x_g[q][:].bitcast(F32), x_r[q][:])
+            if q in TWICE:
+                x_g[q] = sb([128, 2048], BF16, "x_g", 3)
+                nc.vector.transpose(x_g[q][:].bitcast(F32), x_r[q][:])
+            else:
+                x_t[q] = sb([128, 1024], F32, "x_t", 2)
+                nc.vector.transpose(x_t[q][:], x_r[q][:])
+
+        def x_join(q):
+            if q not in TWICE:
+                x_g[q] = sb([128, 2048], BF16, "x_g", 3)
+                nc.scalar.copy(
+                    x_g[q][:].bitcast(F32).rearrange("p (a i u) -> p a i u", u=2, i=32),
+                    x_t[q][:].rearrange("p (a u i) -> p a i u", u=2, i=32),
+                )
 
         def x_quant(q):
             nc.vector.quantize_mx(out=x_c[q][:].bitcast(FP8X4), scales=x_s[q][:], in_=x_g[q][:])
@@ -214,6 +243,7 @@ def tile_pointnet_set_encoder_s12_kernel(tc, x, w, u_words, u_scales, v_words, v
 
         def h_out(q, G, j):
             src = banks["h", q, G, j][:]
+            blocks = 8 if q in TWICE else 4
             if wide(q, G):
                 if j == 0:
                     h_half[q, G] = sb([128, 2, 512], BF16, "h_half", 3)
@@ -221,7 +251,7 @@ def tile_pointnet_set_encoder_s12_kernel(tc, x, w, u_words, u_scales, v_words, v
                 if q < 4:
                     dst, src = dst.rearrange("p (n e) -> p n e", e=2), src.rearrange("p e n -> p n e")
                 else:
-                    dst, src = dst.rearrange("p (a c e) -> p a c e", c=8, e=2), src.rearrange("p e (c a) -> p a c e", c=8)
+                    dst, src = dst.rearrange("p (a c e) -> p a c e", c=blocks, e=2), src.rearrange("p e (c a) -> p a c e", c=blocks)
             else:
                 dst = h_tile(q)[:, 512 * part(q, j, G) : 512 * part(q, j, G) + 512]
                 if q < 4:
@@ -288,7 +318,10 @@ def tile_pointnet_set_encoder_s12_kernel(tc, x, w, u_words, u_scales, v_words, v
         load_w(1, 1)
         load_x(3)
         for q in range(4, 8):
-            load_x_twice(q, 1, 1, q - 4)
+            if q in TWICE:
+                load_x_twice(q)
+            else:
+                load_x_once(q)
 
         for q in range(2):
             for b in range(2):
@@ -350,8 +383,8 @@ def tile_pointnet_set_encoder_s12_kernel(tc, x, w, u_words, u_scales, v_words, v
             while len(waiting) > keep_back or (waiting and waiting[0][0] % 8 == 0):
                 y_out(*waiting.pop(0))
 
-        def due(slot, lead):
-            return (slot + lead) % 4 == 0 and 4 <= (slot + lead) // 4 + 2 < 8
+        def due(slot, lead_twice, lead_once):
+            return [q for q in range(4, 8) if slot + (lead_twice if q in TWICE else lead_once) == 4 * (q - 2)]
 
         slots = [(q, G, j) for q in range(2, 7) for G in range(2) for j in range(2)]
         slots = slots + [(7, G, j) for j in range(2) for G in range(2)]
@@ -362,15 +395,17 @@ def tile_pointnet_set_encoder_s12_kernel(tc, x, w, u_words, u_scales, v_words, v
             if slot >= LATE and slot % 2 == 1:
                 second()
             h_out(q, G, j)
-            if due(slot, PICK_LEAD):
-                x_pick((slot + PICK_LEAD) // 4 + 2)
+            for p in due(slot, PICK_LEAD, SPLIT_LEAD):
+                x_pick(p)
+            for p in due(slot, 4, 4):
+                x_join(p)
             drain(1 if slot < HOLD_UNTIL else 0)
             if slot % 2 == 0 and 0 < slot <= 20:
                 h_zip(*slots[slot - 1][:2], "S" if slot // 2 >= ZIP_ON_SCALAR else "V")
-            if due(slot, PICK_LEAD - 1):
-                x_turn((slot + PICK_LEAD - 1) // 4 + 2)
-            if due(slot, 3):
-                x_quant((slot + 3) // 4 + 2)
+            for p in due(slot, PICK_LEAD - 1, SPLIT_LEAD - 1):
+                x_turn(p)
+            for p in due(slot, 3, 3):
+                x_quant(p)
             if slot % 4 == 1 and slot >= 4:
                 h_quant(q - 1)
             if slot == 22:

@@ -79,15 +79,14 @@ def tile_pointnet_set_encoder_s12_kernel(tc, x, w, u_words, u_scales, v_words, v
 
         def load_x_twice(q):
             t = sb([128, 2, 16, 128], BF16, "x_d%d" % q)
-            flat = x.rearrange("p k -> (p k)")
+            rows = x.rearrange("(s i m r) k -> s r i m k", s=2, i=16, r=4)[1, q - 4]
             for g in range(2):
                 for u in range(2):
-                    first_word = 1024 * 1024 - 2 + 2 * u
-                    rows = flat[first_word : first_word + 1024 * 1024].rearrange("(i m r k) -> r i m k", i=16, m=16, r=4)[q - 4]
                     for Q in (0, 2, 1, 3):
-                        k0 = 512 * g + 128 * Q
-                        nc.sync.dma_start(out=t[32 * Q + u : 32 * Q + 32 : 2, g], in_=rows[:, :, k0 : k0 + 128])
-            x_d[q] = t[:].bitcast(F32).rearrange("p g (c b) (j u) -> p g c b j u", b=2, u=2)[:, :, :, :, :, 1]
+                        k0 = 512 * g + 128 * Q + 2 * u
+                        n = min(128, 1024 - k0)
+                        nc.sync.dma_start(out=t[32 * Q + u : 32 * Q + 32 : 2, g, :, 0:n], in_=rows[:, :, k0 : k0 + n])
+            x_d[q] = t[:].bitcast(F32).rearrange("p g (c b) (j u) -> p g c b j u", b=2, u=2)[:, :, :, :, :, 0]
 
         def load_x_once(q):
             t = sb([128, 2, 8, 128], BF16, "x_d%d" % q)

@@ -16,15 +16,23 @@ MAX = mybir.AluOpType.max
 RELU = mybir.ActivationFunctionType.Relu
 COPY = mybir.ActivationFunctionType.Copy
 
-NARROW = ((0, 0), (0, 1), (1, 0), (7, 0), (7, 1))
+NARROW = ((0, 0), (0, 1), (1, 0), (4, 1), (7, 0), (7, 1))
 FIRST_SECOND = 2
 LATE = 16
 HOLD_UNTIL = 18
-ZIP_ON_SCALAR = 4
+NPE = 4
+SORT = ()
+SORTE = "V"
+TLEAD = 4
+X4E = "SS"
+XE = "VVVS"
+EV = (0,)
+ZE = "VVVSSSSSSSS"
+END = ((0, 256), (256, 256), (512, 256), (768, 256))
 PICK_LEAD = 6
 SPLIT_LEAD = 7
 TWICE = (4, 5, 6, 7)
-SPLIT_ON_VECTOR = (5,)
+SPLIT_ON_VECTOR = (4,)
 
 
 def tile_pointnet_set_encoder_s12_kernel(tc, x, w, u_words, u_scales, v_words, v_scales, out):
@@ -53,7 +61,7 @@ def tile_pointnet_set_encoder_s12_kernel(tc, x, w, u_words, u_scales, v_words, v
         v_w = sb([128, 2048], U8, "v_w")
         v_pl = sb([128, 1024], U8, "v_pl")
         ident = sb([128, 128], F32, "ident")
-        x_sb = [sb([128, 2048], BF16, "x_sb%d" % q) for q in range(4)]
+        x_sb = [sb([128, 2048], BF16, "x_sb%d" % q) for q in range(NPE)]
         x_c = [sb([128, 512], U32, "x_c%d" % q) for q in range(8)]
         x_s = [sb([128, 512], U8, "x_s%d" % q) for q in range(8)]
         w_raw = {k: sb([128, 4, 512], BF16, "w_raw%d%d" % k) for k in quarters}
@@ -73,7 +81,8 @@ def tile_pointnet_set_encoder_s12_kernel(tc, x, w, u_words, u_scales, v_words, v
         w_rows = w.rearrange("(g p j) f -> g p j f", g=2, p=128, j=4)
 
         def load_x(q):
-            nc.sync.dma_start(out=x_sb[q][:].rearrange("p (b k) -> p b k", b=2), in_=x_rows[0][:, 2 * q : 2 * q + 2, :])
+            points = slice(2 * q, 2 * q + 2) if q < 4 else slice(q - 4, 8, 4)
+            nc.sync.dma_start(out=x_sb[q][:].rearrange("p (b k) -> p b k", b=2), in_=x_rows[q // 4][:, points, :])
 
         x_d = {}
 
@@ -161,7 +170,11 @@ def tile_pointnet_set_encoder_s12_kernel(tc, x, w, u_words, u_scales, v_words, v
             for g in range(2):
                 base = b * 512 + g * 256
                 for u in range(2):
-                    nc.tensor.transpose(xt[:, g, u, :], x_sb[q][:].bitcast(F32)[:, base + u : base + 256 : 2], ident[:])
+                    if q in SORT:
+                        words = x_r[q][:, base + 128 * u : base + 128 * u + 128]
+                    else:
+                        words = x_sb[q][:].bitcast(F32)[:, base + u : base + 256 : 2]
+                    nc.tensor.transpose(xt[:, g, u, :], words, ident[:])
 
         def x_out(q, b, engine):
             if q not in x_g:
@@ -177,18 +190,27 @@ def tile_pointnet_set_encoder_s12_kernel(tc, x, w, u_words, u_scales, v_words, v
                 return
             copy(engine, dst, banks["x", q, b][:].rearrange("p g u n -> p g n u"))
 
+        def x_sort(q, engine):
+            x_r[q] = sb([128, 1024], F32, "x_r", 2)
+            copy(
+                engine,
+                x_r[q][:].rearrange("p (a u w) -> p a u w", u=2, w=128),
+                x_sb[q][:].bitcast(F32).rearrange("p (a w u) -> p a u w", u=2, w=128),
+            )
+
         def x_pick(q):
             x_r[q] = sb([128, 1024], F32, "x_r", 2)
             if q not in TWICE:
                 copy("V" if q in SPLIT_ON_VECTOR else "S", x_r[q][:].rearrange("p (a u j) -> p a u j", u=2, j=32), x_d[q])
             elif q == 7:
-                for g in range(2):
-                    nc.scalar.copy(
+                for g in (1, 0):
+                    copy(
+                        "V" if q in SPLIT_ON_VECTOR else "S",
                         x_r[q][:, 512 * g : 512 * g + 512].rearrange("p (b c j) -> p b c j", b=2, c=8),
                         x_d[q][:, g].rearrange("p c b j -> p b c j"),
                     )
             else:
-                nc.scalar.copy(x_r[q][:].rearrange("p (g c b j) -> p g c b j", g=2, c=8, b=2), x_d[q])
+                copy("V" if q in SPLIT_ON_VECTOR else "S", x_r[q][:].rearrange("p (g c b j) -> p g c b j", g=2, c=8, b=2), x_d[q])
 
         x_t = {}
 
@@ -247,16 +269,19 @@ def tile_pointnet_set_encoder_s12_kernel(tc, x, w, u_words, u_scales, v_words, v
                 if j == 0:
                     h_half[q, G] = sb([128, 2, 512], BF16, "h_half", 3)
                 dst = h_half[q, G][:, j, :]
-                if q < 4:
+                if q < NPE:
                     dst, src = dst.rearrange("p (n e) -> p n e", e=2), src.rearrange("p e n -> p n e")
                 else:
                     dst, src = dst.rearrange("p (a c e) -> p a c e", c=blocks, e=2), src.rearrange("p e (c a) -> p a c e", c=blocks)
             else:
                 dst = h_tile(q)[:, 512 * part(q, j, G) : 512 * part(q, j, G) + 512]
-                if q < 4:
+                if q < NPE:
                     dst, src = dst.rearrange("p (n t) -> p n t", t=4), src.rearrange("p t n -> p n t")
-                else:
+                elif q == 7:
                     dst, src = dst.rearrange("p (i c t) -> p i c t", c=8, t=4), src.rearrange("p t (c i) -> p i c t", c=8)
+                else:
+                    dst = h_tile(q)[:, 1024 * G : 1024 * G + 1024].rearrange("p (a c t) -> p a c t", c=8, t=4)[:, :, 4 * j : 4 * j + 4]
+                    src = src.rearrange("p t (c a) -> p a c t", c=4)
             nc.scalar.activation(out=dst, in_=src, func=RELU)
 
         def h_zip(q, G, engine):
@@ -316,7 +341,9 @@ def tile_pointnet_set_encoder_s12_kernel(tc, x, w, u_words, u_scales, v_words, v
         load_x(2)
         load_w(1, 1)
         load_x(3)
-        for q in range(4, 8):
+        for q in range(4, NPE):
+            load_x(q)
+        for q in range(NPE, 8):
             if q in TWICE:
                 load_x_twice(q)
             else:
@@ -334,7 +361,7 @@ def tile_pointnet_set_encoder_s12_kernel(tc, x, w, u_words, u_scales, v_words, v
         x_out(1, 1, "S")
         for k in range(15):
             e_mm(k)
-            e_out(k, "V" if k == 0 else "S")
+            e_out(k, "V" if k in EV else "S")
             if k == 0:
                 w_weave(0, 0)
                 w_weave(1, 0)
@@ -352,12 +379,12 @@ def tile_pointnet_set_encoder_s12_kernel(tc, x, w, u_words, u_scales, v_words, v
                 x_transpose(q + 2, b)
         e_mm(15)
         e_out(15, "S")
-        x_out(2, 0, "V")
+        x_out(2, 0, XE[0])
         w_quant(1, 1)
-        x_out(2, 1, "V")
-        x_out(3, 0, "V")
+        x_out(2, 1, XE[1])
+        x_out(3, 0, XE[2])
         x_quant(2)
-        x_out(3, 1, "S")
+        x_out(3, 1, XE[3])
         e_quant(0, 0)
         for q in range(2):
             for j in range(2):
@@ -367,7 +394,7 @@ def tile_pointnet_set_encoder_s12_kernel(tc, x, w, u_words, u_scales, v_words, v
         x_quant(3)
         h_quant(0)
         e_quant(0, 1)
-        h_zip(1, 1, "V")
+        h_zip(1, 1, ZE[0])
         e_quant(1, 1)
         h_quant(1)
 
@@ -383,16 +410,23 @@ def tile_pointnet_set_encoder_s12_kernel(tc, x, w, u_words, u_scales, v_words, v
                 y_out(*waiting.pop(0))
 
         def due(slot, lead_twice, lead_once):
-            return [q for q in range(4, 8) if slot + (lead_twice if q in TWICE else lead_once) == 4 * (q - 2)]
+            return [q for q in range(NPE, 8) if slot + (lead_twice if q in TWICE else lead_once) == 4 * (q - 2)]
 
         slots = [(q, G, j) for q in range(2, 7) for G in range(2) for j in range(2)]
         slots = slots + [(7, G, j) for j in range(2) for G in range(2)]
         for slot, (q, G, j) in enumerate(slots):
+            turn = [p for p in range(4, NPE) if slot + TLEAD == 4 * (p - 2)]
+            for p in turn:
+                for b in range(2):
+                    x_transpose(p, b)
             first(q, G, j)
             if slot >= FIRST_SECOND:
                 second()
             if slot >= LATE and slot % 2 == 1:
                 second()
+            for p in turn:
+                for b in range(2):
+                    x_out(p, b, X4E[b])
             h_out(q, G, j)
             for p in due(slot, PICK_LEAD, SPLIT_LEAD):
                 x_pick(p)
@@ -400,11 +434,16 @@ def tile_pointnet_set_encoder_s12_kernel(tc, x, w, u_words, u_scales, v_words, v
                 x_join(p)
             drain(1 if slot < HOLD_UNTIL else 0)
             if slot % 2 == 0 and 0 < slot <= 20:
-                h_zip(*slots[slot - 1][:2], "S" if slot // 2 >= ZIP_ON_SCALAR else "V")
+                h_zip(*slots[slot - 1][:2], ZE[slot // 2])
             for p in due(slot, PICK_LEAD - 1, SPLIT_LEAD - 1):
                 x_turn(p)
             for p in due(slot, 3, 3):
                 x_quant(p)
+            for p in range(4, NPE):
+                if slot + TLEAD - 1 == 4 * (p - 2):
+                    x_quant(p)
+                if slot + TLEAD + 2 == 4 * (p - 2) and p in SORT:
+                    x_sort(p, SORTE)
             if slot % 4 == 1 and slot >= 4:
                 h_quant(q - 1)
             if slot == 22:
@@ -414,6 +453,6 @@ def tile_pointnet_set_encoder_s12_kernel(tc, x, w, u_words, u_scales, v_words, v
         while todo:
             second()
             drain(0)
-        for n0 in range(0, 1024, 256):
-            mm2(15, n0, 256)
-            y_out(15, n0, 256)
+        for n0, n in END:
+            mm2(15, n0, n)
+            y_out(15, n0, n)

@@ -16,7 +16,7 @@ MAX = mybir.AluOpType.max
 RELU = mybir.ActivationFunctionType.Relu
 COPY = mybir.ActivationFunctionType.Copy
 
-NARROW = ((0, 0), (0, 1), (1, 0), (4, 1), (7, 0), (7, 1))
+NARROW = ((0, 0), (0, 1), (1, 0), (4, 0), (7, 0), (7, 1))
 FIRST_SECOND = 2
 LATE = 16
 HOLD_UNTIL = 18
@@ -27,11 +27,11 @@ TLEAD = 4
 X4E = "SS"
 XE = "VVVS"
 EV = (0,)
-ZE = "VVVSSSSSSSS"
+ZE = "VVVSVSVSVSS"
 END = ((0, 256), (256, 256), (512, 256), (768, 256))
 PICK_LEAD = 6
 SPLIT_LEAD = 7
-TWICE = (4, 5, 6, 7)
+TWICE = (4,)
 SPLIT_ON_VECTOR = (4,)
 
 
@@ -97,14 +97,15 @@ def tile_pointnet_set_encoder_s12_kernel(tc, x, w, u_words, u_scales, v_words, v
                         nc.sync.dma_start(out=t[32 * Q + u : 32 * Q + 32 : 2, g, :, 0:n], in_=rows[:, :, k0 : k0 + n])
             x_d[q] = t[:].bitcast(F32).rearrange("p g (c b) (j u) -> p g c b j u", b=2, u=2)[:, :, :, :, :, 0]
 
-        def load_x_once(q):
-            t = sb([128, 2, 8, 128], BF16, "x_d%d" % q)
-            rows = x.rearrange("(s i m r) k -> s r i m k", s=2, i=32, r=4)[1, q - 4]
+        def load_x_once(q0, n, r):
+            t = sb([128, 2, 8 * n, 128], BF16, "x_d%d" % q0)
+            rows = x.rearrange("(s i m r) k -> s r i m k", s=2, i=32, r=4 // n)[1, r]
             for g in range(2):
                 for Q in (0, 2, 1, 3):
                     k0 = 512 * g + 128 * Q
                     nc.sync.dma_start(out=t[32 * Q : 32 * Q + 32, g], in_=rows[:, :, k0 : k0 + 128])
-            x_d[q] = t[:].bitcast(F32).rearrange("p g m (j u) -> p (g m) u j", u=2)
+            for a in range(n):
+                x_d[q0 + a] = t[:].bitcast(F32).rearrange("p g (c a b) (j u) -> p a (g c) b u j", a=n, b=2, u=2)[:, a]
 
         def load_w(g, G):
             nc.sync.dma_start(out=w_raw[g, G][:], in_=w_rows[g][:, :, 512 * G : 512 * G + 512])
@@ -201,7 +202,7 @@ def tile_pointnet_set_encoder_s12_kernel(tc, x, w, u_words, u_scales, v_words, v
         def x_pick(q):
             x_r[q] = sb([128, 1024], F32, "x_r", 2)
             if q not in TWICE:
-                copy("V" if q in SPLIT_ON_VECTOR else "S", x_r[q][:].rearrange("p (a u j) -> p a u j", u=2, j=32), x_d[q])
+                copy("V" if q in SPLIT_ON_VECTOR else "S", x_r[q][:].rearrange("p (a b u j) -> p a b u j", b=2, u=2, j=32), x_d[q])
             elif q == 7:
                 for g in (1, 0):
                     copy(
@@ -225,10 +226,17 @@ def tile_pointnet_set_encoder_s12_kernel(tc, x, w, u_words, u_scales, v_words, v
         def x_join(q):
             if q not in TWICE:
                 x_g[q] = sb([128, 2048], BF16, "x_g", 3)
-                nc.scalar.copy(
-                    x_g[q][:].bitcast(F32).rearrange("p (a i u) -> p a i u", u=2, i=32),
-                    x_t[q][:].rearrange("p (a u i) -> p a i u", u=2, i=32),
-                )
+                if q < 7:
+                    nc.scalar.copy(
+                        x_g[q][:].bitcast(F32).rearrange("p (a i u) -> p a i u", u=2, i=32),
+                        x_t[q][:].rearrange("p (a u i) -> p a i u", u=2, i=32),
+                    )
+                else:
+                    for g in range(2):
+                        nc.scalar.copy(
+                            x_g[q][:, 1024 * g : 1024 * g + 1024].bitcast(F32).rearrange("p (b c i u) -> p b c i u", b=2, u=2, i=32),
+                            x_t[q][:].rearrange("p (g c b u i) -> p g b c i u", g=2, b=2, u=2, i=32)[:, g],
+                        )
 
         def x_quant(q):
             nc.vector.quantize_mx(out=x_c[q][:].bitcast(FP8X4), scales=x_s[q][:], in_=x_g[q][:])
@@ -278,10 +286,10 @@ def tile_pointnet_set_encoder_s12_kernel(tc, x, w, u_words, u_scales, v_words, v
                 if q < NPE:
                     dst, src = dst.rearrange("p (n t) -> p n t", t=4), src.rearrange("p t n -> p n t")
                 elif q == 7:
-                    dst, src = dst.rearrange("p (i c t) -> p i c t", c=8, t=4), src.rearrange("p t (c i) -> p i c t", c=8)
+                    dst, src = dst.rearrange("p (i c t) -> p i c t", c=blocks, t=4), src.rearrange("p t (c i) -> p i c t", c=blocks)
                 else:
-                    dst = h_tile(q)[:, 1024 * G : 1024 * G + 1024].rearrange("p (a c t) -> p a c t", c=8, t=4)[:, :, 4 * j : 4 * j + 4]
-                    src = src.rearrange("p t (c a) -> p a c t", c=4)
+                    dst = h_tile(q)[:, 1024 * G : 1024 * G + 1024].rearrange("p (a j c t) -> p j a c t", j=2, c=blocks // 2, t=4)[:, j]
+                    src = src.rearrange("p t (c a) -> p a c t", c=blocks // 2)
             nc.scalar.activation(out=dst, in_=src, func=RELU)
 
         def h_zip(q, G, engine):
@@ -341,13 +349,9 @@ def tile_pointnet_set_encoder_s12_kernel(tc, x, w, u_words, u_scales, v_words, v
         load_x(2)
         load_w(1, 1)
         load_x(3)
-        for q in range(4, NPE):
-            load_x(q)
-        for q in range(NPE, 8):
-            if q in TWICE:
-                load_x_twice(q)
-            else:
-                load_x_once(q)
+        load_x_twice(4)
+        load_x_once(5, 1, 2)
+        load_x_once(6, 2, 1)
 
         for q in range(2):
             for b in range(2):

@@ -21,6 +21,14 @@ FIRST_SECOND = 2
 LATE = 16
 HOLD_UNTIL = 18
 NPE = 4
+X2FIRST = 0
+X1E = "VV"
+X2E = "VVSS"
+WH = 2
+XQ0 = 0
+T1AT = 12
+WARM = 0
+WARM2 = 0
 SORT = ()
 SORTE = "V"
 TLEAD = 4
@@ -131,14 +139,19 @@ def tile_pointnet_set_encoder_s12_kernel(tc, x, w, u_words, u_scales, v_words, v
                 in_=u_pl_raw[:].bitcast(I32).rearrange("p (G q t) -> p G t q", G=2, q=32, t=4),
             )
 
-        def w_weave(g, G):
-            nc.vector.tensor_copy(
-                out=w_grp[g, G][:].rearrange("p (t q r j) -> p t q j r", t=4, q=32, r=4, j=4),
-                in_=w_raw[g, G][:].rearrange("p j (q t r) -> p t q j r", q=32, t=4, r=4),
+        def w_weave(g, G, t0=0, n=4, engine="V"):
+            copy(
+                engine,
+                w_grp[g, G][:].rearrange("p (t q r j) -> p t q j r", t=4, q=32, r=4, j=4)[:, t0 : t0 + n],
+                w_raw[g, G][:].rearrange("p j (q t r) -> p t q j r", q=32, t=4, r=4)[:, t0 : t0 + n],
             )
 
-        def w_quant(g, G):
-            nc.vector.quantize_mx(out=w_c[g, G][:].bitcast(FP8X4), scales=w_s[g, G][:], in_=w_grp[g, G][:])
+        def w_quant(g, G, t0=0, n=4):
+            nc.vector.quantize_mx(
+                out=w_c[g, G][:, 128 * t0 : 128 * (t0 + n)].bitcast(FP8X4),
+                scales=w_s[g, G][:, 128 * t0 : 128 * (t0 + n)],
+                in_=w_grp[g, G][:, 512 * t0 : 512 * (t0 + n)],
+            )
 
         def e_mm(k):
             G, nb = k // 4 % 2, k % 4 + k // 8 * 4
@@ -335,61 +348,74 @@ def tile_pointnet_set_encoder_s12_kernel(tc, x, w, u_words, u_scales, v_words, v
         nc.vector.memset(ident[:], 0.0)
         load_x(0)
         nc.sync.dma_start(out=u_raw[:].bitcast(I32), in_=u_words[0].bitcast(I32))
-        load_x(1)
-        for Q in range(3):
+        for Q in range(2):
             load_scales(nc.gpsimd, v_pl, vs32, Q)
         make_identity(nc, ident[:], nomemset=True)
-        load_scales(nc.scalar, v_pl, vs32, 3)
         for Q in range(4):
             load_scales(nc.scalar, u_pl_raw, us32, Q)
+        load_scales(nc.sync, v_pl, vs32, 2)
         nc.sync.dma_start(out=v_w[:].bitcast(I32), in_=v_words[0].bitcast(I32))
+        load_scales(nc.sync, v_pl, vs32, 3)
         load_w(0, 0)
         load_w(1, 0)
+        load_x(1)
         load_w(0, 1)
-        load_x(2)
+        if X2FIRST:
+            load_x(2)
         load_w(1, 1)
+        if not X2FIRST:
+            load_x(2)
         load_x(3)
         load_x_twice(4)
         load_x_once(5, 1, 2)
         load_x_once(6, 2, 1)
 
-        for q in range(2):
-            for b in range(2):
-                x_transpose(q, b)
-        x_out(0, 0, "A")
-        permute_u_scales()
+        if WARM:
+            zero = sb([128, 512], BF16, "zero")
+            nc.vector.memset(zero[:].bitcast(I32), 0)
+            warm = bank("warm", [128, 512])
+            for i in range(WARM):
+                nc.tensor.matmul(warm[:], lhsT=zero[:, 0:128], rhs=zero[:], start=True, stop=True)
+        for b in range(2):
+            x_transpose(0, b)
+        for i in range(WARM2):
+            nc.tensor.matmul(warm[:], lhsT=zero[:, 0:128], rhs=zero[:], start=True, stop=True)
         permute_u()
+        permute_u_scales()
+        x_out(0, 0, "A")
         x_out(0, 1, "V")
-        x_out(1, 0, "S")
-        x_quant(0)
-        x_out(1, 1, "S")
-        for k in range(15):
+        for k in range(16):
+            if k == T1AT:
+                for b in range(2):
+                    x_transpose(1, b)
             e_mm(k)
             e_out(k, "V" if k in EV else "S")
-            if k == 0:
+            if k == XQ0:
+                x_quant(0)
+            if k == max(EV):
                 w_weave(0, 0)
                 w_weave(1, 0)
                 w_quant(0, 0)
                 w_quant(1, 0)
-                w_weave(0, 1)
-                x_quant(1)
-                w_quant(0, 1)
-                w_weave(1, 1)
+            if k == T1AT:
+                x_out(1, 0, X1E[0])
+                x_out(1, 1, X1E[1])
+        w_weave(0, 1, 0, WH)
+        x_quant(1)
+        w_weave(0, 1, WH, 4 - WH)
+        w_weave(1, 1)
+        w_quant(0, 1)
+        w_quant(1, 1)
         for q in range(2):
             for j in range(2):
                 first(q, 0, j)
                 h_out(q, 0, j)
+        for q in range(2, 4):
             for b in range(2):
-                x_transpose(q + 2, b)
-        e_mm(15)
-        e_out(15, "S")
-        x_out(2, 0, XE[0])
-        w_quant(1, 1)
-        x_out(2, 1, XE[1])
-        x_out(3, 0, XE[2])
-        x_quant(2)
-        x_out(3, 1, XE[3])
+                x_transpose(q, b)
+                x_out(q, b, X2E[2 * q + b - 4])
         e_quant(0, 0)
+        x_quant(2)
         for q in range(2):
             for j in range(2):
                 first(q, 1, j)

@@ -27,8 +27,8 @@ X2E = "VVSS"
 WH = 2
 XQ0 = 0
 T1AT = 12
-WARM = 0
-WARM2 = 0
+WARM = 5
+WARM2 = 1
 SORT = ()
 SORTE = "V"
 TLEAD = 4

@@ -14,33 +14,24 @@ FP8X4 = mybir.dt.float8_e4m3fn_x4
 FP4X4 = mybir.dt.float4_e2m1fn_x4
 MAX = mybir.AluOpType.max
 RELU = mybir.ActivationFunctionType.Relu
-COPY = mybir.ActivationFunctionType.Copy
 
-NARROW = ((0, 0), (0, 1), (1, 0), (4, 0), (7, 0), (7, 1))
-FIRST_SECOND = 2
-LATE = 16
-HOLD_UNTIL = 18
-NPE = 4
-X2FIRST = 0
-X1E = "VV"
-X2E = "VVSS"
-WH = 2
-XQ0 = 0
-T1AT = 12
+SHARE = True
 WARM = 5
 WARM2 = 1
-SORT = ()
-SORTE = "V"
-TLEAD = 4
-X4E = "SS"
-XE = "VVVS"
+XE = "SVVVVVSS"
 EV = (0,)
-ZE = "VVVSVSVSVSS"
-END = ((0, 256), (256, 256), (512, 256), (768, 256))
-PICK_LEAD = 6
-SPLIT_LEAD = 7
-TWICE = (4,)
-SPLIT_ON_VECTOR = (4,)
+T1AT = 12
+W0AT = 0
+FIRST_SECOND = 1
+LATE = 6
+SPLIT_LEAD = 6
+TURN_LEAD = 4
+JOIN_LEAD = 3
+QUANT_LEAD = 2
+SE = "VSSS"
+JE = "SSSS"
+LAST_OUT = "V"
+STORE_PIECE = 256
 
 
 def tile_pointnet_set_encoder_s12_kernel(tc, x, w, u_words, u_scales, v_words, v_scales, out):
@@ -51,8 +42,7 @@ def tile_pointnet_set_encoder_s12_kernel(tc, x, w, u_words, u_scales, v_words, v
         ctx.enter_context(tc.manual_schedule())
 
         def sb(shape, dtype, tag, bufs=1):
-            t = keep.tile(shape, dtype, name=tag, tag=tag, bufs=bufs, align_bytes=256)
-            return t
+            return keep.tile(shape, dtype, name=tag, tag=tag, bufs=bufs, align_bytes=256)
 
         banks = {}
 
@@ -69,7 +59,8 @@ def tile_pointnet_set_encoder_s12_kernel(tc, x, w, u_words, u_scales, v_words, v
         v_w = sb([128, 2048], U8, "v_w")
         v_pl = sb([128, 1024], U8, "v_pl")
         ident = sb([128, 128], F32, "ident")
-        x_sb = [sb([128, 2048], BF16, "x_sb%d" % q) for q in range(NPE)]
+        x_sb = [sb([128, 2048], BF16, "x_sb%d" % q) for q in range(4)]
+        x_quad = [sb([128, 2, 16, 128], BF16, "x_quad%d" % r) for r in range(2)]
         x_c = [sb([128, 512], U32, "x_c%d" % q) for q in range(8)]
         x_s = [sb([128, 512], U8, "x_s%d" % q) for q in range(8)]
         w_raw = {k: sb([128, 4, 512], BF16, "w_raw%d%d" % k) for k in quarters}
@@ -86,34 +77,17 @@ def tile_pointnet_set_encoder_s12_kernel(tc, x, w, u_words, u_scales, v_words, v
         us32 = u_scales[0].bitcast(I32)
         vs32 = v_scales[0].bitcast(I32)
         x_rows = x.rearrange("(s i b) k -> s i b k", s=2, i=128, b=8)
+        x_rows_quad = x.rearrange("(s i m r) k -> s r i m k", s=2, i=32, r=2)[1]
         w_rows = w.rearrange("(g p j) f -> g p j f", g=2, p=128, j=4)
 
         def load_x(q):
-            points = slice(2 * q, 2 * q + 2) if q < 4 else slice(q - 4, 8, 4)
-            nc.sync.dma_start(out=x_sb[q][:].rearrange("p (b k) -> p b k", b=2), in_=x_rows[q // 4][:, points, :])
+            nc.sync.dma_start(out=x_sb[q][:].rearrange("p (b k) -> p b k", b=2), in_=x_rows[0][:, 2 * q : 2 * q + 2, :])
 
-        x_d = {}
-
-        def load_x_twice(q):
-            t = sb([128, 2, 16, 128], BF16, "x_d%d" % q)
-            rows = x.rearrange("(s i m r) k -> s r i m k", s=2, i=16, r=4)[1, q - 4]
-            for g in range(2):
-                for u in range(2):
-                    for Q in (0, 2, 1, 3):
-                        k0 = 512 * g + 128 * Q + 2 * u
-                        n = min(128, 1024 - k0)
-                        nc.sync.dma_start(out=t[32 * Q + u : 32 * Q + 32 : 2, g, :, 0:n], in_=rows[:, :, k0 : k0 + n])
-            x_d[q] = t[:].bitcast(F32).rearrange("p g (c b) (j u) -> p g c b j u", b=2, u=2)[:, :, :, :, :, 0]
-
-        def load_x_once(q0, n, r):
-            t = sb([128, 2, 8 * n, 128], BF16, "x_d%d" % q0)
-            rows = x.rearrange("(s i m r) k -> s r i m k", s=2, i=32, r=4 // n)[1, r]
+        def load_x_quad(r):
             for g in range(2):
                 for Q in (0, 2, 1, 3):
                     k0 = 512 * g + 128 * Q
-                    nc.sync.dma_start(out=t[32 * Q : 32 * Q + 32, g], in_=rows[:, :, k0 : k0 + 128])
-            for a in range(n):
-                x_d[q0 + a] = t[:].bitcast(F32).rearrange("p g (c a b) (j u) -> p a (g c) b u j", a=n, b=2, u=2)[:, a]
+                    nc.sync.dma_start(out=x_quad[r][32 * Q : 32 * Q + 32, g], in_=x_rows_quad[r][:, :, k0 : k0 + 128])
 
         def load_w(g, G):
             nc.sync.dma_start(out=w_raw[g, G][:], in_=w_rows[g][:, :, 512 * G : 512 * G + 512])
@@ -139,27 +113,31 @@ def tile_pointnet_set_encoder_s12_kernel(tc, x, w, u_words, u_scales, v_words, v
                 in_=u_pl_raw[:].bitcast(I32).rearrange("p (G q t) -> p G t q", G=2, q=32, t=4),
             )
 
-        def w_weave(g, G, t0=0, n=4, engine="V"):
-            copy(
-                engine,
-                w_grp[g, G][:].rearrange("p (t q r j) -> p t q j r", t=4, q=32, r=4, j=4)[:, t0 : t0 + n],
-                w_raw[g, G][:].rearrange("p j (q t r) -> p t q j r", q=32, t=4, r=4)[:, t0 : t0 + n],
+        def w_weave(g, G, t0=0, n=4):
+            nc.vector.tensor_copy(
+                out=w_grp[g, G][:].rearrange("p (t q r j) -> p t q j r", t=4, q=32, r=4, j=4)[:, t0 : t0 + n],
+                in_=w_raw[g, G][:].rearrange("p j (q t r) -> p t q j r", q=32, t=4, r=4)[:, t0 : t0 + n],
             )
 
-        def w_quant(g, G, t0=0, n=4):
+        def quantize(codes, scales, values, c0=0, n=512):
             nc.vector.quantize_mx(
-                out=w_c[g, G][:, 128 * t0 : 128 * (t0 + n)].bitcast(FP8X4),
-                scales=w_s[g, G][:, 128 * t0 : 128 * (t0 + n)],
-                in_=w_grp[g, G][:, 512 * t0 : 512 * (t0 + n)],
+                out=codes[:, c0 : c0 + n].bitcast(FP8X4), scales=scales[:, c0 : c0 + n], in_=values[:, 4 * c0 : 4 * (c0 + n)]
             )
 
-        def e_mm(k):
-            G, nb = k // 4 % 2, k % 4 + k // 8 * 4
-            e = bank(("e", k), [128, 4, 128])
-            for t in range(4):
+        def w_quant(g, G):
+            quantize(w_c[g, G], w_s[g, G], w_grp[g, G])
+
+        def e_quant(G, nh):
+            quantize(e_c[G, nh], e_s[G, nh], e_grp[G, nh])
+
+        def e_mm(ks):
+            for k in ks:
+                bank(("e", k), [128, 4, 128])
+            for t, k in [(t, k) for t in range(4) for k in ks] if SHARE else [(t, k) for k in ks for t in range(4)]:
+                G, nb = k // 4 % 2, k % 4 + k // 8 * 4
                 c0 = G * 512 + t * 128
                 nc.tensor.matmul_mx(
-                    out=e[:, t, :],
+                    out=banks["e", k][:, t, :],
                     lhsT=u_w[:, 2 * c0 : 2 * c0 + 256].bitcast(FP4X4), lhsT_scale=u_pl[:, c0 : c0 + 128],
                     rhs=v_w[:, 256 * nb : 256 * nb + 256].bitcast(FP4X4), rhs_scale=v_pl[:, 128 * nb : 128 * nb + 128],
                     start=t == 0, stop=t == 3,
@@ -173,158 +151,87 @@ def tile_pointnet_set_encoder_s12_kernel(tc, x, w, u_words, u_scales, v_words, v
                 banks["e", k][:].rearrange("p t n -> p n t"),
             )
 
-        def e_quant(G, nh):
-            nc.vector.quantize_mx(out=e_c[G, nh][:].bitcast(FP8X4), scales=e_s[G, nh][:], in_=e_grp[G, nh][:])
-
         x_g = {}
         x_r = {}
+        x_t = {}
 
-        def x_transpose(q, b):
-            xt = bank(("x", q, b), [128, 2, 2, 128])
-            for g in range(2):
-                base = b * 512 + g * 256
-                for u in range(2):
-                    if q in SORT:
-                        words = x_r[q][:, base + 128 * u : base + 128 * u + 128]
-                    else:
-                        words = x_sb[q][:].bitcast(F32)[:, base + u : base + 256 : 2]
-                    nc.tensor.transpose(xt[:, g, u, :], words, ident[:])
+        def x_transpose(q):
+            for b in range(2):
+                xt = bank(("x", q, b), [128, 2, 2, 128])
+                for g in range(2):
+                    base = b * 512 + g * 256
+                    for u in range(2):
+                        nc.tensor.transpose(xt[:, g, u, :], x_sb[q][:].bitcast(F32)[:, base + u : base + 256 : 2], ident[:])
 
         def x_out(q, b, engine):
             if q not in x_g:
                 x_g[q] = sb([128, 2048], BF16, "x_g", 3)
-            dst = x_g[q][:].bitcast(F32).rearrange("p (g b n u) -> p b g n u", g=2, b=2, u=2)[:, b]
-            if engine == "A":
-                nc.scalar.activation(
-                    out=x_g[q][:, 0:512].rearrange("p (n u e) -> p n u e", u=2, e=2),
-                    in_=banks["x", q, b][:, 0].bitcast(BF16).rearrange("p u (n e) -> p n u e", e=2),
-                    func=COPY,
-                )
-                nc.scalar.copy(dst[:, 1], banks["x", q, b][:, 1].rearrange("p u n -> p n u"))
-                return
-            copy(engine, dst, banks["x", q, b][:].rearrange("p g u n -> p g n u"))
-
-        def x_sort(q, engine):
-            x_r[q] = sb([128, 1024], F32, "x_r", 2)
             copy(
                 engine,
-                x_r[q][:].rearrange("p (a u w) -> p a u w", u=2, w=128),
-                x_sb[q][:].bitcast(F32).rearrange("p (a w u) -> p a u w", u=2, w=128),
+                x_g[q][:].bitcast(F32).rearrange("p (g b n u) -> p b g n u", g=2, b=2, u=2)[:, b],
+                banks["x", q, b][:].rearrange("p g u n -> p g n u"),
             )
 
-        def x_pick(q):
+        def x_split(q, engine):
             x_r[q] = sb([128, 1024], F32, "x_r", 2)
-            if q not in TWICE:
-                copy("V" if q in SPLIT_ON_VECTOR else "S", x_r[q][:].rearrange("p (a b u j) -> p a b u j", b=2, u=2, j=32), x_d[q])
-            elif q == 7:
-                for g in (1, 0):
-                    copy(
-                        "V" if q in SPLIT_ON_VECTOR else "S",
-                        x_r[q][:, 512 * g : 512 * g + 512].rearrange("p (b c j) -> p b c j", b=2, c=8),
-                        x_d[q][:, g].rearrange("p c b j -> p b c j"),
-                    )
-            else:
-                copy("V" if q in SPLIT_ON_VECTOR else "S", x_r[q][:].rearrange("p (g c b j) -> p g c b j", g=2, c=8, b=2), x_d[q])
-
-        x_t = {}
+            words = x_quad[q // 2 - 2][:].bitcast(F32).rearrange("p g (c a b) (j u) -> p a (g c) b u j", a=2, b=2, u=2)
+            copy(engine, x_r[q][:].rearrange("p (a b u j) -> p a b u j", b=2, u=2, j=32), words[:, q % 2])
 
         def x_turn(q):
-            if q in TWICE:
-                x_g[q] = sb([128, 2048], BF16, "x_g", 3)
-                nc.vector.transpose(x_g[q][:].bitcast(F32), x_r[q][:])
-            else:
-                x_t[q] = sb([128, 1024], F32, "x_t", 2)
-                nc.vector.transpose(x_t[q][:], x_r[q][:])
+            x_t[q] = sb([128, 1024], F32, "x_t", 2)
+            nc.vector.transpose(x_t[q][:], x_r[q][:])
 
-        def x_join(q):
-            if q not in TWICE:
-                x_g[q] = sb([128, 2048], BF16, "x_g", 3)
-                if q < 7:
-                    nc.scalar.copy(
-                        x_g[q][:].bitcast(F32).rearrange("p (a i u) -> p a i u", u=2, i=32),
-                        x_t[q][:].rearrange("p (a u i) -> p a i u", u=2, i=32),
-                    )
-                else:
-                    for g in range(2):
-                        nc.scalar.copy(
-                            x_g[q][:, 1024 * g : 1024 * g + 1024].bitcast(F32).rearrange("p (b c i u) -> p b c i u", b=2, u=2, i=32),
-                            x_t[q][:].rearrange("p (g c b u i) -> p g b c i u", g=2, b=2, u=2, i=32)[:, g],
-                        )
-
-        def x_quant(q):
-            nc.vector.quantize_mx(out=x_c[q][:].bitcast(FP8X4), scales=x_s[q][:], in_=x_g[q][:])
-
-        h_t = {}
-        h_half = {}
-
-        def wide(q, G):
-            return (q, G) not in NARROW
-
-        def part(q, b, G):
-            return 2 * b + G if q == 7 else 2 * G + b
-
-        def h_tile(q):
-            if q not in h_t:
-                h_t[q] = sb([128, 2048], BF16, "h_t", 4)
-            return h_t[q]
-
-        def first(q, G, j):
-            n = 256 if wide(q, G) else 128
-            h = bank(("h", q, G, j), [128, 512 // n, n])
-            for tt in range(512 // n):
-                t = 2 * j + tt if n == 256 else tt
-                for g in range(2):
-                    k0 = 256 * g if n == 256 else 256 * g + 128 * j
-                    nc.tensor.matmul_mx(
-                        out=h[:, tt, :],
-                        lhsT=w_c[g, G][:, 128 * t : 128 * t + 128].bitcast(FP8X4),
-                        lhsT_scale=w_s[g, G][:, 128 * t : 128 * t + 128],
-                        rhs=x_c[q][:, k0 : k0 + n].bitcast(FP8X4), rhs_scale=x_s[q][:, k0 : k0 + n],
-                        start=g == 0, stop=g == 1,
-                    )
-
-        def h_out(q, G, j):
-            src = banks["h", q, G, j][:]
-            blocks = 8 if q in TWICE else 4
-            if wide(q, G):
-                if j == 0:
-                    h_half[q, G] = sb([128, 2, 512], BF16, "h_half", 3)
-                dst = h_half[q, G][:, j, :]
-                if q < NPE:
-                    dst, src = dst.rearrange("p (n e) -> p n e", e=2), src.rearrange("p e n -> p n e")
-                else:
-                    dst, src = dst.rearrange("p (a c e) -> p a c e", c=blocks, e=2), src.rearrange("p e (c a) -> p a c e", c=blocks)
-            else:
-                dst = h_tile(q)[:, 512 * part(q, j, G) : 512 * part(q, j, G) + 512]
-                if q < NPE:
-                    dst, src = dst.rearrange("p (n t) -> p n t", t=4), src.rearrange("p t n -> p n t")
-                elif q == 7:
-                    dst, src = dst.rearrange("p (i c t) -> p i c t", c=blocks, t=4), src.rearrange("p t (c i) -> p i c t", c=blocks)
-                else:
-                    dst = h_tile(q)[:, 1024 * G : 1024 * G + 1024].rearrange("p (a j c t) -> p j a c t", j=2, c=blocks // 2, t=4)[:, j]
-                    src = src.rearrange("p t (c a) -> p a c t", c=blocks // 2)
-            nc.scalar.activation(out=dst, in_=src, func=RELU)
-
-        def h_zip(q, G, engine):
-            if wide(q, G):
-                copy(
-                    engine,
-                    h_tile(q)[:, 1024 * G : 1024 * G + 1024].bitcast(F32).rearrange("p (n i u) -> p n u i", i=2, u=2),
-                    h_half[q, G][:].bitcast(F32).rearrange("p u (n i) -> p n u i", i=2),
-                )
-
-        def h_quant(q, j0=0, n=4):
-            nc.vector.quantize_mx(
-                out=h_c[q][:, 128 * j0 : 128 * (j0 + n)].bitcast(FP8X4),
-                scales=h_s[q][:, 128 * j0 : 128 * (j0 + n)],
-                in_=h_t[q][:, 512 * j0 : 512 * (j0 + n)],
+        def x_join(q, engine):
+            x_g[q] = sb([128, 2048], BF16, "x_g", 3)
+            copy(
+                engine,
+                x_g[q][:].bitcast(F32).rearrange("p (a i u) -> p a i u", u=2, i=32),
+                x_t[q][:].rearrange("p (a u i) -> p a i u", u=2, i=32),
             )
 
-        def mm2(m, n0, n=512):
+        def x_quant(q):
+            quantize(x_c[q], x_s[q], x_g[q])
+
+        h_t = {}
+
+        def first(q, G):
+            for j in range(2):
+                bank(("h", q, G, j), [128, 4, 128])
+            passes = [(t, g, j) for t in range(4) for g in range(2) for j in range(2)]
+            for t, g, j in passes if SHARE else sorted(passes, key=lambda a: a[2]):
+                k0 = 256 * g + 128 * j
+                nc.tensor.matmul_mx(
+                    out=banks["h", q, G, j][:, t, :],
+                    lhsT=w_c[g, G][:, 128 * t : 128 * t + 128].bitcast(FP8X4),
+                    lhsT_scale=w_s[g, G][:, 128 * t : 128 * t + 128],
+                    rhs=x_c[q][:, k0 : k0 + 128].bitcast(FP8X4), rhs_scale=x_s[q][:, k0 : k0 + 128],
+                    start=g == 0, stop=g == 1,
+                )
+
+        def h_out(q, G, j, engine="S"):
+            if q not in h_t:
+                h_t[q] = sb([128, 2048], BF16, "h_t", 4)
+            src = banks["h", q, G, j][:]
+            half = h_t[q][:, 1024 * G : 1024 * G + 1024]
+            if q < 4:
+                dst = half.rearrange("p (j n t) -> p j n t", j=2, t=4)[:, j]
+                src = src.rearrange("p t n -> p n t")
+            else:
+                dst = half.rearrange("p (a j c t) -> p j a c t", j=2, c=2, t=4)[:, j]
+                src = src.rearrange("p t (c a) -> p a c t", c=2)
+            if engine == "S":
+                nc.scalar.activation(out=dst, in_=src, func=RELU)
+            else:
+                nc.vector.tensor_scalar(out=dst, in0=src, scalar1=0.0, scalar2=None, op0=MAX)
+
+        def h_quant(q, c0=0, n=512):
+            quantize(h_c[q], h_s[q], h_t[q], c0, n)
+
+        def second(m, n0, n=512):
             y = bank(("y", m, n0), [128, n])
             nh, j0 = n0 // 512, n0 % 512
             for G in range(2):
-                k = slice(128 * part(m // 2, m % 2, G), 128 * part(m // 2, m % 2, G) + 128)
+                k = slice(256 * G + 128 * (m % 2), 256 * G + 128 * (m % 2) + 128)
                 nc.tensor.matmul_mx(
                     out=y[:],
                     lhsT=h_c[m // 2][:, k].bitcast(FP8X4), lhsT_scale=h_s[m // 2][:, k],
@@ -360,129 +267,105 @@ def tile_pointnet_set_encoder_s12_kernel(tc, x, w, u_words, u_scales, v_words, v
         load_w(1, 0)
         load_x(1)
         load_w(0, 1)
-        if X2FIRST:
-            load_x(2)
         load_w(1, 1)
-        if not X2FIRST:
-            load_x(2)
+        load_x(2)
         load_x(3)
-        load_x_twice(4)
-        load_x_once(5, 1, 2)
-        load_x_once(6, 2, 1)
+        load_x_quad(0)
+        load_x_quad(1)
 
-        if WARM:
-            zero = sb([128, 512], BF16, "zero")
-            nc.vector.memset(zero[:].bitcast(I32), 0)
-            warm = bank("warm", [128, 512])
-            for i in range(WARM):
-                nc.tensor.matmul(warm[:], lhsT=zero[:, 0:128], rhs=zero[:], start=True, stop=True)
-        for b in range(2):
-            x_transpose(0, b)
+        zero = sb([128, 512], BF16, "zero")
+        nc.vector.memset(zero[:].bitcast(I32), 0)
+        warm = bank("warm", [128, 512])
+        for i in range(WARM):
+            nc.tensor.matmul(warm[:], lhsT=zero[:, 0:128], rhs=zero[:], start=True, stop=True)
+        x_transpose(0)
         for i in range(WARM2):
             nc.tensor.matmul(warm[:], lhsT=zero[:, 0:128], rhs=zero[:], start=True, stop=True)
         permute_u()
         permute_u_scales()
-        x_out(0, 0, "A")
-        x_out(0, 1, "V")
-        for k in range(16):
+        x_out(0, 0, XE[0])
+        x_out(0, 1, XE[1])
+        for k in range(0, 16, 2):
             if k == T1AT:
-                for b in range(2):
-                    x_transpose(1, b)
-            e_mm(k)
+                x_transpose(1)
+            e_mm((k, k + 1))
             e_out(k, "V" if k in EV else "S")
-            if k == XQ0:
+            e_out(k + 1, "V" if k + 1 in EV else "S")
+            if k == W0AT:
                 x_quant(0)
-            if k == max(EV):
                 w_weave(0, 0)
                 w_weave(1, 0)
                 w_quant(0, 0)
                 w_quant(1, 0)
             if k == T1AT:
-                x_out(1, 0, X1E[0])
-                x_out(1, 1, X1E[1])
-        w_weave(0, 1, 0, WH)
+                x_out(1, 0, XE[2])
+                x_out(1, 1, XE[3])
+        w_weave(0, 1, 0, 2)
         x_quant(1)
-        w_weave(0, 1, WH, 4 - WH)
+        w_weave(0, 1, 2, 2)
         w_weave(1, 1)
         w_quant(0, 1)
         w_quant(1, 1)
         for q in range(2):
-            for j in range(2):
-                first(q, 0, j)
-                h_out(q, 0, j)
+            first(q, 0)
+            h_out(q, 0, 0)
+            h_out(q, 0, 1)
         for q in range(2, 4):
-            for b in range(2):
-                x_transpose(q, b)
-                x_out(q, b, X2E[2 * q + b - 4])
+            x_transpose(q)
+            x_out(q, 0, XE[2 * q])
+            x_out(q, 1, XE[2 * q + 1])
         e_quant(0, 0)
         x_quant(2)
         for q in range(2):
-            for j in range(2):
-                first(q, 1, j)
-                h_out(q, 1, j)
+            first(q, 1)
+            h_out(q, 1, 0)
+            h_out(q, 1, 1)
+        if SE[0] == "S":
+            x_split(4, "S")
         e_quant(1, 0)
         x_quant(3)
         h_quant(0)
+        if SE[0] == "V":
+            x_split(4, "V")
         e_quant(0, 1)
-        h_zip(1, 1, ZE[0])
         e_quant(1, 1)
-        h_quant(1)
 
         todo = [(m, 0) for m in range(2)] + [(m, 512) for m in range(2)] + [(m, n0) for m in range(2, 15) for n0 in (0, 512)]
-        waiting = []
 
-        def second():
-            mm2(*todo[0])
-            waiting.append(todo.pop(0))
+        def due(step, lead):
+            return [q for q in range(4, 8) if step + lead == 2 * (q - 2)]
 
-        def drain(keep_back):
-            while len(waiting) > keep_back or (waiting and waiting[0][0] % 8 == 0):
-                y_out(*waiting.pop(0))
-
-        def due(slot, lead_twice, lead_once):
-            return [q for q in range(NPE, 8) if slot + (lead_twice if q in TWICE else lead_once) == 4 * (q - 2)]
-
-        slots = [(q, G, j) for q in range(2, 7) for G in range(2) for j in range(2)]
-        slots = slots + [(7, G, j) for j in range(2) for G in range(2)]
-        for slot, (q, G, j) in enumerate(slots):
-            turn = [p for p in range(4, NPE) if slot + TLEAD == 4 * (p - 2)]
-            for p in turn:
-                for b in range(2):
-                    x_transpose(p, b)
-            first(q, G, j)
-            if slot >= FIRST_SECOND:
-                second()
-            if slot >= LATE and slot % 2 == 1:
-                second()
-            for p in turn:
-                for b in range(2):
-                    x_out(p, b, X4E[b])
-            h_out(q, G, j)
-            for p in due(slot, PICK_LEAD, SPLIT_LEAD):
-                x_pick(p)
-            for p in due(slot, 4, 4):
-                x_join(p)
-            drain(1 if slot < HOLD_UNTIL else 0)
-            if slot % 2 == 0 and 0 < slot <= 20:
-                h_zip(*slots[slot - 1][:2], ZE[slot // 2])
-            for p in due(slot, PICK_LEAD - 1, SPLIT_LEAD - 1):
-                x_turn(p)
-            for p in due(slot, 3, 3):
-                x_quant(p)
-            for p in range(4, NPE):
-                if slot + TLEAD - 1 == 4 * (p - 2):
-                    x_quant(p)
-                if slot + TLEAD + 2 == 4 * (p - 2) and p in SORT:
-                    x_sort(p, SORTE)
-            if slot % 4 == 1 and slot >= 4:
+        for step in range(12):
+            q, G = 2 + step // 2, step % 2
+            first(q, G)
+            now = [todo.pop(0) for i in range(0 if step < FIRST_SECOND else 2 if step < LATE else 3)]
+            if G == 0:
                 h_quant(q - 1)
-            if slot == 22:
-                h_quant(7, 0, 2)
-                h_quant(7, 2, 1)
-        h_quant(7, 3, 1)
-        while todo:
-            second()
-            drain(0)
-        for n0, n in END:
-            mm2(15, n0, n)
-            y_out(15, n0, n)
+            for y in now:
+                second(*y)
+            for p in due(step, QUANT_LEAD):
+                x_quant(p)
+            last = step == 11
+            if last:
+                h_quant(7, 0, 256)
+            h_out(q, G, 0)
+            h_out(q, G, 1, LAST_OUT if last else "S")
+            for y in now[:1]:
+                y_out(*y)
+            for p in due(step, TURN_LEAD):
+                x_turn(p)
+            if last:
+                h_quant(7, 256, 256)
+            for y in now[1:]:
+                y_out(*y)
+            for p in due(step, JOIN_LEAD):
+                x_join(p, JE[p - 4])
+            for p in due(step, SPLIT_LEAD):
+                if p > 4:
+                    x_split(p, SE[p - 4])
+        for y in todo:
+            second(*y)
+            y_out(*y)
+        for n0 in range(0, 1024, STORE_PIECE):
+            second(15, n0, STORE_PIECE)
+            y_out(15, n0, STORE_PIECE)

@@ -24,11 +24,11 @@ T1AT = 12
 W0AT = 0
 FIRST_SECOND = 1
 LATE = 6
-SPLIT_LEAD = 6
+SPLIT_LEAD = 5
 TURN_LEAD = 4
 JOIN_LEAD = 3
 QUANT_LEAD = 2
-SE = "VSSS"
+SE = "VVSS"
 JE = "SSSS"
 LAST_OUT = "V"
 STORE_PIECE = 256
@@ -60,7 +60,6 @@ def tile_pointnet_set_encoder_s12_kernel(tc, x, w, u_words, u_scales, v_words, v
         v_pl = sb([128, 1024], U8, "v_pl")
         ident = sb([128, 128], F32, "ident")
         x_sb = [sb([128, 2048], BF16, "x_sb%d" % q) for q in range(4)]
-        x_quad = [sb([128, 2, 16, 128], BF16, "x_quad%d" % r) for r in range(2)]
         x_c = [sb([128, 512], U32, "x_c%d" % q) for q in range(8)]
         x_s = [sb([128, 512], U8, "x_s%d" % q) for q in range(8)]
         w_raw = {k: sb([128, 4, 512], BF16, "w_raw%d%d" % k) for k in quarters}
@@ -77,17 +76,22 @@ def tile_pointnet_set_encoder_s12_kernel(tc, x, w, u_words, u_scales, v_words, v
         us32 = u_scales[0].bitcast(I32)
         vs32 = v_scales[0].bitcast(I32)
         x_rows = x.rearrange("(s i b) k -> s i b k", s=2, i=128, b=8)
-        x_rows_quad = x.rearrange("(s i m r) k -> s r i m k", s=2, i=32, r=2)[1]
         w_rows = w.rearrange("(g p j) f -> g p j f", g=2, p=128, j=4)
 
         def load_x(q):
             nc.sync.dma_start(out=x_sb[q][:].rearrange("p (b k) -> p b k", b=2), in_=x_rows[0][:, 2 * q : 2 * q + 2, :])
 
-        def load_x_quad(r):
+        x_words = {}
+
+        def load_x_quad(q0, n, r):
+            t = sb([128, 2, 8 * n, 128], BF16, "x_quad%d" % q0)
+            rows = x.rearrange("(s i m r) k -> s r i m k", s=2, i=32, r=4 // n)[1, r]
             for g in range(2):
                 for Q in (0, 2, 1, 3):
                     k0 = 512 * g + 128 * Q
-                    nc.sync.dma_start(out=x_quad[r][32 * Q : 32 * Q + 32, g], in_=x_rows_quad[r][:, :, k0 : k0 + 128])
+                    nc.sync.dma_start(out=t[32 * Q : 32 * Q + 32, g], in_=rows[:, :, k0 : k0 + 128])
+            for a in range(n):
+                x_words[q0 + a] = t[:].bitcast(F32).rearrange("p g (c a b) (j u) -> p a (g c) b u j", a=n, b=2, u=2)[:, a]
 
         def load_w(g, G):
             nc.sync.dma_start(out=w_raw[g, G][:], in_=w_rows[g][:, :, 512 * G : 512 * G + 512])
@@ -174,8 +178,7 @@ def tile_pointnet_set_encoder_s12_kernel(tc, x, w, u_words, u_scales, v_words, v
 
         def x_split(q, engine):
             x_r[q] = sb([128, 1024], F32, "x_r", 2)
-            words = x_quad[q // 2 - 2][:].bitcast(F32).rearrange("p g (c a b) (j u) -> p a (g c) b u j", a=2, b=2, u=2)
-            copy(engine, x_r[q][:].rearrange("p (a b u j) -> p a b u j", b=2, u=2, j=32), words[:, q % 2])
+            copy(engine, x_r[q][:].rearrange("p (a b u j) -> p a b u j", b=2, u=2, j=32), x_words[q])
 
         def x_turn(q):
             x_t[q] = sb([128, 1024], F32, "x_t", 2)
@@ -270,8 +273,8 @@ def tile_pointnet_set_encoder_s12_kernel(tc, x, w, u_words, u_scales, v_words, v
         load_w(1, 1)
         load_x(2)
         load_x(3)
-        load_x_quad(0)
-        load_x_quad(1)
+        for q in range(4, 8):
+            load_x_quad(q, 1, q - 4)
 
         zero = sb([128, 512], BF16, "zero")
         nc.vector.memset(zero[:].bitcast(I32), 0)

@@ -15,23 +15,27 @@ FP4X4 = mybir.dt.float4_e2m1fn_x4
 MAX = mybir.AluOpType.max
 RELU = mybir.ActivationFunctionType.Relu
 
-SHARE = True
+NPE = 4
+NARROW = ((0, 0), (0, 1), (1, 0), (1, 1), (3, 1), (4, 0), (7, 0), (7, 1))
 WARM = 5
-WARM2 = 1
-XE = "SVVVVVSS"
-EV = (0,)
-T1AT = 12
+XE = "VSVVVSSS"
+EV = ()
 W0AT = 0
-FIRST_SECOND = 1
-LATE = 6
-SPLIT_LEAD = 5
-TURN_LEAD = 4
-JOIN_LEAD = 3
-QUANT_LEAD = 2
+FIRST_SECOND = 2
+LATE = 16
+HOLD_UNTIL = 18
+SPLIT_LEAD = 7
+TURN_LEAD = 6
+JOIN_LEAD = 4
+QUANT_LEAD = 3
 SE = "VVSS"
 JE = "SSSS"
-LAST_OUT = "V"
+ZE = "VVSVVVSSSS"
 STORE_PIECE = 256
+WARM2 = 1
+T1AT = 12
+XQ0 = 0
+EXTRA = 0
 
 
 def tile_pointnet_set_encoder_s12_kernel(tc, x, w, u_words, u_scales, v_words, v_scales, out):
@@ -111,10 +115,10 @@ def tile_pointnet_set_encoder_s12_kernel(tc, x, w, u_words, u_scales, v_words, v
                 in_=u_raw[:].bitcast(I32).rearrange("p (G q t r) -> p G t q r", G=2, q=32, t=4, r=2),
             )
 
-        def permute_u_scales():
+        def permute_u_scales(Q):
             nc.vector.tensor_copy(
-                out=u_pl[:].bitcast(I32).rearrange("p (G t q) -> p G t q", G=2, t=4, q=32),
-                in_=u_pl_raw[:].bitcast(I32).rearrange("p (G q t) -> p G t q", G=2, q=32, t=4),
+                out=u_pl[32 * Q : 32 * Q + 4, :].bitcast(I32).rearrange("p (G t q) -> p G t q", G=2, t=4, q=32),
+                in_=u_pl_raw[32 * Q : 32 * Q + 4, :].bitcast(I32).rearrange("p (G q t) -> p G t q", G=2, q=32, t=4),
             )
 
         def w_weave(g, G, t0=0, n=4):
@@ -134,11 +138,10 @@ def tile_pointnet_set_encoder_s12_kernel(tc, x, w, u_words, u_scales, v_words, v
         def e_quant(G, nh):
             quantize(e_c[G, nh], e_s[G, nh], e_grp[G, nh])
 
-        def e_mm(ks):
-            for k in ks:
-                bank(("e", k), [128, 4, 128])
-            for t, k in [(t, k) for t in range(4) for k in ks] if SHARE else [(t, k) for k in ks for t in range(4)]:
-                G, nb = k // 4 % 2, k % 4 + k // 8 * 4
+        def e_mm(k):
+            G, nb = k // 4 % 2, k % 4 + k // 8 * 4
+            bank(("e", k), [128, 4, 128])
+            for t in range(4):
                 c0 = G * 512 + t * 128
                 nc.tensor.matmul_mx(
                     out=banks["e", k][:, t, :],
@@ -186,46 +189,80 @@ def tile_pointnet_set_encoder_s12_kernel(tc, x, w, u_words, u_scales, v_words, v
 
         def x_join(q, engine):
             x_g[q] = sb([128, 2048], BF16, "x_g", 3)
-            copy(
-                engine,
-                x_g[q][:].bitcast(F32).rearrange("p (a i u) -> p a i u", u=2, i=32),
-                x_t[q][:].rearrange("p (a u i) -> p a i u", u=2, i=32),
-            )
+            if q < 7:
+                copy(
+                    engine,
+                    x_g[q][:].bitcast(F32).rearrange("p (a i u) -> p a i u", u=2, i=32),
+                    x_t[q][:].rearrange("p (a u i) -> p a i u", u=2, i=32),
+                )
+            else:
+                for g in range(2):
+                    copy(
+                        engine,
+                        x_g[q][:].bitcast(F32).rearrange("p (g b c i u) -> p g b c i u", g=2, b=2, u=2, i=32)[:, g],
+                        x_t[q][:].rearrange("p (g c b u i) -> p g b c i u", g=2, b=2, u=2, i=32)[:, g],
+                    )
 
         def x_quant(q):
             quantize(x_c[q], x_s[q], x_g[q])
 
         h_t = {}
+        h_half = {}
 
-        def first(q, G):
-            for j in range(2):
-                bank(("h", q, G, j), [128, 4, 128])
-            passes = [(t, g, j) for t in range(4) for g in range(2) for j in range(2)]
-            for t, g, j in passes if SHARE else sorted(passes, key=lambda a: a[2]):
-                k0 = 256 * g + 128 * j
-                nc.tensor.matmul_mx(
-                    out=banks["h", q, G, j][:, t, :],
-                    lhsT=w_c[g, G][:, 128 * t : 128 * t + 128].bitcast(FP8X4),
-                    lhsT_scale=w_s[g, G][:, 128 * t : 128 * t + 128],
-                    rhs=x_c[q][:, k0 : k0 + 128].bitcast(FP8X4), rhs_scale=x_s[q][:, k0 : k0 + 128],
-                    start=g == 0, stop=g == 1,
-                )
+        def wide(q, G):
+            return (q, G) not in NARROW
 
-        def h_out(q, G, j, engine="S"):
+        def part(q, b, G):
+            return 2 * b + G if q == 7 else 2 * G + b
+
+        def h_tile(q):
             if q not in h_t:
                 h_t[q] = sb([128, 2048], BF16, "h_t", 4)
+            return h_t[q]
+
+        def first(q, G, j):
+            n = 256 if wide(q, G) else 128
+            h = bank(("h", q, G, j), [128, 512 // n, n])
+            for tt in range(512 // n):
+                t = 2 * j + tt if n == 256 else tt
+                for g in range(2):
+                    k0 = 256 * g if n == 256 else 256 * g + 128 * j
+                    nc.tensor.matmul_mx(
+                        out=h[:, tt, :],
+                        lhsT=w_c[g, G][:, 128 * t : 128 * t + 128].bitcast(FP8X4),
+                        lhsT_scale=w_s[g, G][:, 128 * t : 128 * t + 128],
+                        rhs=x_c[q][:, k0 : k0 + n].bitcast(FP8X4), rhs_scale=x_s[q][:, k0 : k0 + n],
+                        start=g == 0, stop=g == 1,
+                    )
+
+        def h_out(q, G, j):
             src = banks["h", q, G, j][:]
-            half = h_t[q][:, 1024 * G : 1024 * G + 1024]
-            if q < 4:
-                dst = half.rearrange("p (j n t) -> p j n t", j=2, t=4)[:, j]
-                src = src.rearrange("p t n -> p n t")
+            if wide(q, G):
+                if j == 0:
+                    h_half[q, G] = sb([128, 2, 512], BF16, "h_half", 3)
+                dst = h_half[q, G][:, j, :]
+                if q < NPE:
+                    dst, src = dst.rearrange("p (n e) -> p n e", e=2), src.rearrange("p e n -> p n e")
+                else:
+                    dst, src = dst.rearrange("p (a c e) -> p a c e", c=4, e=2), src.rearrange("p e (c a) -> p a c e", c=4)
             else:
-                dst = half.rearrange("p (a j c t) -> p j a c t", j=2, c=2, t=4)[:, j]
-                src = src.rearrange("p t (c a) -> p a c t", c=2)
-            if engine == "S":
-                nc.scalar.activation(out=dst, in_=src, func=RELU)
-            else:
-                nc.vector.tensor_scalar(out=dst, in0=src, scalar1=0.0, scalar2=None, op0=MAX)
+                dst = h_tile(q)[:, 512 * part(q, j, G) : 512 * part(q, j, G) + 512]
+                if q < NPE:
+                    dst, src = dst.rearrange("p (n t) -> p n t", t=4), src.rearrange("p t n -> p n t")
+                elif q == 7:
+                    dst, src = dst.rearrange("p (i c t) -> p i c t", c=4, t=4), src.rearrange("p t (c i) -> p i c t", c=4)
+                else:
+                    dst = h_tile(q)[:, 1024 * G : 1024 * G + 1024].rearrange("p (a j c t) -> p j a c t", j=2, c=2, t=4)[:, j]
+                    src = src.rearrange("p t (c a) -> p a c t", c=2)
+            nc.scalar.activation(out=dst, in_=src, func=RELU)
+
+        def h_zip(q, G, engine):
+            if wide(q, G):
+                copy(
+                    engine,
+                    h_tile(q)[:, 1024 * G : 1024 * G + 1024].bitcast(F32).rearrange("p (n i u) -> p n u i", i=2, u=2),
+                    h_half[q, G][:].bitcast(F32).rearrange("p u (n i) -> p n u i", i=2),
+                )
 
         def h_quant(q, c0=0, n=512):
             quantize(h_c[q], h_s[q], h_t[q], c0, n)
@@ -234,7 +271,7 @@ def tile_pointnet_set_encoder_s12_kernel(tc, x, w, u_words, u_scales, v_words, v
             y = bank(("y", m, n0), [128, n])
             nh, j0 = n0 // 512, n0 % 512
             for G in range(2):
-                k = slice(256 * G + 128 * (m % 2), 256 * G + 128 * (m % 2) + 128)
+                k = slice(128 * part(m // 2, m % 2, G), 128 * part(m // 2, m % 2, G) + 128)
                 nc.tensor.matmul_mx(
                     out=y[:],
                     lhsT=h_c[m // 2][:, k].bitcast(FP8X4), lhsT_scale=h_s[m // 2][:, k],
@@ -253,19 +290,19 @@ def tile_pointnet_set_encoder_s12_kernel(tc, x, w, u_words, u_scales, v_words, v
             if m % 8 == 7:
                 nc.sync.dma_start(out=out[128 * s : 128 * s + 128, n0 : n0 + n], in_=a)
 
-        nc.vector.memset(v_pl[:].bitcast(I32), 0)
-        nc.vector.memset(u_pl_raw[:].bitcast(I32), 0)
         nc.vector.memset(ident[:], 0.0)
-        load_x(0)
-        nc.sync.dma_start(out=u_raw[:].bitcast(I32), in_=u_words[0].bitcast(I32))
-        for Q in range(2):
-            load_scales(nc.gpsimd, v_pl, vs32, Q)
+        zero = sb([128, 512], BF16, "zero")
+        nc.vector.memset(zero[:].bitcast(I32), 0)
+        nc.vector.memset(v_pl[:].bitcast(I32), 0)
+        nc.vector.memset(u_pl[:].bitcast(I32), 0)
         make_identity(nc, ident[:], nomemset=True)
         for Q in range(4):
-            load_scales(nc.scalar, u_pl_raw, us32, Q)
-        load_scales(nc.sync, v_pl, vs32, 2)
+            load_scales(nc.scalar if Q % 2 else nc.sync, u_pl_raw, us32, Q)
+        load_x(0)
+        nc.sync.dma_start(out=u_raw[:].bitcast(I32), in_=u_words[0].bitcast(I32))
         nc.sync.dma_start(out=v_w[:].bitcast(I32), in_=v_words[0].bitcast(I32))
-        load_scales(nc.sync, v_pl, vs32, 3)
+        for Q in range(4):
+            load_scales(nc.sync, v_pl, vs32, Q)
         load_w(0, 0)
         load_w(1, 0)
         load_x(1)
@@ -276,26 +313,25 @@ def tile_pointnet_set_encoder_s12_kernel(tc, x, w, u_words, u_scales, v_words, v
         for q in range(4, 8):
             load_x_quad(q, 1, q - 4)
 
-        zero = sb([128, 512], BF16, "zero")
-        nc.vector.memset(zero[:].bitcast(I32), 0)
         warm = bank("warm", [128, 512])
         for i in range(WARM):
             nc.tensor.matmul(warm[:], lhsT=zero[:, 0:128], rhs=zero[:], start=True, stop=True)
         x_transpose(0)
         for i in range(WARM2):
             nc.tensor.matmul(warm[:], lhsT=zero[:, 0:128], rhs=zero[:], start=True, stop=True)
+        for Q in range(4):
+            permute_u_scales(Q)
         permute_u()
-        permute_u_scales()
         x_out(0, 0, XE[0])
         x_out(0, 1, XE[1])
-        for k in range(0, 16, 2):
+        for k in range(16):
             if k == T1AT:
                 x_transpose(1)
-            e_mm((k, k + 1))
+            e_mm(k)
             e_out(k, "V" if k in EV else "S")
-            e_out(k + 1, "V" if k + 1 in EV else "S")
-            if k == W0AT:
+            if k == XQ0:
                 x_quant(0)
+            if k == W0AT:
                 w_weave(0, 0)
                 w_weave(1, 0)
                 w_quant(0, 0)
@@ -310,65 +346,76 @@ def tile_pointnet_set_encoder_s12_kernel(tc, x, w, u_words, u_scales, v_words, v
         w_quant(0, 1)
         w_quant(1, 1)
         for q in range(2):
-            first(q, 0)
-            h_out(q, 0, 0)
-            h_out(q, 0, 1)
+            for j in range(2):
+                first(q, 0, j)
+                h_out(q, 0, j)
         for q in range(2, 4):
             x_transpose(q)
             x_out(q, 0, XE[2 * q])
             x_out(q, 1, XE[2 * q + 1])
+        h_zip(0, 0, "V")
+        h_zip(1, 0, "V")
         e_quant(0, 0)
         x_quant(2)
         for q in range(2):
-            first(q, 1)
-            h_out(q, 1, 0)
-            h_out(q, 1, 1)
-        if SE[0] == "S":
-            x_split(4, "S")
+            for j in range(2):
+                first(q, 1, j)
+                h_out(q, 1, j)
         e_quant(1, 0)
         x_quant(3)
-        h_quant(0)
-        if SE[0] == "V":
-            x_split(4, "V")
+        h_zip(0, 1, "V")
         e_quant(0, 1)
+        h_quant(0)
+        h_zip(1, 1, "V")
         e_quant(1, 1)
+        h_quant(1)
 
         todo = [(m, 0) for m in range(2)] + [(m, 512) for m in range(2)] + [(m, n0) for m in range(2, 15) for n0 in (0, 512)]
+        waiting = []
 
-        def due(step, lead):
-            return [q for q in range(4, 8) if step + lead == 2 * (q - 2)]
+        def one_second():
+            second(*todo[0])
+            waiting.append(todo.pop(0))
 
-        for step in range(12):
-            q, G = 2 + step // 2, step % 2
-            first(q, G)
-            now = [todo.pop(0) for i in range(0 if step < FIRST_SECOND else 2 if step < LATE else 3)]
-            if G == 0:
-                h_quant(q - 1)
-            for y in now:
-                second(*y)
-            for p in due(step, QUANT_LEAD):
-                x_quant(p)
-            last = step == 11
-            if last:
-                h_quant(7, 0, 256)
-            h_out(q, G, 0)
-            h_out(q, G, 1, LAST_OUT if last else "S")
-            for y in now[:1]:
-                y_out(*y)
-            for p in due(step, TURN_LEAD):
-                x_turn(p)
-            if last:
-                h_quant(7, 256, 256)
-            for y in now[1:]:
-                y_out(*y)
-            for p in due(step, JOIN_LEAD):
+        def drain(keep_back):
+            while len(waiting) > keep_back or (waiting and waiting[0][0] % 8 == 0):
+                y_out(*waiting.pop(0))
+
+        def due(slot, lead):
+            return [q for q in range(4, 8) if slot + lead == 4 * (q - 2)]
+
+        slots = [(q, G, j) for q in range(2, 7) for G in range(2) for j in range(2)]
+        slots = slots + [(7, G, j) for j in range(2) for G in range(2)]
+        for slot, (q, G, j) in enumerate(slots):
+            first(q, G, j)
+            if slot >= FIRST_SECOND:
+                one_second()
+            if slot >= LATE and slot % 2 == 1:
+                one_second()
+            if slot == 22:
+                for i in range(EXTRA):
+                    one_second()
+            h_out(q, G, j)
+            for p in due(slot, SPLIT_LEAD):
+                x_split(p, SE[p - 4])
+            for p in due(slot, JOIN_LEAD):
                 x_join(p, JE[p - 4])
-            for p in due(step, SPLIT_LEAD):
-                if p > 4:
-                    x_split(p, SE[p - 4])
-        for y in todo:
-            second(*y)
-            y_out(*y)
+            drain(1 if slot < HOLD_UNTIL else 0)
+            if slot % 2 == 0 and 0 < slot <= 20:
+                h_zip(*slots[slot - 1][:2], ZE[slot // 2 - 1])
+            for p in due(slot, TURN_LEAD):
+                x_turn(p)
+            for p in due(slot, QUANT_LEAD):
+                x_quant(p)
+            if slot % 4 == 1 and slot >= 4:
+                h_quant(q - 1)
+            if slot == 22:
+                h_quant(7, 0, 256)
+                h_quant(7, 256, 128)
+        h_quant(7, 384, 128)
+        while todo:
+            one_second()
+            drain(0)
         for n0 in range(0, 1024, STORE_PIECE):
             second(15, n0, STORE_PIECE)
             y_out(15, n0, STORE_PIECE)

@@ -13,29 +13,24 @@ U8 = mybir.dt.uint8
 FP8X4 = mybir.dt.float8_e4m3fn_x4
 FP4X4 = mybir.dt.float4_e2m1fn_x4
 MAX = mybir.AluOpType.max
+MULT = mybir.AluOpType.mult
+ADD = mybir.AluOpType.add
 RELU = mybir.ActivationFunctionType.Relu
 
 NPE = 4
-NARROW = ((0, 0), (0, 1), (1, 0), (1, 1), (3, 1), (4, 0), (7, 0), (7, 1))
+NARROW = ((0, 0), (0, 1), (1, 0), (1, 1), (7, 0), (7, 1))
 WARM = 5
 XE = "VSVVVSSS"
 EV = ()
 W0AT = 0
-FIRST_SECOND = 2
-LATE = 16
-HOLD_UNTIL = 18
-SPLIT_LEAD = 7
-TURN_LEAD = 6
-JOIN_LEAD = 4
-QUANT_LEAD = 3
-SE = "VVSS"
-JE = "SSSS"
-ZE = "VVSVVVSSSS"
+ZE = "SSSSSSVVSS"
 STORE_PIECE = 256
 WARM2 = 1
 T1AT = 12
 XQ0 = 0
-EXTRA = 0
+COUNT = "10111111111111110200"
+OPEN = 4
+BAT = "00001"
 
 
 def tile_pointnet_set_encoder_s12_kernel(tc, x, w, u_words, u_scales, v_words, v_scales, out):
@@ -94,8 +89,7 @@ def tile_pointnet_set_encoder_s12_kernel(tc, x, w, u_words, u_scales, v_words, v
                 for Q in (0, 2, 1, 3):
                     k0 = 512 * g + 128 * Q
                     nc.sync.dma_start(out=t[32 * Q : 32 * Q + 32, g], in_=rows[:, :, k0 : k0 + 128])
-            for a in range(n):
-                x_words[q0 + a] = t[:].bitcast(F32).rearrange("p g (c a b) (j u) -> p a (g c) b u j", a=n, b=2, u=2)[:, a]
+            x_words[q0] = t[:].rearrange("p g m k -> p (g m k)").bitcast(F32)
 
         def load_w(g, G):
             nc.sync.dma_start(out=w_raw[g, G][:], in_=w_rows[g][:, :, 512 * G : 512 * G + 512])
@@ -179,28 +173,31 @@ def tile_pointnet_set_encoder_s12_kernel(tc, x, w, u_words, u_scales, v_words, v
                 banks["x", q, b][:].rearrange("p g u n -> p g n u"),
             )
 
-        def x_split(q, engine):
-            x_r[q] = sb([128, 1024], F32, "x_r", 2)
-            copy(engine, x_r[q][:].rearrange("p (a b u j) -> p a b u j", b=2, u=2, j=32), x_words[q])
+        def x_split(q):
+            x_r[q] = sb([128, 2048], BF16, "stage%d" % (q % 4) if q > NPE else "x_r")
+            if q == NPE:
+                copy("V", x_r[q][:].bitcast(F32).rearrange("p (u n) -> p u n", u=2), x_words[q].rearrange("p (n u) -> p u n", u=2))
+            else:
+                nc.gpsimd.tensor_scalar(
+                    out=x_r[q][:].rearrange("p (u n e) -> p u n e", u=2, e=2),
+                    in0=x_words[q].bitcast(BF16).rearrange("p (n u e) -> p u n e", u=2, e=2),
+                    scalar1=1.0, scalar2=0.0, op0=MULT, op1=ADD,
+                )
 
         def x_turn(q):
             x_t[q] = sb([128, 1024], F32, "x_t", 2)
-            nc.vector.transpose(x_t[q][:], x_r[q][:])
+            nc.vector.transpose(x_t[q][:], x_r[q][:].bitcast(F32))
 
-        def x_join(q, engine):
+        def x_join(q):
             x_g[q] = sb([128, 2048], BF16, "x_g", 3)
             if q < 7:
-                copy(
-                    engine,
-                    x_g[q][:].bitcast(F32).rearrange("p (a i u) -> p a i u", u=2, i=32),
-                    x_t[q][:].rearrange("p (a u i) -> p a i u", u=2, i=32),
-                )
+                copy("S", x_g[q][:].bitcast(F32).rearrange("p (n u) -> p n u", u=2), x_t[q][:].rearrange("p (u n) -> p n u", u=2))
             else:
                 for g in range(2):
                     copy(
-                        engine,
-                        x_g[q][:].bitcast(F32).rearrange("p (g b c i u) -> p g b c i u", g=2, b=2, u=2, i=32)[:, g],
-                        x_t[q][:].rearrange("p (g c b u i) -> p g b c i u", g=2, b=2, u=2, i=32)[:, g],
+                        "S",
+                        x_g[q][:].bitcast(F32).rearrange("p (g b c i u) -> p g b c i u", g=2, b=2, c=4, u=2)[:, g],
+                        x_t[q][:].rearrange("p (u g c b i) -> p g b c i u", u=2, g=2, b=2, c=4)[:, g],
                     )
 
         def x_quant(q):
@@ -217,7 +214,7 @@ def tile_pointnet_set_encoder_s12_kernel(tc, x, w, u_words, u_scales, v_words, v
 
         def h_tile(q):
             if q not in h_t:
-                h_t[q] = sb([128, 2048], BF16, "h_t", 4)
+                h_t[q] = sb([128, 2048], BF16, "stage%d" % (q % 4))
             return h_t[q]
 
         def first(q, G, j):
@@ -239,7 +236,7 @@ def tile_pointnet_set_encoder_s12_kernel(tc, x, w, u_words, u_scales, v_words, v
             src = banks["h", q, G, j][:]
             if wide(q, G):
                 if j == 0:
-                    h_half[q, G] = sb([128, 2, 512], BF16, "h_half", 3)
+                    h_half[q, G] = sb([128, 2, 512], BF16, "h_half", 4)
                 dst = h_half[q, G][:, j, :]
                 if q < NPE:
                     dst, src = dst.rearrange("p (n e) -> p n e", e=2), src.rearrange("p e n -> p n e")
@@ -356,66 +353,73 @@ def tile_pointnet_set_encoder_s12_kernel(tc, x, w, u_words, u_scales, v_words, v
         h_zip(0, 0, "V")
         h_zip(1, 0, "V")
         e_quant(0, 0)
+        e_quant(1, 0)
         x_quant(2)
         for q in range(2):
             for j in range(2):
                 first(q, 1, j)
                 h_out(q, 1, j)
-        e_quant(1, 0)
-        x_quant(3)
-        h_zip(0, 1, "V")
         e_quant(0, 1)
+        x_split(4)
         h_quant(0)
-        h_zip(1, 1, "V")
         e_quant(1, 1)
+        x_quant(3)
         h_quant(1)
+        x_split(5)
+        x_turn(4)
 
-        todo = [(m, 0) for m in range(2)] + [(m, 512) for m in range(2)] + [(m, n0) for m in range(2, 15) for n0 in (0, 512)]
-        waiting = []
+        todo = [(m, n0) for m in range(15) for n0 in (0, 512)]
 
-        def one_second():
-            second(*todo[0])
-            waiting.append(todo.pop(0))
+        def seconds(n):
+            for i in range(n):
+                second(*todo[0])
+                y_out(*todo.pop(0))
 
-        def drain(keep_back):
-            while len(waiting) > keep_back or (waiting and waiting[0][0] % 8 == 0):
-                y_out(*waiting.pop(0))
+        def zips(q, engine):
+            for G in range(2):
+                if ZE[2 * q - 4 + G] == engine:
+                    h_zip(q, G, engine)
 
-        def due(slot, lead):
-            return [q for q in range(4, 8) if slot + lead == 4 * (q - 2)]
+        def behind(q):
+            if q + 2 < 8:
+                x_quant(q + 2)
+            zips(q, "V")
+            seconds(1 if q == 2 else 0)
+            h_quant(q)
+            if q + 4 < 8:
+                x_split(q + 4)
+            if q + 3 < 8:
+                x_turn(q + 3)
 
-        slots = [(q, G, j) for q in range(2, 7) for G in range(2) for j in range(2)]
-        slots = slots + [(7, G, j) for j in range(2) for G in range(2)]
+        for j in range(2):
+            first(2, 0, j)
+            h_out(2, 0, j)
+        for j in range(2):
+            first(2, 1, j)
+        seconds(OPEN)
+        for j in range(2):
+            h_out(2, 1, j)
+        x_join(4)
+        zips(2, "S")
+        slots = [(q, G, j) for q in range(3, 7) for G in range(2) for j in range(2)] + [(7, G, j) for j in range(2) for G in range(2)]
         for slot, (q, G, j) in enumerate(slots):
             first(q, G, j)
-            if slot >= FIRST_SECOND:
-                one_second()
-            if slot >= LATE and slot % 2 == 1:
-                one_second()
-            if slot == 22:
-                for i in range(EXTRA):
-                    one_second()
             h_out(q, G, j)
-            for p in due(slot, SPLIT_LEAD):
-                x_split(p, SE[p - 4])
-            for p in due(slot, JOIN_LEAD):
-                x_join(p, JE[p - 4])
-            drain(1 if slot < HOLD_UNTIL else 0)
-            if slot % 2 == 0 and 0 < slot <= 20:
-                h_zip(*slots[slot - 1][:2], ZE[slot // 2 - 1])
-            for p in due(slot, TURN_LEAD):
-                x_turn(p)
-            for p in due(slot, QUANT_LEAD):
-                x_quant(p)
-            if slot % 4 == 1 and slot >= 4:
-                h_quant(q - 1)
-            if slot == 22:
+            seconds(int(COUNT[slot]))
+            if slot % 4 == int(BAT[q - 3]):
+                behind(q - 1)
+                seconds(2 if q == 7 else 0)
+            if slot % 4 == 3 and q < 7:
+                if q + 2 < 8:
+                    x_join(q + 2)
+                zips(q, "S")
+            if slot == 18:
                 h_quant(7, 0, 256)
+                seconds(1)
                 h_quant(7, 256, 128)
+                seconds(2)
         h_quant(7, 384, 128)
-        while todo:
-            one_second()
-            drain(0)
+        seconds(len(todo))
         for n0 in range(0, 1024, STORE_PIECE):
             second(15, n0, STORE_PIECE)
             y_out(15, n0, STORE_PIECE)

@@ -23,14 +23,19 @@ WARM = 5
 XE = "VSVVVSSS"
 EV = ()
 W0AT = 0
-ZE = "SSSSSSVVSS"
+ZE = "SSSSSSGVSS"
 STORE_PIECE = 256
 WARM2 = 1
 T1AT = 12
 XQ0 = 0
-COUNT = "10111111111111110200"
+COUNT = "11111111111111113000"
 OPEN = 4
-BAT = "00001"
+E1 = 1
+E2 = 1
+E3 = 2
+E4 = 1
+A7 = 17
+BAT = "00000"
 
 
 def tile_pointnet_set_encoder_s12_kernel(tc, x, w, u_words, u_scales, v_words, v_scales, out):
@@ -80,16 +85,17 @@ def tile_pointnet_set_encoder_s12_kernel(tc, x, w, u_words, u_scales, v_words, v
         def load_x(q):
             nc.sync.dma_start(out=x_sb[q][:].rearrange("p (b k) -> p b k", b=2), in_=x_rows[0][:, 2 * q : 2 * q + 2, :])
 
-        x_words = {}
+        x_quad = {(q, g): sb([128, 1024], BF16, "x_quad%d%d" % (q, g)) for q in range(4, 8) for g in range(2)}
+        x_rows_quad = x.rearrange("(s i m r) k -> s r i m k", s=2, i=32, r=4)[1]
 
-        def load_x_quad(q0, n, r):
-            t = sb([128, 2, 8 * n, 128], BF16, "x_quad%d" % q0)
-            rows = x.rearrange("(s i m r) k -> s r i m k", s=2, i=32, r=4 // n)[1, r]
+        def load_x_quad(q):
             for g in range(2):
                 for Q in (0, 2, 1, 3):
                     k0 = 512 * g + 128 * Q
-                    nc.sync.dma_start(out=t[32 * Q : 32 * Q + 32, g], in_=rows[:, :, k0 : k0 + 128])
-            x_words[q0] = t[:].rearrange("p g m k -> p (g m k)").bitcast(F32)
+                    nc.sync.dma_start(
+                        out=x_quad[q, g][32 * Q : 32 * Q + 32, :].rearrange("p (m k) -> p m k", m=8),
+                        in_=x_rows_quad[q - 4][:, :, k0 : k0 + 128],
+                    )
 
         def load_w(g, G):
             nc.sync.dma_start(out=w_raw[g, G][:], in_=w_rows[g][:, :, 512 * G : 512 * G + 512])
@@ -174,15 +180,20 @@ def tile_pointnet_set_encoder_s12_kernel(tc, x, w, u_words, u_scales, v_words, v
             )
 
         def x_split(q):
-            x_r[q] = sb([128, 2048], BF16, "stage%d" % (q % 4) if q > NPE else "x_r")
-            if q == NPE:
-                copy("V", x_r[q][:].bitcast(F32).rearrange("p (u n) -> p u n", u=2), x_words[q].rearrange("p (n u) -> p u n", u=2))
-            else:
-                nc.gpsimd.tensor_scalar(
-                    out=x_r[q][:].rearrange("p (u n e) -> p u n e", u=2, e=2),
-                    in0=x_words[q].bitcast(BF16).rearrange("p (n u e) -> p u n e", u=2, e=2),
-                    scalar1=1.0, scalar2=0.0, op0=MULT, op1=ADD,
-                )
+            x_r[q] = sb([128, 2048], BF16, "stage%d" % (q % 4) if q > 5 else "x_r")
+            for g in range(2):
+                if q <= 5:
+                    copy(
+                        "V",
+                        x_r[q][:].bitcast(F32).rearrange("p (u g n) -> p g u n", u=2, g=2)[:, g],
+                        x_quad[q, g][:].bitcast(F32).rearrange("p (n u) -> p u n", u=2),
+                    )
+                else:
+                    nc.gpsimd.tensor_scalar(
+                        out=x_r[q][:].rearrange("p (u g n e) -> p g u n e", u=2, g=2, e=2)[:, g],
+                        in0=x_quad[q, g][:].rearrange("p (n u e) -> p u n e", u=2, e=2),
+                        scalar1=1.0, scalar2=0.0, op0=MULT, op1=ADD,
+                    )
 
         def x_turn(q):
             x_t[q] = sb([128, 1024], F32, "x_t", 2)
@@ -214,7 +225,7 @@ def tile_pointnet_set_encoder_s12_kernel(tc, x, w, u_words, u_scales, v_words, v
 
         def h_tile(q):
             if q not in h_t:
-                h_t[q] = sb([128, 2048], BF16, "stage%d" % (q % 4))
+                h_t[q] = sb([128, 2048], BF16, "stage%d" % (0 if q == 5 else q % 4))
             return h_t[q]
 
         def first(q, G, j):
@@ -254,7 +265,13 @@ def tile_pointnet_set_encoder_s12_kernel(tc, x, w, u_words, u_scales, v_words, v
             nc.scalar.activation(out=dst, in_=src, func=RELU)
 
         def h_zip(q, G, engine):
-            if wide(q, G):
+            if engine == "G":
+                nc.gpsimd.tensor_scalar(
+                    out=h_tile(q)[:, 1024 * G : 1024 * G + 1024].rearrange("p (c u e) -> p c u e", u=2, e=2),
+                    in0=h_half[q, G][:].rearrange("p u (c e) -> p c u e", e=2),
+                    scalar1=1.0, scalar2=0.0, op0=MULT, op1=ADD,
+                )
+            elif wide(q, G):
                 copy(
                     engine,
                     h_tile(q)[:, 1024 * G : 1024 * G + 1024].bitcast(F32).rearrange("p (n i u) -> p n u i", i=2, u=2),
@@ -308,7 +325,7 @@ def tile_pointnet_set_encoder_s12_kernel(tc, x, w, u_words, u_scales, v_words, v
         load_x(2)
         load_x(3)
         for q in range(4, 8):
-            load_x_quad(q, 1, q - 4)
+            load_x_quad(q)
 
         warm = bank("warm", [128, 512])
         for i in range(WARM):
@@ -360,12 +377,11 @@ def tile_pointnet_set_encoder_s12_kernel(tc, x, w, u_words, u_scales, v_words, v
                 first(q, 1, j)
                 h_out(q, 1, j)
         e_quant(0, 1)
-        x_split(4)
-        h_quant(0)
         e_quant(1, 1)
+        h_quant(0)
         x_quant(3)
+        x_split(4)
         h_quant(1)
-        x_split(5)
         x_turn(4)
 
         todo = [(m, n0) for m in range(15) for n0 in (0, 512)]
@@ -381,10 +397,11 @@ def tile_pointnet_set_encoder_s12_kernel(tc, x, w, u_words, u_scales, v_words, v
                     h_zip(q, G, engine)
 
         def behind(q):
+            if q == 2:
+                x_split(5)
+            zips(q, "V")
             if q + 2 < 8:
                 x_quant(q + 2)
-            zips(q, "V")
-            seconds(1 if q == 2 else 0)
             h_quant(q)
             if q + 4 < 8:
                 x_split(q + 4)
@@ -405,19 +422,23 @@ def tile_pointnet_set_encoder_s12_kernel(tc, x, w, u_words, u_scales, v_words, v
         for slot, (q, G, j) in enumerate(slots):
             first(q, G, j)
             h_out(q, G, j)
+            if j == 1 and q < 7 and ZE[2 * q - 4 + G] == "G":
+                h_zip(q, G, "G")
             seconds(int(COUNT[slot]))
             if slot % 4 == int(BAT[q - 3]):
                 behind(q - 1)
-                seconds(2 if q == 7 else 0)
+                seconds(E1 if q == 7 else 0)
             if slot % 4 == 3 and q < 7:
                 if q + 2 < 8:
                     x_join(q + 2)
                 zips(q, "S")
-            if slot == 18:
+            if slot == A7:
                 h_quant(7, 0, 256)
-                seconds(1)
+            if slot == 18:
+                seconds(E2)
                 h_quant(7, 256, 128)
-                seconds(2)
+                seconds(E3)
+        seconds(E4)
         h_quant(7, 384, 128)
         seconds(len(todo))
         for n0 in range(0, 1024, STORE_PIECE):

@@ -18,12 +18,15 @@ ADD = mybir.AluOpType.add
 RELU = mybir.ActivationFunctionType.Relu
 
 NPE = 4
-NARROW = ((0, 0), (0, 1), (1, 0), (1, 1), (7, 0), (7, 1))
+NARROW = ((0, 1), (1, 0), (1, 1), (7, 0), (7, 1))
 WARM = 5
 XE = "VSVVVSSS"
 EV = ()
 W0AT = 0
-ZE = "SSSSSSGVSS"
+POOL_ZIP = (2, 5, 6)
+STAGE_H = ("stage_a", "stage_b", "stage_b", "stage_c", "stage_a", "stage_a", "stage_a", "stage_c")
+STAGE_X = {6: "stage_b", 7: "stage_c"}
+WFILL = 8
 STORE_PIECE = 256
 WARM2 = 1
 T1AT = 12
@@ -70,9 +73,9 @@ def tile_pointnet_set_encoder_s12_kernel(tc, x, w, u_words, u_scales, v_words, v
         w_grp = {k: sb([128, 2048], BF16, "w_grp%d%d" % k) for k in quarters}
         w_c = {k: sb([128, 512], U32, "w_c%d%d" % k) for k in quarters}
         w_s = {k: sb([128, 512], U8, "w_s%d%d" % k) for k in quarters}
-        e_grp = {k: sb([128, 2048], BF16, "e_grp%d%d" % k) for k in quarters}
-        e_c = {k: sb([128, 512], U32, "e_c%d%d" % k) for k in quarters}
-        e_s = {k: sb([128, 512], U8, "e_s%d%d" % k) for k in quarters}
+        e_grp = [sb([128, 4096], BF16, "e_grp%d" % nh) for nh in range(2)]
+        e_c = [sb([128, 1024], U32, "e_c%d" % nh) for nh in range(2)]
+        e_s = [sb([128, 1024], U8, "e_s%d" % nh) for nh in range(2)]
         h_c = [sb([128, 512], U32, "h_c%d" % q) for q in range(8)]
         h_s = [sb([128, 512], U8, "h_s%d" % q) for q in range(8)]
         acc = [sb([128, 1024], F32, "acc%d" % s) for s in range(2)]
@@ -85,7 +88,7 @@ def tile_pointnet_set_encoder_s12_kernel(tc, x, w, u_words, u_scales, v_words, v
         def load_x(q):
             nc.sync.dma_start(out=x_sb[q][:].rearrange("p (b k) -> p b k", b=2), in_=x_rows[0][:, 2 * q : 2 * q + 2, :])
 
-        x_quad = {(q, g): sb([128, 1024], BF16, "x_quad%d%d" % (q, g)) for q in range(4, 8) for g in range(2)}
+        x_quad = {q: sb([128, 2048], BF16, "x_quad%d" % q) for q in range(4, 8)}
         x_rows_quad = x.rearrange("(s i m r) k -> s r i m k", s=2, i=32, r=4)[1]
 
         def load_x_quad(q):
@@ -93,7 +96,7 @@ def tile_pointnet_set_encoder_s12_kernel(tc, x, w, u_words, u_scales, v_words, v
                 for Q in (0, 2, 1, 3):
                     k0 = 512 * g + 128 * Q
                     nc.sync.dma_start(
-                        out=x_quad[q, g][32 * Q : 32 * Q + 32, :].rearrange("p (m k) -> p m k", m=8),
+                        out=x_quad[q][32 * Q : 32 * Q + 32, 1024 * g : 1024 * g + 1024].rearrange("p (m k) -> p m k", m=8),
                         in_=x_rows_quad[q - 4][:, :, k0 : k0 + 128],
                     )
 
@@ -109,6 +112,9 @@ def tile_pointnet_set_encoder_s12_kernel(tc, x, w, u_words, u_scales, v_words, v
             else:
                 nc.vector.tensor_copy(out=out, in_=in_)
 
+        def pool_copy(out, in_):
+            nc.gpsimd.tensor_scalar(out=out, in0=in_, scalar1=1.0, scalar2=0.0, op0=MULT, op1=ADD)
+
         def permute_u():
             nc.vector.tensor_copy(
                 out=u_w[:].bitcast(I32).rearrange("p (G t q r) -> p G t q r", G=2, t=4, q=32, r=2),
@@ -121,10 +127,10 @@ def tile_pointnet_set_encoder_s12_kernel(tc, x, w, u_words, u_scales, v_words, v
                 in_=u_pl_raw[32 * Q : 32 * Q + 4, :].bitcast(I32).rearrange("p (G q t) -> p G t q", G=2, q=32, t=4),
             )
 
-        def w_weave(g, G, t0=0, n=4):
+        def w_weave(g, G, q0=0, q1=32):
             nc.vector.tensor_copy(
-                out=w_grp[g, G][:].rearrange("p (t q r j) -> p t q j r", t=4, q=32, r=4, j=4)[:, t0 : t0 + n],
-                in_=w_raw[g, G][:].rearrange("p j (q t r) -> p t q j r", q=32, t=4, r=4)[:, t0 : t0 + n],
+                out=w_grp[g, G][:].rearrange("p (t q r j) -> p t q j r", t=4, q=32, r=4, j=4)[:, :, q0:q1],
+                in_=w_raw[g, G][:].rearrange("p j (q t r) -> p t q j r", q=32, t=4, r=4)[:, :, q0:q1],
             )
 
         def quantize(codes, scales, values, c0=0, n=512):
@@ -135,8 +141,8 @@ def tile_pointnet_set_encoder_s12_kernel(tc, x, w, u_words, u_scales, v_words, v
         def w_quant(g, G):
             quantize(w_c[g, G], w_s[g, G], w_grp[g, G])
 
-        def e_quant(G, nh):
-            quantize(e_c[G, nh], e_s[G, nh], e_grp[G, nh])
+        def e_quant(nh):
+            quantize(e_c[nh], e_s[nh], e_grp[nh], 0, 1024)
 
         def e_mm(k):
             G, nb = k // 4 % 2, k % 4 + k // 8 * 4
@@ -151,10 +157,10 @@ def tile_pointnet_set_encoder_s12_kernel(tc, x, w, u_words, u_scales, v_words, v
                 )
 
         def e_out(k, engine):
-            j = k % 4
+            j = k % 8
             copy(
                 engine,
-                e_grp[k // 4 % 2, k // 8][:, 512 * j : 512 * j + 512].rearrange("p (n t) -> p n t", t=4),
+                e_grp[k // 8][:, 512 * j : 512 * j + 512].rearrange("p (n t) -> p n t", t=4),
                 banks["e", k][:].rearrange("p t n -> p n t"),
             )
 
@@ -180,19 +186,14 @@ def tile_pointnet_set_encoder_s12_kernel(tc, x, w, u_words, u_scales, v_words, v
             )
 
         def x_split(q):
-            x_r[q] = sb([128, 2048], BF16, "stage%d" % (q % 4) if q > 5 else "x_r")
-            for g in range(2):
-                if q <= 5:
-                    copy(
-                        "V",
-                        x_r[q][:].bitcast(F32).rearrange("p (u g n) -> p g u n", u=2, g=2)[:, g],
-                        x_quad[q, g][:].bitcast(F32).rearrange("p (n u) -> p u n", u=2),
-                    )
-                else:
-                    nc.gpsimd.tensor_scalar(
-                        out=x_r[q][:].rearrange("p (u g n e) -> p g u n e", u=2, g=2, e=2)[:, g],
-                        in0=x_quad[q, g][:].rearrange("p (n u e) -> p u n e", u=2, e=2),
-                        scalar1=1.0, scalar2=0.0, op0=MULT, op1=ADD,
+            x_r[q] = sb([128, 2048], BF16, STAGE_X.get(q, "x_r"))
+            if q <= 5:
+                copy("V", x_r[q][:].bitcast(F32).rearrange("p (u n) -> p u n", u=2), x_quad[q][:].bitcast(F32).rearrange("p (n u) -> p u n", u=2))
+            else:
+                for g in range(2):
+                    pool_copy(
+                        x_r[q][:].rearrange("p (u g n e) -> p g u n e", u=2, g=2, e=2)[:, g],
+                        x_quad[q][:, 1024 * g : 1024 * g + 1024].rearrange("p (n u e) -> p u n e", u=2, e=2),
                     )
 
         def x_turn(q):
@@ -225,7 +226,7 @@ def tile_pointnet_set_encoder_s12_kernel(tc, x, w, u_words, u_scales, v_words, v
 
         def h_tile(q):
             if q not in h_t:
-                h_t[q] = sb([128, 2048], BF16, "stage%d" % (0 if q == 5 else q % 4))
+                h_t[q] = sb([128, 2048], BF16, STAGE_H[q])
             return h_t[q]
 
         def first(q, G, j):
@@ -246,9 +247,9 @@ def tile_pointnet_set_encoder_s12_kernel(tc, x, w, u_words, u_scales, v_words, v
         def h_out(q, G, j):
             src = banks["h", q, G, j][:]
             if wide(q, G):
-                if j == 0:
-                    h_half[q, G] = sb([128, 2, 512], BF16, "h_half", 4)
-                dst = h_half[q, G][:, j, :]
+                if q not in h_half:
+                    h_half[q] = sb([128, 2048], BF16, "h_half", 3)
+                dst = h_half[q][:, 1024 * G + 512 * j : 1024 * G + 512 * j + 512]
                 if q < NPE:
                     dst, src = dst.rearrange("p (n e) -> p n e", e=2), src.rearrange("p e n -> p n e")
                 else:
@@ -264,19 +265,25 @@ def tile_pointnet_set_encoder_s12_kernel(tc, x, w, u_words, u_scales, v_words, v
                     src = src.rearrange("p t (c a) -> p a c t", c=2)
             nc.scalar.activation(out=dst, in_=src, func=RELU)
 
-        def h_zip(q, G, engine):
-            if engine == "G":
-                nc.gpsimd.tensor_scalar(
-                    out=h_tile(q)[:, 1024 * G : 1024 * G + 1024].rearrange("p (c u e) -> p c u e", u=2, e=2),
-                    in0=h_half[q, G][:].rearrange("p u (c e) -> p c u e", e=2),
-                    scalar1=1.0, scalar2=0.0, op0=MULT, op1=ADD,
+        def h_zip_pool(q):
+            pool_copy(
+                h_tile(q)[:, 0:1024].rearrange("p (c u e) -> p c u e", u=2, e=2),
+                h_half[q][:, 0:1024].rearrange("p (u c e) -> p c u e", u=2, e=2),
+            )
+
+        def h_zip_front(q):
+            if wide(q, 0):
+                nc.vector.tensor_copy(
+                    out=h_tile(q)[:, 0:1024].bitcast(F32).rearrange("p (n i u) -> p n u i", i=2, u=2),
+                    in_=h_half[q][:, 0:1024].bitcast(F32).rearrange("p (u n i) -> p n u i", i=2, u=2),
                 )
-            elif wide(q, G):
-                copy(
-                    engine,
-                    h_tile(q)[:, 1024 * G : 1024 * G + 1024].bitcast(F32).rearrange("p (n i u) -> p n u i", i=2, u=2),
-                    h_half[q, G][:].bitcast(F32).rearrange("p u (n i) -> p n u i", i=2),
-                )
+
+        def h_zip(q):
+            G0 = 1 if q in POOL_ZIP else 0
+            nc.scalar.copy(
+                h_tile(q)[:, 1024 * G0 :].bitcast(F32).rearrange("p (G n i u) -> p G n u i", n=128, i=2, u=2),
+                h_half[q][:, 1024 * G0 :].bitcast(F32).rearrange("p (G u n i) -> p G n u i", n=128, i=2, u=2),
+            )
 
         def h_quant(q, c0=0, n=512):
             quantize(h_c[q], h_s[q], h_t[q], c0, n)
@@ -289,7 +296,7 @@ def tile_pointnet_set_encoder_s12_kernel(tc, x, w, u_words, u_scales, v_words, v
                 nc.tensor.matmul_mx(
                     out=y[:],
                     lhsT=h_c[m // 2][:, k].bitcast(FP8X4), lhsT_scale=h_s[m // 2][:, k],
-                    rhs=e_c[G, nh][:, j0 : j0 + n].bitcast(FP8X4), rhs_scale=e_s[G, nh][:, j0 : j0 + n],
+                    rhs=e_c[nh][:, 512 * G + j0 : 512 * G + j0 + n].bitcast(FP8X4), rhs_scale=e_s[nh][:, 512 * G + j0 : 512 * G + j0 + n],
                     start=G == 0, stop=G == 1,
                 )
 
@@ -353,9 +360,9 @@ def tile_pointnet_set_encoder_s12_kernel(tc, x, w, u_words, u_scales, v_words, v
             if k == T1AT:
                 x_out(1, 0, XE[2])
                 x_out(1, 1, XE[3])
-        w_weave(0, 1, 0, 2)
+        w_weave(0, 1, 0, WFILL)
         x_quant(1)
-        w_weave(0, 1, 2, 2)
+        w_weave(0, 1, WFILL, 32)
         w_weave(1, 1)
         w_quant(0, 1)
         w_quant(1, 1)
@@ -367,18 +374,16 @@ def tile_pointnet_set_encoder_s12_kernel(tc, x, w, u_words, u_scales, v_words, v
             x_transpose(q)
             x_out(q, 0, XE[2 * q])
             x_out(q, 1, XE[2 * q + 1])
-        h_zip(0, 0, "V")
-        h_zip(1, 0, "V")
-        e_quant(0, 0)
-        e_quant(1, 0)
+        e_quant(0)
         x_quant(2)
         for q in range(2):
             for j in range(2):
                 first(q, 1, j)
                 h_out(q, 1, j)
-        e_quant(0, 1)
-        e_quant(1, 1)
+        h_zip_front(0)
+        e_quant(1)
         h_quant(0)
+        h_zip_front(1)
         x_quant(3)
         x_split(4)
         h_quant(1)
@@ -391,15 +396,9 @@ def tile_pointnet_set_encoder_s12_kernel(tc, x, w, u_words, u_scales, v_words, v
                 second(*todo[0])
                 y_out(*todo.pop(0))
 
-        def zips(q, engine):
-            for G in range(2):
-                if ZE[2 * q - 4 + G] == engine:
-                    h_zip(q, G, engine)
-
         def behind(q):
             if q == 2:
                 x_split(5)
-            zips(q, "V")
             if q + 2 < 8:
                 x_quant(q + 2)
             h_quant(q)
@@ -411,27 +410,28 @@ def tile_pointnet_set_encoder_s12_kernel(tc, x, w, u_words, u_scales, v_words, v
         for j in range(2):
             first(2, 0, j)
             h_out(2, 0, j)
+        h_zip_pool(2)
         for j in range(2):
             first(2, 1, j)
         seconds(OPEN)
         for j in range(2):
             h_out(2, 1, j)
         x_join(4)
-        zips(2, "S")
+        h_zip(2)
         slots = [(q, G, j) for q in range(3, 7) for G in range(2) for j in range(2)] + [(7, G, j) for j in range(2) for G in range(2)]
         for slot, (q, G, j) in enumerate(slots):
             first(q, G, j)
-            h_out(q, G, j)
-            if j == 1 and q < 7 and ZE[2 * q - 4 + G] == "G":
-                h_zip(q, G, "G")
             seconds(int(COUNT[slot]))
+            h_out(q, G, j)
+            if (G, j) == (0, 1) and q in POOL_ZIP:
+                h_zip_pool(q)
             if slot % 4 == int(BAT[q - 3]):
                 behind(q - 1)
                 seconds(E1 if q == 7 else 0)
             if slot % 4 == 3 and q < 7:
                 if q + 2 < 8:
                     x_join(q + 2)
-                zips(q, "S")
+                h_zip(q)
             if slot == A7:
                 h_quant(7, 0, 256)
             if slot == 18:

@@ -26,7 +26,6 @@ W0AT = 0
 POOL_ZIP = (2, 5, 6)
 STAGE_H = ("stage_a", "stage_b", "stage_b", "stage_c", "stage_a", "stage_a", "stage_a", "stage_c")
 STAGE_X = {6: "stage_b", 7: "stage_c"}
-WFILL = 8
 STORE_PIECE = 256
 WARM2 = 1
 T1AT = 12
@@ -70,7 +69,7 @@ def tile_pointnet_set_encoder_s12_kernel(tc, x, w, u_words, u_scales, v_words, v
         x_c = [sb([128, 512], U32, "x_c%d" % q) for q in range(8)]
         x_s = [sb([128, 512], U8, "x_s%d" % q) for q in range(8)]
         w_raw = {k: sb([128, 4, 512], BF16, "w_raw%d%d" % k) for k in quarters}
-        w_grp = {k: sb([128, 2048], BF16, "w_grp%d%d" % k) for k in quarters}
+        w_grp = {}
         w_c = {k: sb([128, 512], U32, "w_c%d%d" % k) for k in quarters}
         w_s = {k: sb([128, 512], U8, "w_s%d%d" % k) for k in quarters}
         e_grp = [sb([128, 4096], BF16, "e_grp%d" % nh) for nh in range(2)]
@@ -127,10 +126,21 @@ def tile_pointnet_set_encoder_s12_kernel(tc, x, w, u_words, u_scales, v_words, v
                 in_=u_pl_raw[32 * Q : 32 * Q + 4, :].bitcast(I32).rearrange("p (G q t) -> p G t q", G=2, q=32, t=4),
             )
 
-        def w_weave(g, G, q0=0, q1=32):
+        def w_tile(g, G):
+            if (g, G) not in w_grp:
+                w_grp[g, G] = sb([128, 2048], BF16, "w_grp_a" if g != G else "w_grp%d" % g)
+            return w_grp[g, G]
+
+        def w_weave_pool(g, G, t):
+            pool_copy(
+                w_tile(g, G)[:].rearrange("p (t q r j) -> p t q r j", t=4, q=32, r=4, j=4)[:, t],
+                w_raw[g, G][:].rearrange("p j (q t r) -> p t q r j", q=32, t=4, r=4)[:, t],
+            )
+
+        def w_weave(g, G, t0=0, t1=4):
             nc.vector.tensor_copy(
-                out=w_grp[g, G][:].rearrange("p (t q r j) -> p t q j r", t=4, q=32, r=4, j=4)[:, :, q0:q1],
-                in_=w_raw[g, G][:].rearrange("p j (q t r) -> p t q j r", q=32, t=4, r=4)[:, :, q0:q1],
+                out=w_tile(g, G)[:].rearrange("p (t q r j) -> p t q j r", t=4, q=32, r=4, j=4)[:, t0:t1],
+                in_=w_raw[g, G][:].rearrange("p j (q t r) -> p t q j r", q=32, t=4, r=4)[:, t0:t1],
             )
 
         def quantize(codes, scales, values, c0=0, n=512):
@@ -357,12 +367,13 @@ def tile_pointnet_set_encoder_s12_kernel(tc, x, w, u_words, u_scales, v_words, v
                 w_weave(1, 0)
                 w_quant(0, 0)
                 w_quant(1, 0)
+                w_weave_pool(0, 1, 3)
             if k == T1AT:
                 x_out(1, 0, XE[2])
                 x_out(1, 1, XE[3])
-        w_weave(0, 1, 0, WFILL)
+        w_weave(0, 1, 2, 3)
         x_quant(1)
-        w_weave(0, 1, WFILL, 32)
+        w_weave(0, 1, 0, 2)
         w_weave(1, 1)
         w_quant(0, 1)
         w_quant(1, 1)

@@ -17,27 +17,18 @@ MULT = mybir.AluOpType.mult
 ADD = mybir.AluOpType.add
 RELU = mybir.ActivationFunctionType.Relu
 
-NPE = 4
-NARROW = ((0, 1), (1, 0), (1, 1), (7, 0), (7, 1))
-WARM = 5
-XE = "VSVVVSSS"
-EV = ()
-W0AT = 0
+PAIRS = 8
+PE_PAIRS = 4
+LAST = PAIRS - 1
+POOL_SPLIT = (6, 7)
 POOL_ZIP = (2, 5, 6)
-STAGE_H = ("stage_a", "stage_b", "stage_b", "stage_c", "stage_a", "stage_a", "stage_a", "stage_c")
-STAGE_X = {6: "stage_b", 7: "stage_c"}
+NARROW = ((0, 1), (1, 0), (1, 1), (LAST, 0), (LAST, 1))
+WARM_UPS = 5
+E_BEFORE_PAIR_1 = 12
+OPENING = 4
 STORE_PIECE = 256
-WARM2 = 1
-T1AT = 12
-XQ0 = 0
-COUNT = "11111111111111113000"
-OPEN = 4
-E1 = 1
-E2 = 1
-E3 = 2
-E4 = 1
-A7 = 17
-BAT = "00000"
+H_BUFFER = ("stage_a", "stage_b", "stage_b", "stage_c", "stage_a", "stage_a", "stage_a", "stage_c")
+SPLIT_BUFFER = {6: "stage_b", 7: "stage_c"}
 
 
 def tile_pointnet_set_encoder_s12_kernel(tc, x, w, u_words, u_scales, v_words, v_scales, out):
@@ -56,7 +47,7 @@ def tile_pointnet_set_encoder_s12_kernel(tc, x, w, u_words, u_scales, v_words, v
             banks[key] = psum.tile(shape, F32, name="bank", tag="bank", bufs=8)
             return banks[key]
 
-        quarters = [(i, j) for i in range(2) for j in range(2)]
+        quarters = [(g, G) for g in range(2) for G in range(2)]
 
         u_raw = sb([128, 2048], U8, "u_raw")
         u_w = sb([128, 2048], U8, "u_w")
@@ -65,9 +56,9 @@ def tile_pointnet_set_encoder_s12_kernel(tc, x, w, u_words, u_scales, v_words, v
         v_w = sb([128, 2048], U8, "v_w")
         v_pl = sb([128, 1024], U8, "v_pl")
         ident = sb([128, 128], F32, "ident")
-        x_sb = [sb([128, 2048], BF16, "x_sb%d" % q) for q in range(4)]
-        x_c = [sb([128, 512], U32, "x_c%d" % q) for q in range(8)]
-        x_s = [sb([128, 512], U8, "x_s%d" % q) for q in range(8)]
+        x_sb = [sb([128, 2048], BF16, "x_sb%d" % q) for q in range(PE_PAIRS)]
+        x_c = [sb([128, 512], U32, "x_c%d" % q) for q in range(PAIRS)]
+        x_s = [sb([128, 512], U8, "x_s%d" % q) for q in range(PAIRS)]
         w_raw = {k: sb([128, 4, 512], BF16, "w_raw%d%d" % k) for k in quarters}
         w_grp = {}
         w_c = {k: sb([128, 512], U32, "w_c%d%d" % k) for k in quarters}
@@ -75,20 +66,17 @@ def tile_pointnet_set_encoder_s12_kernel(tc, x, w, u_words, u_scales, v_words, v
         e_grp = [sb([128, 4096], BF16, "e_grp%d" % nh) for nh in range(2)]
         e_c = [sb([128, 1024], U32, "e_c%d" % nh) for nh in range(2)]
         e_s = [sb([128, 1024], U8, "e_s%d" % nh) for nh in range(2)]
-        h_c = [sb([128, 512], U32, "h_c%d" % q) for q in range(8)]
-        h_s = [sb([128, 512], U8, "h_s%d" % q) for q in range(8)]
+        h_c = [sb([128, 512], U32, "h_c%d" % q) for q in range(PAIRS)]
+        h_s = [sb([128, 512], U8, "h_s%d" % q) for q in range(PAIRS)]
         acc = [sb([128, 1024], F32, "acc%d" % s) for s in range(2)]
+        x_quad = {q: sb([128, 2048], BF16, "x_quad%d" % q) for q in range(PE_PAIRS, PAIRS)}
 
-        us32 = u_scales[0].bitcast(I32)
-        vs32 = v_scales[0].bitcast(I32)
-        x_rows = x.rearrange("(s i b) k -> s i b k", s=2, i=128, b=8)
+        x_rows = x.rearrange("(s i b) k -> s i b k", s=2, i=128, b=8)[0]
+        x_rows_quad = x.rearrange("(s i m r) k -> s r i m k", s=2, i=32, r=4)[1]
         w_rows = w.rearrange("(g p j) f -> g p j f", g=2, p=128, j=4)
 
         def load_x(q):
-            nc.sync.dma_start(out=x_sb[q][:].rearrange("p (b k) -> p b k", b=2), in_=x_rows[0][:, 2 * q : 2 * q + 2, :])
-
-        x_quad = {q: sb([128, 2048], BF16, "x_quad%d" % q) for q in range(4, 8)}
-        x_rows_quad = x.rearrange("(s i m r) k -> s r i m k", s=2, i=32, r=4)[1]
+            nc.sync.dma_start(out=x_sb[q][:].rearrange("p (b k) -> p b k", b=2), in_=x_rows[:, 2 * q : 2 * q + 2, :])
 
         def load_x_quad(q):
             for g in range(2):
@@ -96,17 +84,17 @@ def tile_pointnet_set_encoder_s12_kernel(tc, x, w, u_words, u_scales, v_words, v
                     k0 = 512 * g + 128 * Q
                     nc.sync.dma_start(
                         out=x_quad[q][32 * Q : 32 * Q + 32, 1024 * g : 1024 * g + 1024].rearrange("p (m k) -> p m k", m=8),
-                        in_=x_rows_quad[q - 4][:, :, k0 : k0 + 128],
+                        in_=x_rows_quad[q - PE_PAIRS][:, :, k0 : k0 + 128],
                     )
 
         def load_w(g, G):
             nc.sync.dma_start(out=w_raw[g, G][:], in_=w_rows[g][:, :, 512 * G : 512 * G + 512])
 
-        def load_scales(engine, plane, rows, Q):
-            engine.dma_start(out=plane[32 * Q : 32 * Q + 4, :].bitcast(I32), in_=rows[4 * Q : 4 * Q + 4, :])
+        def load_scales(engine, plane, scales, Q):
+            engine.dma_start(out=plane[32 * Q : 32 * Q + 4, :].bitcast(I32), in_=scales[0].bitcast(I32)[4 * Q : 4 * Q + 4, :])
 
-        def copy(engine, out, in_):
-            if engine == "S":
+        def copy(on_scalar, out, in_):
+            if on_scalar:
                 nc.scalar.copy(out, in_)
             else:
                 nc.vector.tensor_copy(out=out, in_=in_)
@@ -114,28 +102,46 @@ def tile_pointnet_set_encoder_s12_kernel(tc, x, w, u_words, u_scales, v_words, v
         def pool_copy(out, in_):
             nc.gpsimd.tensor_scalar(out=out, in0=in_, scalar1=1.0, scalar2=0.0, op0=MULT, op1=ADD)
 
-        def permute_u():
-            nc.vector.tensor_copy(
-                out=u_w[:].bitcast(I32).rearrange("p (G t q r) -> p G t q r", G=2, t=4, q=32, r=2),
-                in_=u_raw[:].bitcast(I32).rearrange("p (G q t r) -> p G t q r", G=2, q=32, t=4, r=2),
+        def quantize(codes, scales, values, c0=0, n=512):
+            nc.vector.quantize_mx(
+                out=codes[:, c0 : c0 + n].bitcast(FP8X4), scales=scales[:, c0 : c0 + n], in_=values[:, 4 * c0 : 4 * (c0 + n)]
             )
 
-        def permute_u_scales(Q):
+        def deal_u_scales(Q):
             nc.vector.tensor_copy(
                 out=u_pl[32 * Q : 32 * Q + 4, :].bitcast(I32).rearrange("p (G t q) -> p G t q", G=2, t=4, q=32),
                 in_=u_pl_raw[32 * Q : 32 * Q + 4, :].bitcast(I32).rearrange("p (G q t) -> p G t q", G=2, q=32, t=4),
             )
 
+        def deal_u_words():
+            nc.vector.tensor_copy(
+                out=u_w[:].bitcast(I32).rearrange("p (G t q r) -> p G t q r", G=2, t=4, q=32, r=2),
+                in_=u_raw[:].bitcast(I32).rearrange("p (G q t r) -> p G t q r", G=2, q=32, t=4, r=2),
+            )
+
+        def e_bank(k):
+            G, nb = k // 4 % 2, k % 4 + k // 8 * 4
+            e = bank(("e", k), [128, 4, 128])
+            for t in range(4):
+                c0 = G * 512 + t * 128
+                nc.tensor.matmul_mx(
+                    out=e[:, t, :],
+                    lhsT=u_w[:, 2 * c0 : 2 * c0 + 256].bitcast(FP4X4), lhsT_scale=u_pl[:, c0 : c0 + 128],
+                    rhs=v_w[:, 256 * nb : 256 * nb + 256].bitcast(FP4X4), rhs_scale=v_pl[:, 128 * nb : 128 * nb + 128],
+                    start=t == 0, stop=t == 3,
+                )
+            j = k % 8
+            nc.scalar.copy(
+                e_grp[k // 8][:, 512 * j : 512 * j + 512].rearrange("p (n t) -> p n t", t=4), e[:].rearrange("p t n -> p n t")
+            )
+
+        def e_quant(nh):
+            quantize(e_c[nh], e_s[nh], e_grp[nh], 0, 1024)
+
         def w_tile(g, G):
             if (g, G) not in w_grp:
-                w_grp[g, G] = sb([128, 2048], BF16, "w_grp_a" if g != G else "w_grp%d" % g)
+                w_grp[g, G] = sb([128, 2048], BF16, "w_grp%d" % g if g == G else "w_grp_a")
             return w_grp[g, G]
-
-        def w_weave_pool(g, G, t):
-            pool_copy(
-                w_tile(g, G)[:].rearrange("p (t q r j) -> p t q r j", t=4, q=32, r=4, j=4)[:, t],
-                w_raw[g, G][:].rearrange("p j (q t r) -> p t q r j", q=32, t=4, r=4)[:, t],
-            )
 
         def w_weave(g, G, t0=0, t1=4):
             nc.vector.tensor_copy(
@@ -143,36 +149,14 @@ def tile_pointnet_set_encoder_s12_kernel(tc, x, w, u_words, u_scales, v_words, v
                 in_=w_raw[g, G][:].rearrange("p j (q t r) -> p t q j r", q=32, t=4, r=4)[:, t0:t1],
             )
 
-        def quantize(codes, scales, values, c0=0, n=512):
-            nc.vector.quantize_mx(
-                out=codes[:, c0 : c0 + n].bitcast(FP8X4), scales=scales[:, c0 : c0 + n], in_=values[:, 4 * c0 : 4 * (c0 + n)]
+        def w_weave_pool(g, G, t):
+            pool_copy(
+                w_tile(g, G)[:].rearrange("p (t q r j) -> p t q r j", t=4, q=32, r=4, j=4)[:, t],
+                w_raw[g, G][:].rearrange("p j (q t r) -> p t q r j", q=32, t=4, r=4)[:, t],
             )
 
         def w_quant(g, G):
             quantize(w_c[g, G], w_s[g, G], w_grp[g, G])
-
-        def e_quant(nh):
-            quantize(e_c[nh], e_s[nh], e_grp[nh], 0, 1024)
-
-        def e_mm(k):
-            G, nb = k // 4 % 2, k % 4 + k // 8 * 4
-            bank(("e", k), [128, 4, 128])
-            for t in range(4):
-                c0 = G * 512 + t * 128
-                nc.tensor.matmul_mx(
-                    out=banks["e", k][:, t, :],
-                    lhsT=u_w[:, 2 * c0 : 2 * c0 + 256].bitcast(FP4X4), lhsT_scale=u_pl[:, c0 : c0 + 128],
-                    rhs=v_w[:, 256 * nb : 256 * nb + 256].bitcast(FP4X4), rhs_scale=v_pl[:, 128 * nb : 128 * nb + 128],
-                    start=t == 0, stop=t == 3,
-                )
-
-        def e_out(k, engine):
-            j = k % 8
-            copy(
-                engine,
-                e_grp[k // 8][:, 512 * j : 512 * j + 512].rearrange("p (n t) -> p n t", t=4),
-                banks["e", k][:].rearrange("p t n -> p n t"),
-            )
 
         x_g = {}
         x_r = {}
@@ -186,25 +170,28 @@ def tile_pointnet_set_encoder_s12_kernel(tc, x, w, u_words, u_scales, v_words, v
                     for u in range(2):
                         nc.tensor.transpose(xt[:, g, u, :], x_sb[q][:].bitcast(F32)[:, base + u : base + 256 : 2], ident[:])
 
-        def x_out(q, b, engine):
-            if q not in x_g:
-                x_g[q] = sb([128, 2048], BF16, "x_g", 3)
-            copy(
-                engine,
-                x_g[q][:].bitcast(F32).rearrange("p (g b n u) -> p b g n u", g=2, b=2, u=2)[:, b],
-                banks["x", q, b][:].rearrange("p g u n -> p g n u"),
-            )
+        def x_out(q, units_on_vector):
+            x_g[q] = sb([128, 2048], BF16, "x_g", 3)
+            for b in range(2):
+                copy(
+                    b >= units_on_vector,
+                    x_g[q][:].bitcast(F32).rearrange("p (g b n u) -> p b g n u", g=2, b=2, u=2)[:, b],
+                    banks["x", q, b][:].rearrange("p g u n -> p g n u"),
+                )
 
         def x_split(q):
-            x_r[q] = sb([128, 2048], BF16, STAGE_X.get(q, "x_r"))
-            if q <= 5:
-                copy("V", x_r[q][:].bitcast(F32).rearrange("p (u n) -> p u n", u=2), x_quad[q][:].bitcast(F32).rearrange("p (n u) -> p u n", u=2))
-            else:
+            x_r[q] = sb([128, 2048], BF16, SPLIT_BUFFER.get(q, "x_r"))
+            if q in POOL_SPLIT:
                 for g in range(2):
                     pool_copy(
                         x_r[q][:].rearrange("p (u g n e) -> p g u n e", u=2, g=2, e=2)[:, g],
                         x_quad[q][:, 1024 * g : 1024 * g + 1024].rearrange("p (n u e) -> p u n e", u=2, e=2),
                     )
+            else:
+                nc.vector.tensor_copy(
+                    out=x_r[q][:].bitcast(F32).rearrange("p (u n) -> p u n", u=2),
+                    in_=x_quad[q][:].bitcast(F32).rearrange("p (n u) -> p u n", u=2),
+                )
 
         def x_turn(q):
             x_t[q] = sb([128, 1024], F32, "x_t", 2)
@@ -212,12 +199,11 @@ def tile_pointnet_set_encoder_s12_kernel(tc, x, w, u_words, u_scales, v_words, v
 
         def x_join(q):
             x_g[q] = sb([128, 2048], BF16, "x_g", 3)
-            if q < 7:
-                copy("S", x_g[q][:].bitcast(F32).rearrange("p (n u) -> p n u", u=2), x_t[q][:].rearrange("p (u n) -> p n u", u=2))
+            if q < LAST:
+                nc.scalar.copy(x_g[q][:].bitcast(F32).rearrange("p (n u) -> p n u", u=2), x_t[q][:].rearrange("p (u n) -> p n u", u=2))
             else:
                 for g in range(2):
-                    copy(
-                        "S",
+                    nc.scalar.copy(
                         x_g[q][:].bitcast(F32).rearrange("p (g b c i u) -> p g b c i u", g=2, b=2, c=4, u=2)[:, g],
                         x_t[q][:].rearrange("p (u g c b i) -> p g b c i u", u=2, g=2, b=2, c=4)[:, g],
                     )
@@ -226,28 +212,28 @@ def tile_pointnet_set_encoder_s12_kernel(tc, x, w, u_words, u_scales, v_words, v
             quantize(x_c[q], x_s[q], x_g[q])
 
         h_t = {}
-        h_half = {}
+        h_two = {}
 
         def wide(q, G):
             return (q, G) not in NARROW
 
         def part(q, b, G):
-            return 2 * b + G if q == 7 else 2 * G + b
+            return 2 * b + G if q == LAST else 2 * G + b
 
         def h_tile(q):
             if q not in h_t:
-                h_t[q] = sb([128, 2048], BF16, STAGE_H[q])
+                h_t[q] = sb([128, 2048], BF16, H_BUFFER[q])
             return h_t[q]
 
         def first(q, G, j):
             n = 256 if wide(q, G) else 128
             h = bank(("h", q, G, j), [128, 512 // n, n])
-            for tt in range(512 // n):
-                t = 2 * j + tt if n == 256 else tt
+            for a in range(512 // n):
+                t = 2 * j + a if wide(q, G) else a
                 for g in range(2):
-                    k0 = 256 * g if n == 256 else 256 * g + 128 * j
+                    k0 = 256 * g if wide(q, G) else 256 * g + 128 * j
                     nc.tensor.matmul_mx(
-                        out=h[:, tt, :],
+                        out=h[:, a, :],
                         lhsT=w_c[g, G][:, 128 * t : 128 * t + 128].bitcast(FP8X4),
                         lhsT_scale=w_s[g, G][:, 128 * t : 128 * t + 128],
                         rhs=x_c[q][:, k0 : k0 + n].bitcast(FP8X4), rhs_scale=x_s[q][:, k0 : k0 + n],
@@ -257,42 +243,38 @@ def tile_pointnet_set_encoder_s12_kernel(tc, x, w, u_words, u_scales, v_words, v
         def h_out(q, G, j):
             src = banks["h", q, G, j][:]
             if wide(q, G):
-                if q not in h_half:
-                    h_half[q] = sb([128, 2048], BF16, "h_half", 3)
-                dst = h_half[q][:, 1024 * G + 512 * j : 1024 * G + 512 * j + 512]
-                if q < NPE:
-                    dst, src = dst.rearrange("p (n e) -> p n e", e=2), src.rearrange("p e n -> p n e")
-                else:
+                if q not in h_two:
+                    h_two[q] = sb([128, 2048], BF16, "h_two", 3)
+                dst = h_two[q][:, 1024 * G + 512 * j : 1024 * G + 512 * j + 512]
+                if q >= PE_PAIRS:
                     dst, src = dst.rearrange("p (a c e) -> p a c e", c=4, e=2), src.rearrange("p e (c a) -> p a c e", c=4)
+                else:
+                    dst, src = dst.rearrange("p (n e) -> p n e", e=2), src.rearrange("p e n -> p n e")
             else:
                 dst = h_tile(q)[:, 512 * part(q, j, G) : 512 * part(q, j, G) + 512]
-                if q < NPE:
-                    dst, src = dst.rearrange("p (n t) -> p n t", t=4), src.rearrange("p t n -> p n t")
-                elif q == 7:
+                if q == LAST:
                     dst, src = dst.rearrange("p (i c t) -> p i c t", c=4, t=4), src.rearrange("p t (c i) -> p i c t", c=4)
                 else:
-                    dst = h_tile(q)[:, 1024 * G : 1024 * G + 1024].rearrange("p (a j c t) -> p j a c t", j=2, c=2, t=4)[:, j]
-                    src = src.rearrange("p t (c a) -> p a c t", c=2)
+                    dst, src = dst.rearrange("p (n t) -> p n t", t=4), src.rearrange("p t n -> p n t")
             nc.scalar.activation(out=dst, in_=src, func=RELU)
 
-        def h_zip_pool(q):
-            pool_copy(
-                h_tile(q)[:, 0:1024].rearrange("p (c u e) -> p c u e", u=2, e=2),
-                h_half[q][:, 0:1024].rearrange("p (u c e) -> p c u e", u=2, e=2),
+        def zip_first_vector(q):
+            nc.vector.tensor_copy(
+                out=h_tile(q)[:, 0:1024].bitcast(F32).rearrange("p (n i u) -> p n u i", i=2, u=2),
+                in_=h_two[q][:, 0:1024].bitcast(F32).rearrange("p (u n i) -> p n u i", i=2, u=2),
             )
 
-        def h_zip_front(q):
-            if wide(q, 0):
-                nc.vector.tensor_copy(
-                    out=h_tile(q)[:, 0:1024].bitcast(F32).rearrange("p (n i u) -> p n u i", i=2, u=2),
-                    in_=h_half[q][:, 0:1024].bitcast(F32).rearrange("p (u n i) -> p n u i", i=2, u=2),
-                )
+        def zip_first_pool(q):
+            pool_copy(
+                h_tile(q)[:, 0:1024].rearrange("p (c u e) -> p c u e", u=2, e=2),
+                h_two[q][:, 0:1024].rearrange("p (u c e) -> p c u e", u=2, e=2),
+            )
 
-        def h_zip(q):
-            G0 = 1 if q in POOL_ZIP else 0
+        def zip_rest(q):
+            c0 = 1024 if q in POOL_ZIP else 0
             nc.scalar.copy(
-                h_tile(q)[:, 1024 * G0 :].bitcast(F32).rearrange("p (G n i u) -> p G n u i", n=128, i=2, u=2),
-                h_half[q][:, 1024 * G0 :].bitcast(F32).rearrange("p (G u n i) -> p G n u i", n=128, i=2, u=2),
+                h_tile(q)[:, c0:].bitcast(F32).rearrange("p (G n i u) -> p G n u i", n=128, i=2, u=2),
+                h_two[q][:, c0:].bitcast(F32).rearrange("p (G u n i) -> p G n u i", n=128, i=2, u=2),
             )
 
         def h_quant(q, c0=0, n=512):
@@ -303,15 +285,13 @@ def tile_pointnet_set_encoder_s12_kernel(tc, x, w, u_words, u_scales, v_words, v
             nh, j0 = n0 // 512, n0 % 512
             for G in range(2):
                 k = slice(128 * part(m // 2, m % 2, G), 128 * part(m // 2, m % 2, G) + 128)
+                c = slice(512 * G + j0, 512 * G + j0 + n)
                 nc.tensor.matmul_mx(
                     out=y[:],
                     lhsT=h_c[m // 2][:, k].bitcast(FP8X4), lhsT_scale=h_s[m // 2][:, k],
-                    rhs=e_c[nh][:, 512 * G + j0 : 512 * G + j0 + n].bitcast(FP8X4), rhs_scale=e_s[nh][:, 512 * G + j0 : 512 * G + j0 + n],
+                    rhs=e_c[nh][:, c].bitcast(FP8X4), rhs_scale=e_s[nh][:, c],
                     start=G == 0, stop=G == 1,
                 )
-
-        def y_out(m, n0, n=512):
-            y = banks["y", m, n0]
             s = m // 8
             a = acc[s][:, n0 : n0 + n]
             if m % 8 == 0:
@@ -321,6 +301,12 @@ def tile_pointnet_set_encoder_s12_kernel(tc, x, w, u_words, u_scales, v_words, v
             if m % 8 == 7:
                 nc.sync.dma_start(out=out[128 * s : 128 * s + 128, n0 : n0 + n], in_=a)
 
+        waiting = [(m, n0) for m in range(15) for n0 in (0, 512)]
+
+        def seconds(count):
+            for i in range(count):
+                second(*waiting.pop(0))
+
         nc.vector.memset(ident[:], 0.0)
         zero = sb([128, 512], BF16, "zero")
         nc.vector.memset(zero[:].bitcast(I32), 0)
@@ -328,12 +314,12 @@ def tile_pointnet_set_encoder_s12_kernel(tc, x, w, u_words, u_scales, v_words, v
         nc.vector.memset(u_pl[:].bitcast(I32), 0)
         make_identity(nc, ident[:], nomemset=True)
         for Q in range(4):
-            load_scales(nc.scalar if Q % 2 else nc.sync, u_pl_raw, us32, Q)
+            load_scales(nc.scalar if Q % 2 else nc.sync, u_pl_raw, u_scales, Q)
         load_x(0)
         nc.sync.dma_start(out=u_raw[:].bitcast(I32), in_=u_words[0].bitcast(I32))
         nc.sync.dma_start(out=v_w[:].bitcast(I32), in_=v_words[0].bitcast(I32))
         for Q in range(4):
-            load_scales(nc.sync, v_pl, vs32, Q)
+            load_scales(nc.sync, v_pl, v_scales, Q)
         load_w(0, 0)
         load_w(1, 0)
         load_x(1)
@@ -341,36 +327,31 @@ def tile_pointnet_set_encoder_s12_kernel(tc, x, w, u_words, u_scales, v_words, v
         load_w(1, 1)
         load_x(2)
         load_x(3)
-        for q in range(4, 8):
+        for q in range(PE_PAIRS, PAIRS):
             load_x_quad(q)
 
         warm = bank("warm", [128, 512])
-        for i in range(WARM):
+        for i in range(WARM_UPS):
             nc.tensor.matmul(warm[:], lhsT=zero[:, 0:128], rhs=zero[:], start=True, stop=True)
         x_transpose(0)
-        for i in range(WARM2):
-            nc.tensor.matmul(warm[:], lhsT=zero[:, 0:128], rhs=zero[:], start=True, stop=True)
+        nc.tensor.matmul(warm[:], lhsT=zero[:, 0:128], rhs=zero[:], start=True, stop=True)
+
         for Q in range(4):
-            permute_u_scales(Q)
-        permute_u()
-        x_out(0, 0, XE[0])
-        x_out(0, 1, XE[1])
-        for k in range(16):
-            if k == T1AT:
-                x_transpose(1)
-            e_mm(k)
-            e_out(k, "V" if k in EV else "S")
-            if k == XQ0:
-                x_quant(0)
-            if k == W0AT:
-                w_weave(0, 0)
-                w_weave(1, 0)
-                w_quant(0, 0)
-                w_quant(1, 0)
-                w_weave_pool(0, 1, 3)
-            if k == T1AT:
-                x_out(1, 0, XE[2])
-                x_out(1, 1, XE[3])
+            deal_u_scales(Q)
+        deal_u_words()
+        x_out(0, 1)
+        x_quant(0)
+        w_weave(0, 0)
+        w_weave(1, 0)
+        w_quant(0, 0)
+        w_quant(1, 0)
+        w_weave_pool(0, 1, 3)
+        for k in range(E_BEFORE_PAIR_1):
+            e_bank(k)
+        x_transpose(1)
+        x_out(1, 2)
+        for k in range(E_BEFORE_PAIR_1, 16):
+            e_bank(k)
         w_weave(0, 1, 2, 3)
         x_quant(1)
         w_weave(0, 1, 0, 2)
@@ -381,77 +362,74 @@ def tile_pointnet_set_encoder_s12_kernel(tc, x, w, u_words, u_scales, v_words, v
             for j in range(2):
                 first(q, 0, j)
                 h_out(q, 0, j)
-        for q in range(2, 4):
-            x_transpose(q)
-            x_out(q, 0, XE[2 * q])
-            x_out(q, 1, XE[2 * q + 1])
-        e_quant(0)
+        x_transpose(2)
+        x_out(2, 2)
+        x_transpose(3)
+        x_out(3, 0)
+        zip_first_vector(0)
         x_quant(2)
+        e_quant(0)
         for q in range(2):
             for j in range(2):
                 first(q, 1, j)
                 h_out(q, 1, j)
-        h_zip_front(0)
         e_quant(1)
         h_quant(0)
-        h_zip_front(1)
         x_quant(3)
         x_split(4)
         h_quant(1)
         x_turn(4)
 
-        todo = [(m, n0) for m in range(15) for n0 in (0, 512)]
-
-        def seconds(n):
-            for i in range(n):
-                second(*todo[0])
-                y_out(*todo.pop(0))
-
-        def behind(q):
-            if q == 2:
-                x_split(5)
-            if q + 2 < 8:
-                x_quant(q + 2)
-            h_quant(q)
-            if q + 4 < 8:
-                x_split(q + 4)
-            if q + 3 < 8:
-                x_turn(q + 3)
-
         for j in range(2):
             first(2, 0, j)
             h_out(2, 0, j)
-        h_zip_pool(2)
+        zip_first_pool(2)
         for j in range(2):
             first(2, 1, j)
-        seconds(OPEN)
+        seconds(OPENING)
         for j in range(2):
             h_out(2, 1, j)
         x_join(4)
-        h_zip(2)
-        slots = [(q, G, j) for q in range(3, 7) for G in range(2) for j in range(2)] + [(7, G, j) for j in range(2) for G in range(2)]
-        for slot, (q, G, j) in enumerate(slots):
-            first(q, G, j)
-            seconds(int(COUNT[slot]))
-            h_out(q, G, j)
-            if (G, j) == (0, 1) and q in POOL_ZIP:
-                h_zip_pool(q)
-            if slot % 4 == int(BAT[q - 3]):
-                behind(q - 1)
-                seconds(E1 if q == 7 else 0)
-            if slot % 4 == 3 and q < 7:
-                if q + 2 < 8:
-                    x_join(q + 2)
-                h_zip(q)
-            if slot == A7:
-                h_quant(7, 0, 256)
-            if slot == 18:
-                seconds(E2)
-                h_quant(7, 256, 128)
-                seconds(E3)
-        seconds(E4)
-        h_quant(7, 384, 128)
-        seconds(len(todo))
+        zip_rest(2)
+
+        for q in range(3, LAST):
+            for G in range(2):
+                for j in range(2):
+                    first(q, G, j)
+                    seconds(1)
+                    h_out(q, G, j)
+                    if (G, j) == (0, 0):
+                        if q + 2 < POOL_SPLIT[0]:
+                            x_split(q + 2)
+                        x_quant(q + 1)
+                        h_quant(q - 1)
+                        if q + 3 in POOL_SPLIT:
+                            x_split(q + 3)
+                        if q + 2 < PAIRS:
+                            x_turn(q + 2)
+                    if (G, j) == (0, 1) and q in POOL_ZIP:
+                        zip_first_pool(q)
+            if q + 2 < PAIRS:
+                x_join(q + 2)
+            zip_rest(q)
+
+        first(LAST, 0, 0)
+        seconds(3)
+        h_out(LAST, 0, 0)
+        h_quant(LAST - 1)
+        seconds(1)
+        first(LAST, 1, 0)
+        h_out(LAST, 1, 0)
+        h_quant(LAST, 0, 256)
+        first(LAST, 0, 1)
+        h_out(LAST, 0, 1)
+        seconds(1)
+        h_quant(LAST, 256, 128)
+        seconds(2)
+        first(LAST, 1, 1)
+        h_out(LAST, 1, 1)
+        seconds(1)
+        h_quant(LAST, 384, 128)
+        seconds(2)
         for n0 in range(0, 1024, STORE_PIECE):
             second(15, n0, STORE_PIECE)
-            y_out(15, n0, STORE_PIECE)

from contextlib import ExitStack

import concourse.mybir as mybir
from concourse.masks import make_identity

FLOPS = 2 * 2048 * 1024 * 1024 * 2 + 2 * 512 * 1024 * 1024

F32 = mybir.dt.float32
BF16 = mybir.dt.bfloat16
I32 = mybir.dt.int32
U32 = mybir.dt.uint32
U8 = mybir.dt.uint8
FP8X4 = mybir.dt.float8_e4m3fn_x4
FP4X4 = mybir.dt.float4_e2m1fn_x4
MAX = mybir.AluOpType.max
MULT = mybir.AluOpType.mult
ADD = mybir.AluOpType.add
RELU = mybir.ActivationFunctionType.Relu

PAIRS = 8
PE_PAIRS = 4
LAST = PAIRS - 1
POOL_SPLIT = (6, 7)
POOL_ZIP = (2, 5, 6)
NARROW = ((0, 1), (1, 0), (1, 1), (LAST, 0), (LAST, 1))
WARM_UPS = 5
E_BEFORE_PAIR_1 = 12
OPENING = 4
STORE_PIECE = 256
H_BUFFER = ("stage_a", "stage_b", "stage_b", "stage_c", "stage_a", "stage_a", "stage_a", "stage_c")
SPLIT_BUFFER = {6: "stage_b", 7: "stage_c"}


def tile_pointnet_set_encoder_s12_kernel(tc, x, w, u_words, u_scales, v_words, v_scales, out):
    nc = tc.nc
    with ExitStack() as ctx:
        keep = ctx.enter_context(tc.tile_pool(name="keep", bufs=1))
        psum = ctx.enter_context(tc.psum_pool(name="psum", bufs=1))
        ctx.enter_context(tc.manual_schedule())

        def sb(shape, dtype, tag, bufs=1):
            return keep.tile(shape, dtype, name=tag, tag=tag, bufs=bufs, align_bytes=256)

        banks = {}

        def bank(key, shape):
            banks[key] = psum.tile(shape, F32, name="bank", tag="bank", bufs=8)
            return banks[key]

        quarters = [(g, G) for g in range(2) for G in range(2)]

        u_raw = sb([128, 2048], U8, "u_raw")
        u_w = sb([128, 2048], U8, "u_w")
        u_pl_raw = sb([128, 1024], U8, "u_pl_raw")
        u_pl = sb([128, 1024], U8, "u_pl")
        v_w = sb([128, 2048], U8, "v_w")
        v_pl = sb([128, 1024], U8, "v_pl")
        ident = sb([128, 128], F32, "ident")
        x_sb = [sb([128, 2048], BF16, "x_sb%d" % q) for q in range(PE_PAIRS)]
        x_c = [sb([128, 512], U32, "x_c%d" % q) for q in range(PAIRS)]
        x_s = [sb([128, 512], U8, "x_s%d" % q) for q in range(PAIRS)]
        w_raw = {k: sb([128, 4, 512], BF16, "w_raw%d%d" % k) for k in quarters}
        w_grp = {}
        w_c = {k: sb([128, 512], U32, "w_c%d%d" % k) for k in quarters}
        w_s = {k: sb([128, 512], U8, "w_s%d%d" % k) for k in quarters}
        e_grp = [sb([128, 4096], BF16, "e_grp%d" % nh) for nh in range(2)]
        e_c = [sb([128, 1024], U32, "e_c%d" % nh) for nh in range(2)]
        e_s = [sb([128, 1024], U8, "e_s%d" % nh) for nh in range(2)]
        h_c = [sb([128, 512], U32, "h_c%d" % q) for q in range(PAIRS)]
        h_s = [sb([128, 512], U8, "h_s%d" % q) for q in range(PAIRS)]
        acc = [sb([128, 1024], F32, "acc%d" % s) for s in range(2)]
        x_quad = {q: sb([128, 2048], BF16, "x_quad%d" % q) for q in range(PE_PAIRS, PAIRS)}

        x_rows = x.rearrange("(s i b) k -> s i b k", s=2, i=128, b=8)[0]
        x_rows_quad = x.rearrange("(s i m r) k -> s r i m k", s=2, i=32, r=4)[1]
        w_rows = w.rearrange("(g p j) f -> g p j f", g=2, p=128, j=4)

        def load_x(q):
            nc.sync.dma_start(out=x_sb[q][:].rearrange("p (b k) -> p b k", b=2), in_=x_rows[:, 2 * q : 2 * q + 2, :])

        def load_x_quad(q):
            for g in range(2):
                for Q in (0, 2, 1, 3):
                    k0 = 512 * g + 128 * Q
                    nc.sync.dma_start(
                        out=x_quad[q][32 * Q : 32 * Q + 32, 1024 * g : 1024 * g + 1024].rearrange("p (m k) -> p m k", m=8),
                        in_=x_rows_quad[q - PE_PAIRS][:, :, k0 : k0 + 128],
                    )

        def load_w(g, G):
            nc.sync.dma_start(out=w_raw[g, G][:], in_=w_rows[g][:, :, 512 * G : 512 * G + 512])

        def load_scales(engine, plane, scales, Q):
            engine.dma_start(out=plane[32 * Q : 32 * Q + 4, :].bitcast(I32), in_=scales[0].bitcast(I32)[4 * Q : 4 * Q + 4, :])

        def copy(on_scalar, out, in_):
            if on_scalar:
                nc.scalar.copy(out, in_)
            else:
                nc.vector.tensor_copy(out=out, in_=in_)

        def pool_copy(out, in_):
            nc.gpsimd.tensor_scalar(out=out, in0=in_, scalar1=1.0, scalar2=0.0, op0=MULT, op1=ADD)

        def quantize(codes, scales, values, c0=0, n=512):
            nc.vector.quantize_mx(
                out=codes[:, c0 : c0 + n].bitcast(FP8X4), scales=scales[:, c0 : c0 + n], in_=values[:, 4 * c0 : 4 * (c0 + n)]
            )

        def deal_u_scales(Q):
            nc.vector.tensor_copy(
                out=u_pl[32 * Q : 32 * Q + 4, :].bitcast(I32).rearrange("p (G t q) -> p G t q", G=2, t=4, q=32),
                in_=u_pl_raw[32 * Q : 32 * Q + 4, :].bitcast(I32).rearrange("p (G q t) -> p G t q", G=2, q=32, t=4),
            )

        def deal_u_words():
            nc.vector.tensor_copy(
                out=u_w[:].bitcast(I32).rearrange("p (G t q r) -> p G t q r", G=2, t=4, q=32, r=2),
                in_=u_raw[:].bitcast(I32).rearrange("p (G q t r) -> p G t q r", G=2, q=32, t=4, r=2),
            )

        def e_bank(k):
            G, nb = k // 4 % 2, k % 4 + k // 8 * 4
            e = bank(("e", k), [128, 4, 128])
            for t in range(4):
                c0 = G * 512 + t * 128
                nc.tensor.matmul_mx(
                    out=e[:, t, :],
                    lhsT=u_w[:, 2 * c0 : 2 * c0 + 256].bitcast(FP4X4), lhsT_scale=u_pl[:, c0 : c0 + 128],
                    rhs=v_w[:, 256 * nb : 256 * nb + 256].bitcast(FP4X4), rhs_scale=v_pl[:, 128 * nb : 128 * nb + 128],
                    start=t == 0, stop=t == 3,
                )
            j = k % 8
            nc.scalar.copy(
                e_grp[k // 8][:, 512 * j : 512 * j + 512].rearrange("p (n t) -> p n t", t=4), e[:].rearrange("p t n -> p n t")
            )

        def e_quant(nh):
            quantize(e_c[nh], e_s[nh], e_grp[nh], 0, 1024)

        def w_tile(g, G):
            if (g, G) not in w_grp:
                w_grp[g, G] = sb([128, 2048], BF16, "w_grp%d" % g if g == G else "w_grp_a")
            return w_grp[g, G]

        def w_weave(g, G, t0=0, t1=4):
            nc.vector.tensor_copy(
                out=w_tile(g, G)[:].rearrange("p (t q r j) -> p t q j r", t=4, q=32, r=4, j=4)[:, t0:t1],
                in_=w_raw[g, G][:].rearrange("p j (q t r) -> p t q j r", q=32, t=4, r=4)[:, t0:t1],
            )

        def w_weave_pool(g, G, t):
            pool_copy(
                w_tile(g, G)[:].rearrange("p (t q r j) -> p t q r j", t=4, q=32, r=4, j=4)[:, t],
                w_raw[g, G][:].rearrange("p j (q t r) -> p t q r j", q=32, t=4, r=4)[:, t],
            )

        def w_quant(g, G):
            quantize(w_c[g, G], w_s[g, G], w_grp[g, G])

        x_g = {}
        x_r = {}
        x_t = {}

        def x_transpose(q):
            for b in range(2):
                xt = bank(("x", q, b), [128, 2, 2, 128])
                for g in range(2):
                    base = b * 512 + g * 256
                    for u in range(2):
                        nc.tensor.transpose(xt[:, g, u, :], x_sb[q][:].bitcast(F32)[:, base + u : base + 256 : 2], ident[:])

        def x_out(q, units_on_vector):
            x_g[q] = sb([128, 2048], BF16, "x_g", 3)
            for b in range(2):
                copy(
                    b >= units_on_vector,
                    x_g[q][:].bitcast(F32).rearrange("p (g b n u) -> p b g n u", g=2, b=2, u=2)[:, b],
                    banks["x", q, b][:].rearrange("p g u n -> p g n u"),
                )

        def x_split(q):
            x_r[q] = sb([128, 2048], BF16, SPLIT_BUFFER.get(q, "x_r"))
            if q in POOL_SPLIT:
                for g in range(2):
                    pool_copy(
                        x_r[q][:].rearrange("p (u g n e) -> p g u n e", u=2, g=2, e=2)[:, g],
                        x_quad[q][:, 1024 * g : 1024 * g + 1024].rearrange("p (n u e) -> p u n e", u=2, e=2),
                    )
            else:
                nc.vector.tensor_copy(
                    out=x_r[q][:].bitcast(F32).rearrange("p (u n) -> p u n", u=2),
                    in_=x_quad[q][:].bitcast(F32).rearrange("p (n u) -> p u n", u=2),
                )

        def x_turn(q):
            x_t[q] = sb([128, 1024], F32, "x_t", 2)
            nc.vector.transpose(x_t[q][:], x_r[q][:].bitcast(F32))

        def x_join(q):
            x_g[q] = sb([128, 2048], BF16, "x_g", 3)
            if q < LAST:
                nc.scalar.copy(x_g[q][:].bitcast(F32).rearrange("p (n u) -> p n u", u=2), x_t[q][:].rearrange("p (u n) -> p n u", u=2))
            else:
                for g in range(2):
                    nc.scalar.copy(
                        x_g[q][:].bitcast(F32).rearrange("p (g b c i u) -> p g b c i u", g=2, b=2, c=4, u=2)[:, g],
                        x_t[q][:].rearrange("p (u g c b i) -> p g b c i u", u=2, g=2, b=2, c=4)[:, g],
                    )

        def x_quant(q):
            quantize(x_c[q], x_s[q], x_g[q])

        h_t = {}
        h_two = {}

        def wide(q, G):
            return (q, G) not in NARROW

        def part(q, b, G):
            return 2 * b + G if q == LAST else 2 * G + b

        def h_tile(q):
            if q not in h_t:
                h_t[q] = sb([128, 2048], BF16, H_BUFFER[q])
            return h_t[q]

        def first(q, G, j):
            n = 256 if wide(q, G) else 128
            h = bank(("h", q, G, j), [128, 512 // n, n])
            for a in range(512 // n):
                t = 2 * j + a if wide(q, G) else a
                for g in range(2):
                    k0 = 256 * g if wide(q, G) else 256 * g + 128 * j
                    nc.tensor.matmul_mx(
                        out=h[:, a, :],
                        lhsT=w_c[g, G][:, 128 * t : 128 * t + 128].bitcast(FP8X4),
                        lhsT_scale=w_s[g, G][:, 128 * t : 128 * t + 128],
                        rhs=x_c[q][:, k0 : k0 + n].bitcast(FP8X4), rhs_scale=x_s[q][:, k0 : k0 + n],
                        start=g == 0, stop=g == 1,
                    )

        def h_out(q, G, j):
            src = banks["h", q, G, j][:]
            if wide(q, G):
                if q not in h_two:
                    h_two[q] = sb([128, 2048], BF16, "h_two", 3)
                dst = h_two[q][:, 1024 * G + 512 * j : 1024 * G + 512 * j + 512]
                if q >= PE_PAIRS:
                    dst, src = dst.rearrange("p (a c e) -> p a c e", c=4, e=2), src.rearrange("p e (c a) -> p a c e", c=4)
                else:
                    dst, src = dst.rearrange("p (n e) -> p n e", e=2), src.rearrange("p e n -> p n e")
            else:
                dst = h_tile(q)[:, 512 * part(q, j, G) : 512 * part(q, j, G) + 512]
                if q == LAST:
                    dst, src = dst.rearrange("p (i c t) -> p i c t", c=4, t=4), src.rearrange("p t (c i) -> p i c t", c=4)
                else:
                    dst, src = dst.rearrange("p (n t) -> p n t", t=4), src.rearrange("p t n -> p n t")
            nc.scalar.activation(out=dst, in_=src, func=RELU)

        def zip_first_vector(q):
            nc.vector.tensor_copy(
                out=h_tile(q)[:, 0:1024].bitcast(F32).rearrange("p (n i u) -> p n u i", i=2, u=2),
                in_=h_two[q][:, 0:1024].bitcast(F32).rearrange("p (u n i) -> p n u i", i=2, u=2),
            )

        def zip_first_pool(q):
            pool_copy(
                h_tile(q)[:, 0:1024].rearrange("p (c u e) -> p c u e", u=2, e=2),
                h_two[q][:, 0:1024].rearrange("p (u c e) -> p c u e", u=2, e=2),
            )

        def zip_rest(q):
            c0 = 1024 if q in POOL_ZIP else 0
            nc.scalar.copy(
                h_tile(q)[:, c0:].bitcast(F32).rearrange("p (G n i u) -> p G n u i", n=128, i=2, u=2),
                h_two[q][:, c0:].bitcast(F32).rearrange("p (G u n i) -> p G n u i", n=128, i=2, u=2),
            )

        def h_quant(q, c0=0, n=512):
            quantize(h_c[q], h_s[q], h_t[q], c0, n)

        def second(m, n0, n=512):
            y = bank(("y", m, n0), [128, n])
            nh, j0 = n0 // 512, n0 % 512
            for G in range(2):
                k = slice(128 * part(m // 2, m % 2, G), 128 * part(m // 2, m % 2, G) + 128)
                c = slice(512 * G + j0, 512 * G + j0 + n)
                nc.tensor.matmul_mx(
                    out=y[:],
                    lhsT=h_c[m // 2][:, k].bitcast(FP8X4), lhsT_scale=h_s[m // 2][:, k],
                    rhs=e_c[nh][:, c].bitcast(FP8X4), rhs_scale=e_s[nh][:, c],
                    start=G == 0, stop=G == 1,
                )
            s = m // 8
            a = acc[s][:, n0 : n0 + n]
            if m % 8 == 0:
                nc.scalar.activation(out=a, in_=y[:], func=RELU)
            else:
                nc.vector.tensor_tensor(out=a, in0=y[:], in1=a, op=MAX)
            if m % 8 == 7:
                nc.sync.dma_start(out=out[128 * s : 128 * s + 128, n0 : n0 + n], in_=a)

        waiting = [(m, n0) for m in range(15) for n0 in (0, 512)]

        def seconds(count):
            for i in range(count):
                second(*waiting.pop(0))

        nc.vector.memset(ident[:], 0.0)
        zero = sb([128, 512], BF16, "zero")
        nc.vector.memset(zero[:].bitcast(I32), 0)
        nc.vector.memset(v_pl[:].bitcast(I32), 0)
        nc.vector.memset(u_pl[:].bitcast(I32), 0)
        make_identity(nc, ident[:], nomemset=True)
        for Q in range(4):
            load_scales(nc.scalar if Q % 2 else nc.sync, u_pl_raw, u_scales, Q)
        load_x(0)
        nc.sync.dma_start(out=u_raw[:].bitcast(I32), in_=u_words[0].bitcast(I32))
        nc.sync.dma_start(out=v_w[:].bitcast(I32), in_=v_words[0].bitcast(I32))
        for Q in range(4):
            load_scales(nc.sync, v_pl, v_scales, Q)
        load_w(0, 0)
        load_w(1, 0)
        load_x(1)
        load_w(0, 1)
        load_w(1, 1)
        load_x(2)
        load_x(3)
        for q in range(PE_PAIRS, PAIRS):
            load_x_quad(q)

        warm = bank("warm", [128, 512])
        for i in range(WARM_UPS):
            nc.tensor.matmul(warm[:], lhsT=zero[:, 0:128], rhs=zero[:], start=True, stop=True)
        x_transpose(0)
        nc.tensor.matmul(warm[:], lhsT=zero[:, 0:128], rhs=zero[:], start=True, stop=True)

        for Q in range(4):
            deal_u_scales(Q)
        deal_u_words()
        x_out(0, 1)
        x_quant(0)
        w_weave(0, 0)
        w_weave(1, 0)
        w_quant(0, 0)
        w_quant(1, 0)
        w_weave_pool(0, 1, 3)
        for k in range(E_BEFORE_PAIR_1):
            e_bank(k)
        x_transpose(1)
        x_out(1, 2)
        for k in range(E_BEFORE_PAIR_1, 16):
            e_bank(k)
        w_weave(0, 1, 2, 3)
        x_quant(1)
        w_weave(0, 1, 0, 2)
        w_weave(1, 1)
        w_quant(0, 1)
        w_quant(1, 1)
        for q in range(2):
            for j in range(2):
                first(q, 0, j)
                h_out(q, 0, j)
        x_transpose(2)
        x_out(2, 2)
        x_transpose(3)
        x_out(3, 0)
        zip_first_vector(0)
        x_quant(2)
        e_quant(0)
        for q in range(2):
            for j in range(2):
                first(q, 1, j)
                h_out(q, 1, j)
        e_quant(1)
        h_quant(0)
        x_quant(3)
        x_split(4)
        h_quant(1)
        x_turn(4)

        for j in range(2):
            first(2, 0, j)
            h_out(2, 0, j)
        zip_first_pool(2)
        for j in range(2):
            first(2, 1, j)
        seconds(OPENING)
        for j in range(2):
            h_out(2, 1, j)
        x_join(4)
        zip_rest(2)

        for q in range(3, LAST):
            for G in range(2):
                for j in range(2):
                    first(q, G, j)
                    seconds(1)
                    h_out(q, G, j)
                    if (G, j) == (0, 0):
                        if q + 2 < POOL_SPLIT[0]:
                            x_split(q + 2)
                        x_quant(q + 1)
                        h_quant(q - 1)
                        if q + 3 in POOL_SPLIT:
                            x_split(q + 3)
                        if q + 2 < PAIRS:
                            x_turn(q + 2)
                    if (G, j) == (0, 1) and q in POOL_ZIP:
                        zip_first_pool(q)
            if q + 2 < PAIRS:
                x_join(q + 2)
            zip_rest(q)

        first(LAST, 0, 0)
        seconds(3)
        h_out(LAST, 0, 0)
        h_quant(LAST - 1)
        seconds(1)
        first(LAST, 1, 0)
        h_out(LAST, 1, 0)
        h_quant(LAST, 0, 256)
        first(LAST, 0, 1)
        h_out(LAST, 0, 1)
        seconds(1)
        h_quant(LAST, 256, 128)
        seconds(2)
        first(LAST, 1, 1)
        h_out(LAST, 1, 1)
        seconds(1)
        h_quant(LAST, 384, 128)
        seconds(2)
        for n0 in range(0, 1024, STORE_PIECE):
            second(15, n0, STORE_PIECE)
